import numpy as np, ml_dtypes
CORES = [2,6,10,14,18,22,26,30]
N = 8
BF = ml_dtypes.bfloat16
def gentries(a):
    return np.ascontiguousarray(a.reshape(8, 16, -1).transpose(0, 2, 1)).reshape(8, -1)
def gtable(e):
    e = np.asarray(e); return np.ascontiguousarray(e.reshape(8, -1, 16).transpose(0, 2, 1)).reshape(128, -1).astype(np.int32)
V, L, TV, LV, H = 2304, 192, 3, 3, 3
W = V + TV * LV * L
def parts(rng):
    x = rng.integers(0, 64, (N, 8, 16, V)); ch = rng.integers(0, V, (N, 8, 16, V)); b, a, c = rng.integers(0, V, (3, N, 8, L))
    y = rng.integers(0, 64, (N, 8, 16, L)); th = rng.integers(285, 361, (N, 8, 1)) + rng.integers(-40, 41, (N, 8, 16))
    return x, ch, b, a, c, y, th
def pack(x, ch, b, a, c, y, th):
    return {"x": x.reshape(N, 128, V).astype(np.float32).astype(BF), "ch": np.ascontiguousarray(ch.reshape(N, 128, V)).astype(np.int32), "sb": np.stack([gtable(e) for e in b]),
            "ia": np.stack([gtable(e) for e in a]), "ic": np.stack([gtable(e) for e in c]), "y": y.reshape(N, 128, L).astype(np.float32).astype(BF), "th": np.ascontiguousarray(th.reshape(N, 128, 1)).astype(np.int32)}
def setup_inputs(rng):
    x, ch, b, a, c, y, th = parts(rng); m = rng.random((N, 8, L))
    c = np.where(m < 0.06, a, np.where(m < 0.12, b, c))
    return pack(x, ch, b, a, c, y, th)
def setup_inputs_spread(rng):
    x, ch, b, a, c, y, th = parts(rng)
    x = np.floor(np.exp2(6 * rng.random((N, 8, 1, V))) * rng.random((N, 8, 16, V))).astype(np.int64)
    y = np.floor(np.exp2(6 * rng.random((N, 8, 1, L))) * rng.random((N, 8, 16, L))).astype(np.int64)
    e = rng.integers(1, 4, (N, 8, 1, 1))
    ch = np.minimum(np.floor(V * rng.random((N, 8, 16, V)) ** e).astype(np.int64), V - 1)
    b, a, c = [np.minimum(np.floor(V * rng.random((N, 8, L)) ** e[:, :, 0]).astype(np.int64), V - 1) for i in range(3)]
    th = np.minimum(np.exp2(9 * rng.random((N, 8, 16))).astype(np.int64) - 1, 511)
    return pack(x, ch, b, a, c, y, th)
def setup_inputs_ends(rng):
    x, ch, b, a, c, y, th = parts(rng)
    x = np.where(rng.random((N, 8, 1, V)) < 0.5, 63 * rng.integers(0, 2, (N, 8, 1, V)), 63 * rng.integers(0, 2, x.shape))
    s = rng.integers(0, 2, (N, 8, 1)); s[:, 6:] = 1
    x[..., 0] = 63 * (1 - s); x[..., V - 1] = 63 * s; x[..., V - 2] = 63 * (np.arange(16) % 2)
    y = 63 * rng.integers(0, 2, y.shape); th = 511 * rng.integers(0, 2, th.shape)
    u = rng.random(ch.shape); ch = np.where(u < 0.75, (V - 1) * rng.integers(0, 2, ch.shape), np.where(u < 0.85, V - 2, ch))
    o = []
    for e in (b, a, c):
        u = rng.random(e.shape); o.append(np.where(u < 0.7, (V - 1) * rng.integers(0, 2, e.shape), np.where(u < 0.8, V - 2, e)))
    b, a, c = o
    for k in (3, 14, 15):
        ch[:, 7, k, V - 1] = V - 1; ch[:, 7, k, 0] = 0; ch[:, 7, k, V - 2] = V - 2; th[:, 7, k] = 0
    x[:, 7, :, V - 3] = 0; x[:, 7, 15, V - 3] = 1
    ch[:, 7, 0, V - 1] = V - 1; ch[:, 7, 0, 0] = V - 3; ch[:, 7, 0, V - 2] = V - 2; th[:, 7, 0] = 0
    ch[:, 6, :15, V - 2] = ch[:, 6, :15, 0]
    ch[:, 6, 15, V - 1] = V - 1; ch[:, 6, 15, 0] = 0; ch[:, 6, 15, V - 2] = V - 2; th[:, 6, 15] = 0
    for i in (0, 2, L - 1):
        a[:, 6:, i] = V - 1; b[:, 6:, i] = 0; c[:, 6:, i] = V - 2
    return pack(x, ch, b, a, c, y, th)
def setup_inputs_crowd(rng):
    x, ch, b, a, c, y, th = parts(rng)
    for q in range(N):
        for g in range(8):
            o = rng.permutation(V); mode = (q + g) % 4
            if mode == 3:
                b[q, g], a[q, g], c[q, g] = o[rng.integers(0, 3, (3, L))]; ch[q, g][:, o[:3]] = o[rng.integers(3, 7, (16, 3))]
                continue
            a[q, g] = o[0]; b[q, g] = o[1]; c[q, g] = o[2]
            ch[q, g, :, o[0]] = o[3]; ch[q, g, :, o[1]] = o[4]; ch[q, g, :, o[2]] = o[5]
            x[q, g, :, o[3]] = 63; x[q, g, :, o[4]] = 0; x[q, g, :, o[5]] = 63 * (np.arange(16) % 2)
            j = int(rng.choice(np.array([0, L - 1, L // 2])))
            if mode < 2: th[q, g] = rng.integers(100, 251, 16)
            if mode == 1: c[q, g, j] = o[1]
            if mode == 2:
                th[q, g] = rng.integers(420, 501, 16); ch[q, g, :7, o[2]] = o[4]
                ch[q, g, :, o[6]] = o[5]; ch[q, g, :8, o[6]] = o[4]
                n = int(rng.choice(np.array([1, L // 2, L - 1]))); c[q, g, rng.permutation(L)[:n]] = o[6]
                ch[q, g, :, o[7]] = o[8]; x[q, g, :, o[8]] = 0; b[q, g, j] = o[7]
    return pack(x, ch, b, a, c, y, th)
def setup_inputs_brink(rng):
    x, ch, b, a, c, y, th = parts(rng); h = V // 3; k = h // 2
    for q in range(N):
        for g in range(8):
            o = rng.permutation(V); ca, cb, cc = o[:h], o[h:2 * h], o[2 * h:]
            m = int(rng.integers(5, 15)); th[q, g] = 16 * m
            x[q, g][:, cc] = 31
            sg = np.where(np.argsort(rng.random((16, h)), axis=0) < rng.choice(np.array([7, 8, 9, 10]), h), 1, -1)
            for cls, sign in ((ca, sg), (cb, np.ones((16, h), np.int64))):
                big = np.full((16, h), m); ex = np.where(np.arange(h) < k, 1, rng.integers(-1, 1, h)); big[rng.integers(0, 16, h), np.arange(h)] += ex
                x[q, g][:, cls] = 31 + sign * big
            for cls, cnt in ((ca, (0, 1, 8, 9, 15, 16)), (cb, (16, 16, 16, 8, 9, 15))):
                on = np.argsort(rng.random((16, h)), axis=0) < rng.choice(np.array(cnt), h)
                ch[q, g][:, cls] = np.where(on, cls[rng.integers(0, k, (16, h))], cls[rng.integers(k, h, (16, h))])
            ch[q, g][:, cc] = cc[rng.integers(0, len(cc), (16, len(cc)))]
            a[q, g] = ca[rng.integers(0, h, L)]; b[q, g] = cb[rng.integers(0, h, L)]; c[q, g] = cc[rng.integers(0, len(cc), L)]
            y[q, g] = np.where(rng.random((16, L)) < 0.8, 31 + m, y[q, g])
    return pack(x, ch, b, a, c, y, th)
def setup_inputs_corners(rng):
    x, ch, b, a, c, y, th = parts(rng)
    kind = rng.integers(0, 4, (N, 8, 1, V)); v = np.arange(V)
    ch = np.where(kind == 0, v, np.where(kind == 1, (V - 1) * rng.integers(0, 2, ch.shape), np.where((kind == 3) & (rng.random(ch.shape) < 0.5), v, ch)))
    b = np.where(rng.random(b.shape) < 0.2, (V - 1) * rng.integers(0, 2, b.shape), b)
    a = np.where(rng.random(a.shape) < 0.2, (V - 1) * rng.integers(0, 2, a.shape), a)
    m = rng.integers(0, 7, (N, 8, L)); a = np.where(m < 2, b, a); c = np.where((m == 0) | (m == 2), b, np.where(m == 3, a, c))
    th[:, 0] = 0; th[:, 1] = 511; th[:, 2] = 511 * rng.integers(0, 2, (N, 16))
    x[:, 3] = rng.integers(0, 64, (N, 1, 1)); x[:, 4] = 63 * rng.integers(0, 2, (N, 16, V))
    y = np.where(rng.random((N, 8, 1, L)) < 0.3, 63 * rng.integers(0, 2, (N, 8, 1, L)), y)
    return pack(x, ch, b, a, c, y, th)
def check_inputs(d):
    bad = []
    for k, lo, hi in (("x", 0, 63), ("ch", 0, V - 1), ("sb", 0, V - 1), ("ia", 0, V - 1), ("ic", 0, V - 1), ("y", 0, 63), ("th", 0, 511)):
        v = np.asarray(d[k]).astype(np.float64)
        if not (np.min(v) >= lo and np.max(v) <= hi): bad.append("range of " + k)
        elif np.any(v != np.floor(v)): bad.append("whole numbers of " + k)
    return bad
def pick(s, ix):
    return np.array([[np.take(s[q, g], ix[q, g], axis=1) for g in range(8)] for q in range(N)])
def kids(s, ch):
    return pick(s, ch.reshape(N, 8, 16 * L)).reshape(N, 8, 16, 16, L)
def reference(x, ch, sb, ia, ic, y, th):
    X = np.zeros((N, 8, 16, W), np.int32); C = np.zeros((N, 8, 16, W), np.int32)
    X[..., :V] = x.astype(np.float32).astype(np.int32).reshape(N, 8, 16, V); C[..., :V] = ch.reshape(N, 8, 16, V)
    b, a, c = [np.stack([gentries(e) for e in z]).astype(np.int32) for z in (sb, ia, ic)]
    Y = y.astype(np.float32).astype(np.int32).reshape(N, 8, 16, L); t0 = th.astype(np.int32).reshape(N, 8, 16, 1)
    lane = np.arange(L, dtype=np.int32); slot = np.arange(16)[:, None]; A = np.zeros((N, 8, 1, 1), np.int32)
    for t in range(TV):
        pa, pb, pc = a, b, c; off = np.zeros((N, 8, L), bool)
        for lev in range(LV):
            n = V + (t * LV + lev) * L
            ka, kb, kc = pick(C, pa), pick(C, pb), pick(C, pc)
            xa, xb, xc = kids(X, ka), kids(X, kb), kids(X, kc)
            al = np.add.reduce(np.abs(xa - xc), axis=2) > t0 + A; be = np.add.reduce(np.abs(xb - xc), axis=2) > t0 + A
            dist = np.add.reduce(np.abs(xa - xb), axis=2); vote = np.add.reduce((xa >= xb).astype(np.int32), axis=2) >= 9
            col = al & be
            M = np.where(al & (~be | vote), ka, kb)
            ks = np.argmax(np.where(col | ~np.any(col, axis=2, keepdims=True), dist, -1), axis=2)[:, :, None]
            off = off | (np.add.reduce(col.astype(np.int32), axis=2) >= 9)
            if lev < LV - 1: M = np.where(slot == ks, n + L + lane, M)
            na, nb, nc = [np.take_along_axis(z, ks, 2)[:, :, 0] for z in (ka, kb, kc)]
            new = np.clip(pick(X, pa) + pick(X, pb) - pick(X, pc), 0, 63)
            half = (pick(X, nb) + Y) >> 1
            first = np.argmax(nb[:, :, :, None] == nb[:, :, None, :], axis=3) == lane
            for q in range(N):
                for g in range(8):
                    w = first[q, g]; X[q, g][:, nb[q, g][w]] = half[q, g][:, w]
            X[..., n:n + L] = new; C[..., n:n + L] = M
            pa, pb, pc = na, nb, nc
        n0 = V + t * LV * L; x0 = X[..., n0:n0 + L]
        Y = np.where(off[:, :, None], np.abs(Y - x0), x0)
        c = b; a = np.where(off, a, n0 + lane); b = np.where(off, b, n0 + lane)
        A = np.add.reduce(off.astype(np.int32), axis=2).reshape(N, 8, 1, 1)
        if t < TV - 1: a, c, Y = np.roll(a, H, axis=0), np.roll(c, H, axis=0), np.roll(Y, H, axis=0)
    return {"xo": X.reshape(N, 128, W).astype(np.float32).astype(BF), "co": np.ascontiguousarray(C[..., V:]).reshape(N, 128, W - V).astype(np.float32),
            "so": np.stack([gtable(e) for e in b]).astype(np.float32), "yo": Y.reshape(N, 128, L).astype(np.float32).astype(BF)}

@@ -1,0 +1,526 @@
+from concourse.mybir import AluOpType, ActivationFunctionType
+import numpy as np
+
+V, L, TV, LV, HOP = 2304, 192, 3, 3, 3
+XW = V + 2 * LV * L
+PLAN = [(64, 192, (32, -32, 32, 32), (64, 64)), (0, 64, (32, 32), (64,))]
+PLACE = ["LS", "OH"]
+NM = 160
+MAGIC = 12582912.0
+
+B16, F16, F32, I32, U16 = "bfloat16", "float16", "float32", "int32", "uint16"
+SIZES = {B16: 2, F16: 2, F32: 4, I32: 4, U16: 2}
+
+
+def _sb(n, d):
+    return ("sbuf", [128, n], d)
+
+
+SCRATCH = {
+    "X": _sb(XW + 16, B16), "XN": _sb(576, B16), "C": _sb(XW, I32), "Cf": _sb(1728, F32),
+    "sbi": _sb(12, I32), "iai": _sb(12, I32), "ici": _sb(12, I32), "thi": _sb(1, I32),
+    "y0": _sb(L, B16), "y1": _sb(L, B16), "y2": _sb(L, B16),
+    "ys0": _sb(L, B16), "ys1": _sb(L, B16), "ys2": _sb(L, B16), "yt": _sb(L, B16), "yd": _sb(L, B16),
+    "au": _sb(12, U16), "bu": _sb(12, U16), "cu": _sb(12, U16),
+    "cin": _sb(12, U16), "acin": _sb(24, U16), "ain": _sb(12, U16), "snd0": _sb(24, U16), "snd1": _sb(24, U16),
+    "aL": _sb(12, F32), "bL0": _sb(12, F32), "bL1": _sb(12, F32), "bL2": _sb(12, F32), "bL3": _sb(12, F32),
+    "an": _sb(12, F32), "mxL": _sb(12, F32), "tl": _sb(12, F32), "tl2": _sb(12, F32), "nlv": _sb(12, F32),
+    "Bt": _sb(3072, B16), "E": _sb(3072, B16), "Fd": _sb(3072, B16), "U": _sb(3072, F16),
+    "AF": _sb(3072, B16), "AH": _sb(3072, B16),
+    "ku0": _sb(576, U16), "ku1": _sb(576, U16), "kf0": _sb(576, F16), "kf1": _sb(576, F16),
+    "Lu0": _sb(48, U16), "Lu1": _sb(48, U16), "Lf": _sb(192, F32), "PV": _sb(576, B16),
+    "S": _sb(384, B16), "PR": _sb(960, F16), "key": _sb(L, F32), "keyT": _sb(L, F32), "FT": _sb(L, F32),
+    "ohT": _sb(L, F32), "ohB": _sb(L, B16), "ZR": _sb(L, F32), "eq": _sb(L, F32), "sc": _sb(L, F32),
+    "tg": _sb(12, F32), "Tu": _sb(24, U16), "sm": _sb(L, B16), "hb": _sb(L, B16),
+    "RC": _sb(576, B16), "r1": _sb(L, F32), "r2": _sb(L, F32), "vt": _sb(L, B16), "sg": _sb(L, B16),
+    "x1": _sb(L, F32), "m1": _sb(L, F32), "sa": _sb(L, B16), "acc": _sb(1, F32), "nb": _sb(1, F32), "nh": _sb(1, F32),
+    "pid": _sb(1, I32), "ri": _sb(1, I32), "rf": _sb(1, F32), "pf": _sb(1, F32), "g16": _sb(1, F32), "g15": _sb(1, F32),
+    "kc": _sb(1, F32), "dc": _sb(1, F32), "xr": _sb(144, F32), "blk": _sb(128, F32), "rp": _sb(NM, F32),
+    "Ct": _sb(3072, B16), "nv": _sb(L, B16), "ji": _sb(NM, F32), "I": _sb(128, B16), "NI": _sb(128, B16), "I2": _sb(128, B16), "IP": _sb(128, B16),
+    "IN": _sb(128, B16), "I16": _sb(128, F16), "E1": _sb(144, B16), "En": _sb(144, B16), "E2": _sb(144, F16),
+    "E16": _sb(144, F16), "BO": _sb(128, F16), "MZ": _sb(2 * NM, B16), "kk": _sb(NM, F16), "rst": _sb(NM, F32),
+    "d0": _sb(NM, F32), "d1": _sb(NM, F32), "jc": _sb(NM, F16), "lan": _sb(L, B16), "li": _sb(40, I32),
+    "lu": _sb(40, U16), "lf": _sb(12, F32), "laneL": _sb(12, F32), "n128": _sb(16, B16),
+}
+BANKS = ("H0", "H1", "SA", "SB", "OH", "LS", "MX", "MY")
+for _b in BANKS:
+    SCRATCH[_b] = ("psum", [128, 512], F32)
+
+DMAS = ["l_sb", "l_ia", "l_ic", "l_th", "l_y", "l_ch", "l_x", "s_c0", "s_c1", "s_c2", "s_xn", "s_x0", "s_x1", "s_so", "s_yo"]
+ARRIVE = ["r_c", "r_a0", "r_y0", "r_a1", "r_y1"]
+SEMAPHORES = ["pe", "dve", "act", "pool", "sent"] + DMAS + ARRIVE
+
+CY, PCY, GA, SCA = 1.04e-3, 0.52e-3, 1.56, 3.8
+HOP_SAME, HOP_OTHER = 0.08, 0.2
+LOOKS, ROUNDS, TRIES, SOFT = (0.2, 0.5, 0.35), 3, 160, False
+
+
+def one_pass(qs, dur, lat, pred, succ, free_pairs, prio, back, look):
+    n = len(qs)
+    left = [len(p) for p in pred]
+    ready_at = [lat[i] if back else 0.0 for i in range(n)]
+    ready, free, order = {}, {}, []
+    start, fin = [0.0] * n, [0.0] * n
+    for i in range(n):
+        if left[i] == 0:
+            ready.setdefault(qs[i], []).append(i)
+    while len(order) < n:
+        pick, pt = None, None
+        for q, lst in ready.items():
+            if not lst:
+                continue
+            t0 = max(free.get(q, 0.0), min(ready_at[i] for i in lst))
+            if pt is not None and t0 >= pt[0]:
+                continue
+            now = max((i for i in lst if ready_at[i] <= t0), key=lambda i: (prio[i], -i))
+            for i in lst:
+                if ready_at[i] > t0 and prio[i] > prio[now] and ready_at[i] - t0 < look * dur[now]:
+                    now = i
+            pick, pt = now, (t0, max(t0, ready_at[now]))
+        q = qs[pick]
+        ready[q].remove(pick)
+        start[pick] = pt[1]
+        free[q] = pt[1] + dur[pick]
+        fin[pick] = free[q] + (0.0 if back else lat[pick])
+        order.append(pick)
+        for s in succ[pick]:
+            hop = HOP_OTHER if qs[s] != q else 0.0 if (min(s, pick), max(s, pick)) in free_pairs else HOP_SAME
+            r = fin[pick] + hop + (lat[s] if back else 0.0)
+            ready_at[s] = max(ready_at[s], r)
+            left[s] -= 1
+            if left[s] == 0:
+                ready.setdefault(qs[s], []).append(s)
+    return order, start, fin, max(fin)
+
+
+PLANNED = {}
+
+
+def order_ops(ops):
+    n = len(ops)
+    qs, dur, lat = [o["q"] for o in ops], [o["dur"] for o in ops], [o["lat"] for o in ops]
+    pred = [o["deps"] + o["soft"] for o in ops]
+    pairs = {(d, i) for i, o in enumerate(ops) for d in o["soft"]}
+    keyed = (n, sum(dur), sum(len(p) for p in pred))
+    if keyed not in PLANNED:
+        succ = [[] for _ in range(n)]
+        for i in range(n):
+            for d in pred[i]:
+                succ[d].append(i)
+        base = [0.0] * n
+        for i in range(n - 1, -1, -1):
+            base[i] = dur[i] + lat[i] + max([base[s] + HOP_OTHER for s in succ[i]] + [0.0])
+        best = None
+        rng = np.random.default_rng(1)
+        for trial in range(TRIES):
+            look = LOOKS[trial % len(LOOKS)]
+            prio = base if best is None or trial % 4 == 0 else [-s for s in best[1]]
+            prio = [p + float(e) for p, e in zip(prio, rng.normal(0.0, 0.3 if trial else 1e-9, n))]
+            for _ in range(ROUNDS):
+                fw = one_pass(qs, dur, lat, pred, succ, pairs, prio, False, look)
+                if best is None or fw[3] < best[3]:
+                    best = fw
+                prio = one_pass(qs, dur, lat, succ, pred, pairs, fw[2], True, look)[2]
+        PLANNED[keyed] = best
+    order, start, _fin, end = PLANNED[keyed]
+    for i in range(n):
+        ops[i]["start"] = start[i]
+    return order, end
+
+
+def rank_program(g, core, T, topo):
+    rank = T.rank_of(core)
+    if rank is None:
+        return
+    A, AF = AluOpType, ActivationFunctionType
+    nr = len(T.cores)
+    dst = T.cores[(rank + HOP) % nr]
+    src = T.cores[(rank - HOP) % nr]
+    rid, pid, _ = topo.addr(dst)
+    mask_out = topo.mask(core, dst)
+    n_out = len(topo.engines(core, dst))
+    n_in = len(topo.engines(src, core))
+    Q = {"pe": g.tensor, "dve": g.vector, "act": g.scalar, "pool": g, "sp": g.sync}
+    ops, hist, bank_last = [], {}, {}
+    CHUNKS = [c[:2] for c in PLAN]
+    NVB, ZB = PLACE
+
+    def v(name, a=0, b=None, s=1):
+        return (name, a, SCRATCH[name][1][1] if b is None else b, s)
+
+    def ap(w):
+        if len(w) == 2:
+            return ap(w[0]).indirect(ap(w[1]))
+        return T[w[0]][:, w[1]:w[2]] if w[3] == 1 else T[w[0]][:, w[1]:w[2]:w[3]]
+
+    def cnt(w):
+        return 16 * (w[1][2] - w[1][1]) if len(w) == 2 else len(range(w[1], w[2], w[3]))
+
+    def narrow(*ws):
+        return all(SIZES[SCRATCH[w[0]][2]] == 2 for w in ws)
+
+    def add(q, fn, rd, wr, dur, lat=0.0, sem=None, after=()):
+        i = len(ops)
+        r2, w2 = [], []
+        for w in rd:
+            r2.extend(list(w) if len(w) == 2 else [w])
+        for w in wr:
+            if len(w) == 2:
+                w2.append(w[0]); r2.append(w[1])
+            else:
+                w2.append(w)
+        deps, soft = set(after), set()
+        for lst, isw in ((r2, False), (w2, True)):
+            for w in lst:
+                for (a, b, j, jw) in hist.get(w[0], ()):
+                    if (isw or jw) and a < w[2] and w[1] < b:
+                        if isw and ops[j]["q"] == q and q in ("dve", "act", "pe"):
+                            soft.add(j)
+                        else:
+                            deps.add(j)
+        for b in {w[0] for w in r2 + w2 if w[0] in BANKS}:
+            run = bank_last.setdefault(b, [q, [], []])
+            if run[0] != q:
+                run[0], run[2], run[1] = q, run[1], []
+            run[1].append(i)
+            deps.update(run[2])
+        for lst, isw in ((r2, False), (w2, True)):
+            for w in lst:
+                h = hist.setdefault(w[0], [])
+                if isw:
+                    h[:] = [e for e in h if not (w[3] == 1 and w[1] <= e[0] and e[1] <= w[2])]
+                h.append((w[1], w[2], i, isw))
+        deps.discard(i)
+        soft.discard(i)
+        if not SOFT:
+            deps |= soft
+        ops.append({"q": q, "fn": fn, "deps": sorted(deps), "soft": sorted(soft - deps), "dur": dur, "lat": lat, "sem": sem})
+        return i
+
+    def vdur(out, ins, per):
+        if len(out) == 2:
+            return 0.05 + cnt(out) * SCA * CY
+        if any(len(w) == 2 for w in ins):
+            return 0.05 + cnt(out) * GA * CY
+        return max(64, cnt(out) * per) * CY + 0.02
+
+    def sc_(x):
+        return x if isinstance(x, (int, float)) or x is None else ap(x)
+
+    def cols(*xs):
+        return [x for x in xs if isinstance(x, tuple)]
+
+    def tt(out, a, b, op):
+        per = 1.0 if (len(a) == 4 and a[0] in BANKS) or b[0] in BANKS else 1.5
+        return add("dve", lambda: g.vector.tensor_tensor(ap(out), ap(a), ap(b), op), [a, b], [out], vdur(out, [a], per))
+
+    def ts(out, a, s1, op0, s2=None, op1=None):
+        per = 0.5 if len(a) == 4 and narrow(out, a) else 1.0
+        if op1 is None:
+            fn = lambda: g.vector.tensor_scalar(ap(out), ap(a), sc_(s1), None, op0)
+        else:
+            fn = lambda: g.vector.tensor_scalar(ap(out), ap(a), sc_(s1), sc_(s2), op0, op1)
+        return add("dve", fn, [a] + cols(s1, s2), [out], vdur(out, [a], per))
+
+    def cp(out, a):
+        per = 0.5 if len(a) == 4 and narrow(out, a) else 1.0
+        return add("dve", lambda: g.vector.tensor_copy(ap(out), ap(a)), [a], [out], vdur(out, [a], per))
+
+    def scan(out, d0, d1, init, op0, op1):
+        return add("dve", lambda: g.vector.tensor_tensor_scan(ap(out), ap(d0), ap(d1), init, op0, op1),
+                   [d0, d1], [out], vdur(out, [d1], 1.0))
+
+    def tr(out, a):
+        return add("dve", lambda: g.vector.transpose(ap(out), ap(a)), [a], [out], vdur(out, [a], 1.0))
+
+    def fill(out, c):
+        return add("dve", lambda: g.vector.memset(ap(out), c), [], [out], vdur(out, [], 0.5))
+
+    def act(out, a, func, bias=0.0, scale=1.0, accum=None):
+        dur = 0.065 + cnt(out) * GA * CY if len(a) == 2 else max(64, cnt(out)) * CY + 0.03
+        if accum is None:
+            fn = lambda: g.scalar.activation(ap(out), ap(a), func, bias=sc_(bias), scale=scale)
+        else:
+            fn = lambda: g.scalar.activation(ap(out), ap(a), func, bias=sc_(bias), scale=scale, accum_out=ap(accum))
+        return add("act", fn, [a] + cols(bias), [out] + cols(accum), dur)
+
+    def mm(out, terms):
+        def fn():
+            last = None
+            for k, (w, x) in enumerate(terms):
+                last = g.tensor.matmul(ap(out), ap(w), ap(x), k == 0, k == len(terms) - 1)
+            return last
+        rd = list({z: 0 for t in terms for z in t})
+        return add("pe", fn, rd, [out], len(terms) * max(64, cnt(out)) * PCY + 0.05)
+
+    def iota(out, pat, base, mult):
+        if SCRATCH[out[0]][2] == I32:
+            fn = lambda: g.iota(ap(out), pat, base, mult)
+        else:
+            fn = lambda: g.iota(ap(out), pat, base, mult, allow_small_or_imprecise_dtypes=True)
+        return add("pool", fn, [], [out], 0.13 + 2 * cnt(out) * CY)
+
+    def load(q, sem, out, hbm, lat):
+        return add(q, lambda: Q[q].dma_start(ap(out), hbm), [], [out], 0.1, lat, (sem, 16))
+
+    def store(q, sem, hbm, a, lat):
+        return add(q, lambda: Q[q].dma_start(hbm, ap(a)), [a], [], 0.1, lat, (sem, 16))
+
+    def send(sem, land, a):
+        i = add("pool", lambda: g.remote_dma(ap(land), ap(a), T.sem[sem], T.sem.sent, pid, rid, mask_out),
+                [a], [], 1.0, 0.0, ("sent", 0))
+        return add("net", None, [], [land], 0.0, 3.5, (sem, n_in), after=[i])
+
+    def sel(name, m):
+        return v(name, 15 - m, 143 - m)
+
+    load("sp", "l_ch", v("C", 0, V), T.ch[:], 6.0)
+    load("act", "l_sb", v("sbi"), T.sb[:], 2.0)
+    load("act", "l_ia", v("iai"), T.ia[:], 2.0)
+    load("act", "l_ic", v("ici"), T.ic[:], 2.0)
+    load("act", "l_x", v("X", 0, V), T.x[:], 6.5)
+    load("sp", "l_th", v("thi"), T.th[:], 2.0)
+    load("sp", "l_y", v("y0"), T.y[:], 2.0)
+    cp(v("bu"), v("sbi")); cp(v("au"), v("iai")); cp(v("cu"), v("ici"))
+    send("r_c", v("cin"), v("bu"))
+    cp(v("aL"), v("iai")); cp(v("bL0"), v("sbi"))
+    ts(v("nb"), v("thi"), -1.0, A.mult, -0.5, A.add)
+    ts(v("nh"), v("thi"), -1.0, A.mult, -96.5, A.add)
+
+    iota(v("pid"), [[0, 1]], 0, 1)
+    iota(v("xr"), [[1, 144]], 0, 0)
+    iota(v("li", 0, 12), [[16, 12]], 15, 0)
+    off = 12
+    bc = []
+    for (l0, l1) in CHUNKS:
+        nc = (l1 - l0) // 16
+        iota(v("li", off, off + nc), [[1, nc]], 3 * nc, 0)
+        bc.append(v("lu", off, off + nc)); off += nc
+    cp(v("lu", 0, off), v("li", 0, off))
+    iota(v("rp"), [[0, NM // 16], [1, 16]], 0, 0)
+    iota(v("blk"), [[16, 8], [0, 16]], 0, 0)
+    iota(v("ji"), [[16, NM]], -2048, 0)
+    iota(v("lan"), [[1, L]], -L, 0)
+    iota(v("lf"), [[16, 12]], 0, 0)
+    ts(v("ri"), v("pid"), 15, A.bitwise_and)
+    cp(v("rf"), v("ri")); cp(v("pf"), v("pid"))
+    tt(v("g16"), v("pf"), v("rf"), A.subtract)
+    ts(v("g15"), v("g16"), 15.0, A.add)
+    ts(v("I"), v("xr", 0, 128), v("pf"), A.is_equal)
+    for nm, c in (("NI", -1.0), ("I2", 2.0), ("IP", 2048.0), ("IN", -2048.0), ("I16", 1.0)):
+        ts(v(nm), v("I"), c, A.mult)
+    ts(v("E1"), v("xr"), v("g15"), A.is_equal)
+    for nm, c in (("En", -2.0 ** -9), ("E2", 2.0 ** -8), ("E16", 1.0)):
+        ts(v(nm), v("E1"), c, A.mult)
+    ts(v("BO"), v("blk"), v("g16"), A.is_equal)
+    ts(v("MZ", 0, NM), v("rp"), v("rf"), A.is_ge, 8192.0, A.mult)
+    fill(v("MZ", NM, 2 * NM), 0.0)
+    ts(v("kc"), v("rf"), -64.0 * 2.0 ** -19, A.mult, -49.0 * 2.0 ** -19, A.add)
+    ts(v("kk"), v("rp"), 0.0, A.mult, v("kc"), A.add)
+    ts(v("rst"), v("rp"), 0.0, A.is_equal, -8.0, A.mult)
+    ts(v("dc"), v("rf"), float(XW - 1), A.add)
+    ts(v("d1"), v("rp"), 15.0, A.is_equal, v("dc"), A.mult)
+    ts(v("d0"), v("rp"), 0.0, A.not_equal)
+    tt(v("d0"), v("d0"), v("d1"), A.add)
+    ts(v("jc"), v("ji"), v("rf"), A.add)
+    ts(v("laneL"), v("lf"), v("rf"), A.add)
+    fill(v("n128"), -128.0)
+
+    first = {0: (v("au"), v("cu"), v("bu")),
+             1: (v("acin", 0, 12), v("cin"), v("snd0", 12, 24)),
+             2: (v("ain"), v("acin", 12, 24), v("snd1", 12, 24))}
+    for t in range(TV):
+        lim = V + t * LV * L
+        Xw, Cw = v("X", 0, lim), v("C", 0, lim)
+        yv = "y%d" % t
+        ts(v("nlv"), v("laneL"), float(lim), A.add)
+        if t > 0:
+            cp(v("aL"), first[t][0])
+        for lev in range(LV):
+            step = t * LV + lev
+            ku, kf, Lu, Lp = "ku%d" % (step % 2), "kf%d" % (step % 2), "Lu%d" % (step % 2), "Lu%d" % ((step + 1) % 2)
+            nbase = lim + lev * L
+            for (l0, l1) in CHUNKS:
+                n, nc = l1 - l0, (l1 - l0) // 16
+                if lev == 0:
+                    for q in (2, 1, 0):
+                        w = first[t][q]
+                        lst = v(w[0], w[1] + l0 // 16, w[1] + l1 // 16)
+                        o = 3 * l0 + q * n
+                        cp(v(ku, o, o + n), (Cw, lst))
+                        ts(v(kf, o, o + n), v(ku, o, o + n), -2048.0, A.add)
+                        act(v("PV", o, o + n), (Xw, lst), AF.Copy)
+                else:
+                    lst = v(Lp, l0 // 4 + nc, l0 // 4 + 4 * nc)
+                    cp(v(ku, 3 * l0, 3 * l1), (Cw, lst))
+                    ts(v(kf, 3 * l0, 3 * l1), v(ku, 3 * l0, 3 * l1), -2048.0, A.add)
+                    act(v("PV", 3 * l0, 3 * l1), (Xw, lst), AF.Copy)
+                o = 3 * l0
+                mm(v(NVB, 192 + l0, 192 + l1), [(v("I"), v("PV", o, o + n)), (v("NI"), v("PV", o + n, o + 2 * n)),
+                                                 (v("I"), v("PV", o + 2 * n, o + 3 * n))])
+            newx = v("X", nbase, nbase + L) if t < 2 else v("XN", lev * L, lev * L + L)
+            act(v("nv"), v(NVB, 192, 384), AF.Relu, bias=63.0, scale=-1.0)
+            act(newx, v("nv"), AF.Relu, bias=63.0, scale=-1.0)
+            piece = 0
+            for ci, (l0, l1, pieces, subs) in enumerate(PLAN):
+                n, nc = l1 - l0, (l1 - l0) // 16
+                p0 = l0
+                for pw in pieces:
+                    w = abs(pw)
+                    c0, c1 = 16 * p0, 16 * (p0 + w)
+                    kid = [v(ku, 3 * l0 + q * n + p0 - l0, 3 * l0 + q * n + p0 - l0 + w) for q in range(3)]
+                    p0 += w
+                    Bt, E, Fd = v("Bt", c0, c1), v("E", c0, c1), v("Fd", c0, c1)
+                    act(Bt, (Xw, kid[2]), AF.Copy)
+                    if pw > 0:
+                        tt(Fd, (Xw, kid[1]), Bt, A.subtract)
+                        act(v("AF", c0, c1), Fd, AF.Abs)
+                        terms = [(v("NI"), Fd)]
+                    else:
+                        Ct = v("Ct", c0, c1)
+                        act(Ct, (Xw, kid[1]), AF.Copy)
+                        H = v("H%d" % (piece % 2), 0, 16 * w); piece += 1
+                        mm(H, [(v("I"), Ct), (v("NI"), Bt)])
+                        act(v("AF", c0, c1), H, AF.Abs)
+                        terms = [(v("I"), Bt), (v("NI"), Ct)]
+                    tt(E, (Xw, kid[0]), Bt, A.subtract)
+                    H = v("H%d" % (piece % 2), 0, 16 * w); piece += 1
+                    mm(H, terms + [(v("I"), E)])
+                    act(v("AH", c0, c1), H, AF.Abs)
+                    ts(v("U", c0, c1), E, 1.0 / 32, A.add, 31.0 / 1024, A.max)
+                SB = "SA" if ci % 2 == 0 else "SB"
+                s0 = 0
+                for w in subs:
+                    c0, c1 = 16 * (l0 + s0), 16 * (l0 + s0 + w)
+                    mm(v(SB, s0, s0 + w), [(sel("E1", k), v("AF", c0 + k, c1, 16)) for k in range(16)])
+                    mm(v(SB, 2 * n + s0, 2 * n + s0 + w), [(v("I16"), v("kk", 0, w))]
+                       + [(sel("En", k), v("E", c0 + k, c1, 16)) for k in range(16)]
+                       + [(sel("E2", k), v("U", c0 + k, c1, 16)) for k in range(16)])
+                    mm(v(SB, n + s0, n + s0 + w), [(sel("E1", k), v("AH", c0 + k, c1, 16)) for k in range(16)])
+                    s0 += w
+                c0, c1 = 16 * l0, 16 * l1
+                so, po, lo, fo = 2 * l0, 5 * l0, l0 // 4, 64 * ci
+                act(v("S", so, so + 2 * n), v(SB, 0, 2 * n), AF.Sign, bias=v("nb"))
+                col = v("PR", po + 4 * n, po + 5 * n)
+                tt(col, v("S", so, so + n), v("S", so + n, so + 2 * n), A.min)
+                tt(v("key", l0, l1), v(SB, 2 * n, 3 * n), col, A.add)
+                tr(v("keyT", l0, l1), v("key", l0, l1))
+                scan(v("FT", l0, l1), v("rst", 0, n), v("keyT", l0, l1), 0.0, A.add, A.max)
+                tt(v("ohT", l0, l1), (v("FT", l0, l1), v("lu", 0, nc)), v("keyT", l0, l1), A.is_equal)
+                oh = v("OH", l0, l1)
+                tr(oh, v("ohT", l0, l1))
+                for q in ((2, 0, 1) if lev < LV - 1 else (2,)):
+                    tt(v("PR", po + (q + 1) * n, po + (q + 2) * n), oh, v(kf, 3 * l0 + q * n, 3 * l0 + (q + 1) * n), A.mult)
+                tt(v("PR", po, po + n), oh, v("jc", 0, n), A.mult)
+                mm(v("LS", 0, 5 * nc), [(sel("E16", r), v("PR", po + r, po + 5 * n, 16)) for r in range(16)])
+                mm(v(ZB, 192, 192 + 2 * n), [(v("BO"), v("PR", po + 3 * n, po + 5 * n)), (v("I"), v("MZ", NM - n, NM + n))])
+                act(v("Lf", fo, fo + 5 * nc), v("LS", 0, 5 * nc), AF.Identity, bias=2048.0)
+                cp(v(Lu, lo, lo + 4 * nc), v("Lf", fo, fo + 4 * nc))
+                act(v("ZR", l0, l1), v(ZB, 192, 192 + n), AF.Identity, bias=2048.0)
+                act(v("RC", lev * L + l0, lev * L + l1), v(ZB, 192 + n, 192 + 2 * n), AF.Relu, bias=-1.0)
+                mx = v("mxL", l0 // 16, l1 // 16)
+                if lev == 0:
+                    cp(mx, v("Lf", fo + 4 * nc, fo + 5 * nc))
+                else:
+                    tt(mx, mx, v("Lf", fo + 4 * nc, fo + 5 * nc), A.max)
+                tt(v("eq", l0, l1), (v("Lf", fo, fo + 5 * nc), bc[ci]), v("ZR", l0, l1), A.is_equal)
+                scan(v("sc", l0, l1), v("d0", 0, n), v("eq", l0, l1), 0.0, A.mult, A.max)
+                tg = v("tg", l0 // 16, l1 // 16)
+                tt(tg, v("sc", l0 + 15, l1, 16), v("Lf", fo + 3 * nc, fo + 4 * nc), A.max)
+                cp(v("Tu", l0 // 8, l1 // 8, 2), tg)
+                tt(v("sm", l0, l1), (v("Bt", c0, c1), v(Lu, lo, lo + nc)), v(yv, l0, l1), A.add)
+                act(v("hb", l0, l1), v("sm", l0, l1), AF.Identity, bias=127.75, scale=0.5)
+            if lev == LV - 1:
+                ts(v("tl"), v("mxL"), 2049.0, A.is_le, 8192.0, A.mult)
+                tt(v("tl2"), v("tl"), v("nlv"), A.min)
+                bn = v("bL%d" % (t + 1))
+                if t < TV - 1:
+                    snd = "snd%d" % t
+                    tt(v("an"), v("tl2"), v("aL"), A.max)
+                    cp(v(snd, 0, 12), v("an"))
+                tt(bn, v("tl2"), v("bL%d" % t), A.max)
+                if t == 0:
+                    cp(v(snd, 12, 24), bn)
+                    send("r_a0", v("acin"), v(snd))
+                elif t == 1:
+                    send("r_a1", v("ain"), v(snd, 0, 12))
+                    cp(v(snd, 12, 24), bn)
+                else:
+                    store("sp", "s_so", T.so[:], bn, 2.0)
+            for c in range(L // 16 - 1, -1, -1):
+                tt((v("X"), v("Tu", 2 * c, 2 * c + 1)), v("hb", 16 * c, 16 * c + 16), v("n128"), A.add)
+            act(v("r1"), v("key"), AF.Identity, bias=MAGIC, scale=8192.0)
+            act(v("r2"), v("r1"), AF.Identity, bias=-MAGIC / 8192, scale=1.0 / 8192)
+            tt(v("vt"), v("key"), v("r2"), A.is_gt)
+            for (l0, l1) in CHUNKS:
+                n, so = l1 - l0, 2 * l0
+                mm(v("MX", l0, l1), [(v("I2"), v("S", so + n, so + 2 * n)), (v("NI"), v("S", so, so + n)), (v("I"), v("vt", l0, l1))])
+            act(v("sg"), v("MX", 0, L), AF.Sign, bias=-1.5)
+            for (l0, l1) in CHUNKS:
+                n = l1 - l0
+                mm(v("MY", l0, l1), [(v("I16"), v(kf, 3 * l0 + 2 * n, 3 * l1)), (v("IN"), v("sg", l0, l1))])
+                mm(v("MY", L + l0, L + l1), [(v("I16"), v(kf, 3 * l0, 3 * l0 + n)), (v("IP"), v("sg", l0, l1))])
+            act(v("x1"), v("MY", 0, L), AF.Copy)
+            mo = v("Cf", step * L, step * L + L)
+            if lev < LV - 1:
+                act(v("ohB"), v("OH", 0, L), AF.Copy, scale=float(nbase + 2 * L))
+                mm(v("MX", L, 2 * L), [(v("I"), v("lan")), (v("I"), v("ohB"))])
+                tt(v("m1"), v("MY", L, 2 * L), v("x1"), A.max)
+                tt(mo, v("MX", L, 2 * L), v("m1"), A.max)
+            else:
+                tt(mo, v("MY", L, 2 * L), v("x1"), A.max)
+            if t < TV - 1:
+                cp(v("C", nbase, nbase + L), mo)
+        store("sp", "s_c%d" % t, T.co[:, t * 576:(t + 1) * 576], v("Cf", t * 576, (t + 1) * 576), 3.0)
+        mm(v("MX", 2 * L - L, 2 * L), [(v("IP"), v("RC", k * L, k * L + L)) for k in range(LV)])
+        x0 = v("X", lim, lim + L) if t < 2 else v("XN", 0, L)
+        if t < TV - 1:
+            act(v("sa"), v("MX", L, 2 * L), AF.Sign, bias=-1.0, accum=v("acc"))
+            ts(v("nb"), v("acc"), -0.5, A.mult, v("nh"), A.add)
+        tt(v("yt"), v("MX", L, 2 * L), v(yv), A.min)
+        tt(v("yd"), v("yt"), x0, A.subtract)
+        act(v("ys%d" % t), v("yd"), AF.Abs)
+        if t < TV - 1:
+            send("r_y%d" % t, v("y%d" % (t + 1)), v("ys%d" % t))
+    store("sp", "s_xn", T.xo[:, XW:XW + 576], v("XN"), 2.5)
+    store("sp", "s_yo", T.yo[:], v("ys2"), 2.0)
+    store("sp", "s_x0", T.xo[:, 0:XW // 2], v("X", 0, XW // 2), 4.0)
+    store("act", "s_x1", T.xo[:, XW // 2:XW], v("X", XW // 2, XW), 4.0)
+
+    order, _end = order_ops(ops)
+    count = {"pe": 0, "dve": 0, "act": 0, "pool": 0}
+    known = {q: {} for q in Q}
+    sent = 0
+    for i in order:
+        o = ops[i]
+        q = o["q"]
+        if q == "net":
+            o["mark"], o["clock"] = o["sem"], {}
+            continue
+        kn = known[q]
+        need = {}
+        for d in o["deps"]:
+            s, val = ops[d]["mark"]
+            if val > need.get(s, (0, 0))[0]:
+                need[s] = (val, d)
+        for s, (val, d) in sorted(need.items(), key=lambda e: -ops[e[1][1]].get("start", 0.0)):
+            if kn.get(s, 0) < val:
+                Q[q].wait_ge(T.sem[s], val)
+                kn[s] = val
+                for s2, v2 in ops[d]["clock"].items():
+                    if kn.get(s2, 0) < v2:
+                        kn[s2] = v2
+        ins = o["fn"]()
+        o["clock"] = dict(kn)
+        if o["sem"] is None:
+            count[q] += 1
+            ins.then_inc(T.sem[q], 1)
+            o["mark"] = (q, count[q])
+        elif o["sem"][0] == "sent":
+            sent += n_out
+            o["mark"] = ("sent", 0)
+        else:
+            ins.then_inc(T.sem[o["sem"][0]], 16)
+            o["mark"] = o["sem"]
+    for s, val in list(count.items()) + [("sent", sent)] + [(s, 16) for s in DMAS] + [(s, n_in) for s in ARRIVE]:
+        g.wait_ge(T.sem[s], val)

@@ -3,8 +3,11 @@ import numpy as np
 
 V, L, TV, LV, HOP = 2304, 192, 3, 3, 3
 XW = V + 2 * LV * L
-PLAN = [(64, 192, (32, -32, 32, 32), (64, 64)), (0, 64, (32, 32), (64,))]
+PLAN = [(64, 192, (16, -32, 16, 32, 32), (64, 64)), (0, 64, (32, 32), (64,))]
 PLACE = ["LS", "OH"]
+QUICK = [0, 6]
+LEAD = [16]
+WIDE = [0, 0]
 NM = 160
 MAGIC = 12582912.0
 
@@ -34,6 +37,8 @@ SCRATCH = {
     "tg": _sb(12, F32), "Tu": _sb(24, U16), "sm": _sb(L, B16), "hb": _sb(L, B16),
     "RC": _sb(576, B16), "r1": _sb(L, F32), "r2": _sb(L, F32), "vt": _sb(L, B16), "sg": _sb(L, B16),
     "x1": _sb(L, F32), "m1": _sb(L, F32), "sa": _sb(L, B16), "acc": _sb(1, F32), "nb": _sb(1, F32), "nh": _sb(1, F32),
+    "I32": _sb(128, F32), "NI32": _sb(128, F32), "NI2": _sb(128, B16), "k2": _sb(L, F32), "x12": _sb(2 * L, F32),
+    "pb": _sb(1, F32), "thL": _sb(12, F32),
     "pid": _sb(1, I32), "ri": _sb(1, I32), "rf": _sb(1, F32), "pf": _sb(1, F32), "g16": _sb(1, F32), "g15": _sb(1, F32),
     "kc": _sb(1, F32), "dc": _sb(1, F32), "xr": _sb(144, F32), "blk": _sb(128, F32), "rp": _sb(NM, F32),
     "Ct": _sb(3072, B16), "nv": _sb(L, B16), "ji": _sb(NM, F32), "I": _sb(128, B16), "NI": _sb(128, B16), "I2": _sb(128, B16), "IP": _sb(128, B16),
@@ -50,9 +55,12 @@ DMAS = ["l_sb", "l_ia", "l_ic", "l_th", "l_y", "l_ch", "l_x", "s_c0", "s_c1", "s
 ARRIVE = ["r_c", "r_a0", "r_y0", "r_a1", "r_y1"]
 SEMAPHORES = ["pe", "dve", "act", "pool", "sent"] + DMAS + ARRIVE
 
-CY, PCY, GA, SCA = 1.04e-3, 0.52e-3, 1.56, 3.8
-HOP_SAME, HOP_OTHER = 0.08, 0.2
-LOOKS, ROUNDS, TRIES, SOFT = (0.2, 0.5, 0.35), 3, 160, False
+CY, PCY = np.array([0.92e-3, 1.04e-3, 0.85e-3, 1.2e-3]), np.array([0.47e-3, 0.52e-3, 0.44e-3, 0.6e-3])
+GA, SCA = np.array([1.56, 1.56, 1.2, 2.0]), np.array([3.8, 3.8, 2.5, 5.5])
+HS, HO, WEIGHT = (0.13, 0.08, 0.2, 0.15), (0.27, 0.2, 0.33, 0.3), (1.0, 1.0, 1.0, 0.75)
+HOP_SAME, HOP_OTHER = HS[0], HO[0]
+LOOKS, ROUNDS, TRIES, SOFT = (0.2, 0.5, 0.35), 3, 20, False
+POLISH = 2200
 
 
 def one_pass(qs, dur, lat, pred, succ, free_pairs, prio, back, look):
@@ -121,6 +129,35 @@ def order_ops(ops):
                 if best is None or fw[3] < best[3]:
                     best = fw
                 prio = one_pass(qs, dur, lat, succ, pred, pairs, fw[2], True, look)[2]
+        durs = [[float(x) for x in np.broadcast_to(o["durs"], CY.shape)] for o in ops]
+
+        def length(order):
+            total = 0.0
+            for m in range(len(CY)):
+                hs, ho = float(HS[m]), float(HO[m])
+                free, fin = {}, [0.0] * n
+                for i in order:
+                    q = qs[i]
+                    t = free.get(q, 0.0)
+                    for d in pred[i]:
+                        r = fin[d] + (hs if qs[d] == q else ho)
+                        if r > t:
+                            t = r
+                    free[q] = t + durs[i][m]
+                    fin[i] = free[q] + lat[i]
+                total += max(fin) * WEIGHT[m]
+            return total
+
+        score = length(best[0])
+        for trial in range(POLISH):
+            a = float(rng.uniform(-5.0, best[3]))
+            b = a + float(rng.uniform(3.0, 14.0))
+            noise = rng.normal(0.0, (0.15, 0.4, 1.0)[trial % 3], n)
+            prio = [-s + (float(e) if a < s < b else 0.0) for s, e in zip(best[1], noise)]
+            fw = one_pass(qs, dur, lat, pred, succ, pairs, prio, False, LOOKS[trial % 2])
+            sc = length(fw[0])
+            if sc <= score:
+                best, score = fw, sc
         PLANNED[keyed] = best
     order, start, _fin, end = PLANNED[keyed]
     for i in range(n):
@@ -194,7 +231,8 @@ def rank_program(g, core, T, topo):
         soft.discard(i)
         if not SOFT:
             deps |= soft
-        ops.append({"q": q, "fn": fn, "deps": sorted(deps), "soft": sorted(soft - deps), "dur": dur, "lat": lat, "sem": sem})
+        ops.append({"q": q, "fn": fn, "deps": sorted(deps), "soft": sorted(soft - deps), "durs": dur,
+                    "dur": float(np.ravel(dur)[0]), "lat": lat, "sem": sem})
         return i
 
     def vdur(out, ins, per):
@@ -251,7 +289,8 @@ def rank_program(g, core, T, topo):
                 last = g.tensor.matmul(ap(out), ap(w), ap(x), k == 0, k == len(terms) - 1)
             return last
         rd = list({z: 0 for t in terms for z in t})
-        return add("pe", fn, rd, [out], len(terms) * max(64, cnt(out)) * PCY + 0.05)
+        return add("pe", fn, rd, [out],
+                   sum(1 if narrow(x) else 4 for _, x in terms) * max(64, cnt(out)) * PCY + 0.05)
 
     def iota(out, pat, base, mult):
         if SCRATCH[out[0]][2] == I32:
@@ -286,6 +325,9 @@ def rank_program(g, core, T, topo):
     cp(v("aL"), v("iai")); cp(v("bL0"), v("sbi"))
     ts(v("nb"), v("thi"), -1.0, A.mult, -0.5, A.add)
     ts(v("nh"), v("thi"), -1.0, A.mult, -96.5, A.add)
+    ts(v("pb"), v("thi"), 0.5, A.add)
+    for ci, (l0, l1) in enumerate(CHUNKS):
+        fill(v("thL", l0 // 16, l1 // 16), 2049.0 + 16.0 * (QUICK[ci] & 1))
 
     iota(v("pid"), [[0, 1]], 0, 1)
     iota(v("xr"), [[1, 144]], 0, 0)
@@ -294,7 +336,7 @@ def rank_program(g, core, T, topo):
     bc = []
     for (l0, l1) in CHUNKS:
         nc = (l1 - l0) // 16
-        iota(v("li", off, off + nc), [[1, nc]], 3 * nc, 0)
+        iota(v("li", off, off + nc), [[1, nc]], (3 if bc else 2) * nc, 0)
         bc.append(v("lu", off, off + nc)); off += nc
     cp(v("lu", 0, off), v("li", 0, off))
     iota(v("rp"), [[0, NM // 16], [1, 16]], 0, 0)
@@ -307,7 +349,8 @@ def rank_program(g, core, T, topo):
     tt(v("g16"), v("pf"), v("rf"), A.subtract)
     ts(v("g15"), v("g16"), 15.0, A.add)
     ts(v("I"), v("xr", 0, 128), v("pf"), A.is_equal)
-    for nm, c in (("NI", -1.0), ("I2", 2.0), ("IP", 2048.0), ("IN", -2048.0), ("I16", 1.0)):
+    for nm, c in (("NI", -1.0), ("I2", 2.0), ("IP", 2048.0), ("IN", -2048.0), ("I16", 1.0),
+                  ("I32", 1.0), ("NI32", -1.0), ("NI2", -2.0)):
         ts(v(nm), v("I"), c, A.mult)
     ts(v("E1"), v("xr"), v("g15"), A.is_equal)
     for nm, c in (("En", -2.0 ** -9), ("E2", 2.0 ** -8), ("E16", 1.0)):
@@ -371,7 +414,10 @@ def rank_program(g, core, T, topo):
                     kid = [v(ku, 3 * l0 + q * n + p0 - l0, 3 * l0 + q * n + p0 - l0 + w) for q in range(3)]
                     p0 += w
                     Bt, E, Fd = v("Bt", c0, c1), v("E", c0, c1), v("Fd", c0, c1)
-                    act(Bt, (Xw, kid[2]), AF.Copy)
+                    if ci == 0 and p0 - l0 <= LEAD[0]:
+                        cp(Bt, (Xw, kid[2]))
+                    else:
+                        act(Bt, (Xw, kid[2]), AF.Copy)
                     if pw > 0:
                         tt(Fd, (Xw, kid[1]), Bt, A.subtract)
                         act(v("AF", c0, c1), Fd, AF.Abs)
@@ -384,9 +430,11 @@ def rank_program(g, core, T, topo):
                         act(v("AF", c0, c1), H, AF.Abs)
                         terms = [(v("I"), Bt), (v("NI"), Ct)]
                     tt(E, (Xw, kid[0]), Bt, A.subtract)
-                    H = v("H%d" % (piece % 2), 0, 16 * w); piece += 1
-                    mm(H, terms + [(v("I"), E)])
-                    act(v("AH", c0, c1), H, AF.Abs)
+                    for h0 in range(c0, c1, 512):
+                        h1 = min(c1, h0 + 512)
+                        H = v("H%d" % (piece % 2), 0, h1 - h0); piece += 1
+                        mm(H, [(m, v(x[0], h0, h1)) for m, x in terms + [(v("I"), E)]])
+                        act(v("AH", h0, h1), H, AF.Abs)
                     ts(v("U", c0, c1), E, 1.0 / 32, A.add, 31.0 / 1024, A.max)
                 SB = "SA" if ci % 2 == 0 else "SB"
                 s0 = 0
@@ -400,7 +448,11 @@ def rank_program(g, core, T, topo):
                     s0 += w
                 c0, c1 = 16 * l0, 16 * l1
                 so, po, lo, fo = 2 * l0, 5 * l0, l0 // 4, 64 * ci
-                act(v("S", so, so + 2 * n), v(SB, 0, 2 * n), AF.Sign, bias=v("nb"))
+                quick = QUICK[ci]
+                if quick & 1:
+                    ts(v("S", so, so + 2 * n), v(SB, 0, 2 * n), v("pb"), A.is_gt, 2.0, A.mult)
+                else:
+                    act(v("S", so, so + 2 * n), v(SB, 0, 2 * n), AF.Sign, bias=v("nb"))
                 col = v("PR", po + 4 * n, po + 5 * n)
                 tt(col, v("S", so, so + n), v("S", so + n, so + 2 * n), A.min)
                 tt(v("key", l0, l1), v(SB, 2 * n, 3 * n), col, A.add)
@@ -411,28 +463,43 @@ def rank_program(g, core, T, topo):
                 tr(oh, v("ohT", l0, l1))
                 for q in ((2, 0, 1) if lev < LV - 1 else (2,)):
                     tt(v("PR", po + (q + 1) * n, po + (q + 2) * n), oh, v(kf, 3 * l0 + q * n, 3 * l0 + (q + 1) * n), A.mult)
-                tt(v("PR", po, po + n), oh, v("jc", 0, n), A.mult)
-                mm(v("LS", 0, 5 * nc), [(sel("E16", r), v("PR", po + r, po + 5 * n, 16)) for r in range(16)])
+                j0 = 1 if ci == 0 else 0
+                if j0 == 0:
+                    tt(v("PR", po, po + n), oh, v("jc", 0, n), A.mult)
+                mm(v("LS", j0 * nc, 5 * nc), [(sel("E16", r), v("PR", po + j0 * n + r, po + 5 * n, 16)) for r in range(16)])
+                zold = (Xw, v(Lu, lo + 3 * nc, lo + 4 * nc)) if j0 else (v("Bt", c0, c1), v(Lu, lo, lo + nc))
+                fj, lj = fo + j0 * nc, lo + j0 * nc
                 mm(v(ZB, 192, 192 + 2 * n), [(v("BO"), v("PR", po + 3 * n, po + 5 * n)), (v("I"), v("MZ", NM - n, NM + n))])
-                act(v("Lf", fo, fo + 5 * nc), v("LS", 0, 5 * nc), AF.Identity, bias=2048.0)
-                cp(v(Lu, lo, lo + 4 * nc), v("Lf", fo, fo + 4 * nc))
+                if quick & 2:
+                    ts(v("Lf", fj, fo + 5 * nc), v("LS", j0 * nc, 5 * nc), 2048.0, A.add)
+                    ts(v(Lu, lj, lo + 4 * nc), v("LS", j0 * nc, 4 * nc), 2048.0, A.add)
+                else:
+                    act(v("Lf", fj, fo + 5 * nc), v("LS", j0 * nc, 5 * nc), AF.Identity, bias=2048.0)
+                    cp(v(Lu, lj, lo + 4 * nc), v("Lf", fj, fo + 4 * nc))
                 act(v("ZR", l0, l1), v(ZB, 192, 192 + n), AF.Identity, bias=2048.0)
-                act(v("RC", lev * L + l0, lev * L + l1), v(ZB, 192 + n, 192 + 2 * n), AF.Relu, bias=-1.0)
+                act(v("RC", lev * L + l0, lev * L + l1), v(ZB, 192 + n, 192 + 2 * n), AF.Relu, bias=-1.0 - 16.0 * (quick & 1))
+                if lev < LV - 1:
+                    act(v("ohB", l0, l1), oh, AF.Copy, scale=float(nbase + 2 * L))
                 mx = v("mxL", l0 // 16, l1 // 16)
                 if lev == 0:
                     cp(mx, v("Lf", fo + 4 * nc, fo + 5 * nc))
                 else:
                     tt(mx, mx, v("Lf", fo + 4 * nc, fo + 5 * nc), A.max)
-                tt(v("eq", l0, l1), (v("Lf", fo, fo + 5 * nc), bc[ci]), v("ZR", l0, l1), A.is_equal)
+                tt(v("eq", l0, l1), (v("Lf", fj, fo + 5 * nc), bc[ci]), v("ZR", l0, l1), A.is_equal)
                 scan(v("sc", l0, l1), v("d0", 0, n), v("eq", l0, l1), 0.0, A.mult, A.max)
                 tg = v("tg", l0 // 16, l1 // 16)
                 tt(tg, v("sc", l0 + 15, l1, 16), v("Lf", fo + 3 * nc, fo + 4 * nc), A.max)
                 cp(v("Tu", l0 // 8, l1 // 8, 2), tg)
-                tt(v("sm", l0, l1), (v("Bt", c0, c1), v(Lu, lo, lo + nc)), v(yv, l0, l1), A.add)
-                act(v("hb", l0, l1), v("sm", l0, l1), AF.Identity, bias=127.75, scale=0.5)
+                if quick & 4:
+                    tt(v("sm", l0, l1), zold, v(yv, l0, l1), A.add)
+                    ts(v("hb", l0, l1), v("sm", l0, l1), 0.5, A.mult, 127.75, A.add)
+                else:
+                    act(v("sm", l0, l1), zold, AF.Copy)
+                    mm(v("LS", 384, 384 + n), [(v("I"), v(yv, l0, l1)), (v("I"), v("sm", l0, l1))])
+                    act(v("hb", l0, l1), v("LS", 384, 384 + n), AF.Identity, bias=127.75, scale=0.5)
             if lev == LV - 1:
-                ts(v("tl"), v("mxL"), 2049.0, A.is_le, 8192.0, A.mult)
-                tt(v("tl2"), v("tl"), v("nlv"), A.min)
+                tt(v("tl"), v("mxL"), v("thL"), A.is_le)
+                tt(v("tl2"), v("tl"), v("nlv"), A.mult)
                 bn = v("bL%d" % (t + 1))
                 if t < TV - 1:
                     snd = "snd%d" % t
@@ -449,34 +516,51 @@ def rank_program(g, core, T, topo):
                     store("sp", "s_so", T.so[:], bn, 2.0)
             for c in range(L // 16 - 1, -1, -1):
                 tt((v("X"), v("Tu", 2 * c, 2 * c + 1)), v("hb", 16 * c, 16 * c + 16), v("n128"), A.add)
-            act(v("r1"), v("key"), AF.Identity, bias=MAGIC, scale=8192.0)
-            act(v("r2"), v("r1"), AF.Identity, bias=-MAGIC / 8192, scale=1.0 / 8192)
-            tt(v("vt"), v("key"), v("r2"), A.is_gt)
-            for (l0, l1) in CHUNKS:
+            for ci, (l0, l1) in enumerate(CHUNKS):
                 n, so = l1 - l0, 2 * l0
-                mm(v("MX", l0, l1), [(v("I2"), v("S", so + n, so + 2 * n)), (v("NI"), v("S", so, so + n)), (v("I"), v("vt", l0, l1))])
-            act(v("sg"), v("MX", 0, L), AF.Sign, bias=-1.5)
-            for (l0, l1) in CHUNKS:
-                n = l1 - l0
-                mm(v("MY", l0, l1), [(v("I16"), v(kf, 3 * l0 + 2 * n, 3 * l1)), (v("IN"), v("sg", l0, l1))])
-                mm(v("MY", L + l0, L + l1), [(v("I16"), v(kf, 3 * l0, 3 * l0 + n)), (v("IP"), v("sg", l0, l1))])
-            act(v("x1"), v("MY", 0, L), AF.Copy)
-            mo = v("Cf", step * L, step * L + L)
-            if lev < LV - 1:
-                act(v("ohB"), v("OH", 0, L), AF.Copy, scale=float(nbase + 2 * L))
-                mm(v("MX", L, 2 * L), [(v("I"), v("lan")), (v("I"), v("ohB"))])
-                tt(v("m1"), v("MY", L, 2 * L), v("x1"), A.max)
-                tt(mo, v("MX", L, 2 * L), v("m1"), A.max)
-            else:
-                tt(mo, v("MY", L, 2 * L), v("x1"), A.max)
+                key, r1, r2, sg = v("key", l0, l1), v("r1", l0, l1), v("r2", l0, l1), v("sg", l0, l1)
+                act(r1, key, AF.Identity, bias=MAGIC, scale=8192.0)
+                if WIDE[0]:
+                    act(v("k2", l0, l1), key, AF.Identity, bias=0.5, scale=8192.0)
+                    act(r2, v("k2", l0, l1), AF.Identity, bias=MAGIC)
+                    vote = [(v("I32"), r2), (v("NI32"), r1)]
+                else:
+                    act(r2, r1, AF.Identity, bias=-MAGIC / 8192, scale=1.0 / 8192)
+                    tt(v("vt", l0, l1), key, r2, A.is_gt)
+                    vote = [(v("I"), v("vt", l0, l1))]
+                mm(v("MX", l0, l1), vote + [(v("I2"), v("S", so + n, so + 2 * n)), (v("NI"), v("S", so, so + n))])
+                act(sg, v("MX", l0, l1), AF.Sign, bias=-1.5 - (QUICK[ci] & 1))
+                out = [(v("NI2"), v("ohB", l0, l1))] if WIDE[1] and lev < LV - 1 else []
+                X1, X2, X3 = v("MY", so, so + n), v("MY", so + n, so + 2 * n), v("MX", L + l0, L + l1)
+                mm(X1, [(v("I16"), v(kf, 3 * l0 + 2 * n, 3 * l1)), (v("IN"), sg)] + out)
+                mm(X2, [(v("I16"), v(kf, 3 * l0, 3 * l0 + n)), (v("IP"), sg)] + out)
+                if lev < LV - 1:
+                    mm(X3, [(v("I"), v("lan", l0, l1)), (v("I"), v("ohB", l0, l1))])
+                mo, x1 = v("Cf", step * L + l0, step * L + l1), v("x1", l0, l1)
+                if WIDE[1]:
+                    act(v("x12", so, so + 2 * n), v("MY", so, so + 2 * n), AF.Relu)
+                    parts = [v("x12", so, so + n), v("x12", so + n, so + 2 * n)]
+                    if lev < LV - 1:
+                        act(x1, X3, AF.Relu)
+                        parts.append(x1)
+                    mm(v("MX", l0, l1), [(v("I32"), p) for p in parts])
+                    act(mo, v("MX", l0, l1), AF.Copy)
+                else:
+                    act(x1, X1, AF.Copy)
+                    if lev < LV - 1:
+                        tt(v("m1", l0, l1), X2, x1, A.max)
+                        tt(mo, X3, v("m1", l0, l1), A.max)
+                    else:
+                        tt(mo, X2, x1, A.max)
             if t < TV - 1:
-                cp(v("C", nbase, nbase + L), mo)
+                cp(v("C", nbase, nbase + L), v("Cf", step * L, step * L + L))
         store("sp", "s_c%d" % t, T.co[:, t * 576:(t + 1) * 576], v("Cf", t * 576, (t + 1) * 576), 3.0)
         mm(v("MX", 2 * L - L, 2 * L), [(v("IP"), v("RC", k * L, k * L + L)) for k in range(LV)])
         x0 = v("X", lim, lim + L) if t < 2 else v("XN", 0, L)
         if t < TV - 1:
             act(v("sa"), v("MX", L, 2 * L), AF.Sign, bias=-1.0, accum=v("acc"))
             ts(v("nb"), v("acc"), -0.5, A.mult, v("nh"), A.add)
+            ts(v("pb"), v("acc"), 0.5, A.mult, v("nh"), A.subtract)
         tt(v("yt"), v("MX", L, 2 * L), v(yv), A.min)
         tt(v("yd"), v("yt"), x0, A.subtract)
         act(v("ys%d" % t), v("yd"), AF.Abs)

@@ -2,14 +2,21 @@ from concourse.mybir import AluOpType, ActivationFunctionType
 import numpy as np
 
 V, L, TV, LV, HOP = 2304, 192, 3, 3, 3
+N = L // 2
 XW = V + 2 * LV * L
-PLAN = [(64, 192, (16, -32, 16, 32, 32), (64, 64)), (0, 64, (32, 32), (64,))]
-PLACE = ["LS", "OH"]
-QUICK = [0, 6]
-LEAD = [16]
-WIDE = [0, 0]
-NM = 160
-MAGIC = 12582912.0
+XO = 96
+WALK = (("b", 0, 16), ("F", 0, 16), ("B", 16, 48), ("E", 0, 16), ("C", 16, 48), ("B", 48, 80), ("E", 16, 48),
+        ("C", 48, 80), ("B", 80, 96), ("E", 48, 80), ("F", 80, 96), ("E", 80, 96))
+UCUT = ((0, 48), (48, 96))
+HCUT = ((0, 16), (16, 48), (48, 80), (80, 96))
+SUMS = {"AF": ((0, 96),), "E": ((0, 96),), "U": ((0, 96),), "AH": ((0, 64), (64, 96))}
+CLIP_ON_VECTOR = False
+SOFT = False
+AFT = True
+COL_ON_VECTOR = False
+ROUND_ON_SCALAR = False
+WALK0 = None
+MAGIC = 1536.0
 
 B16, F16, F32, I32, U16 = "bfloat16", "float16", "float32", "int32", "uint16"
 SIZES = {B16: 2, F16: 2, F32: 4, I32: 4, U16: 2}
@@ -19,54 +26,51 @@ def _sb(n, d):
     return ("sbuf", [128, n], d)
 
 
-SCRATCH = {
-    "X": _sb(XW + 16, B16), "XN": _sb(576, B16), "C": _sb(XW, I32), "Cf": _sb(1728, F32),
-    "sbi": _sb(12, I32), "iai": _sb(12, I32), "ici": _sb(12, I32), "thi": _sb(1, I32),
-    "y0": _sb(L, B16), "y1": _sb(L, B16), "y2": _sb(L, B16),
-    "ys0": _sb(L, B16), "ys1": _sb(L, B16), "ys2": _sb(L, B16), "yt": _sb(L, B16), "yd": _sb(L, B16),
-    "au": _sb(12, U16), "bu": _sb(12, U16), "cu": _sb(12, U16),
-    "cin": _sb(12, U16), "acin": _sb(24, U16), "ain": _sb(12, U16), "snd0": _sb(24, U16), "snd1": _sb(24, U16),
-    "aL": _sb(12, F32), "bL0": _sb(12, F32), "bL1": _sb(12, F32), "bL2": _sb(12, F32), "bL3": _sb(12, F32),
-    "an": _sb(12, F32), "mxL": _sb(12, F32), "tl": _sb(12, F32), "tl2": _sb(12, F32), "nlv": _sb(12, F32),
-    "Bt": _sb(3072, B16), "E": _sb(3072, B16), "Fd": _sb(3072, B16), "U": _sb(3072, F16),
-    "AF": _sb(3072, B16), "AH": _sb(3072, B16),
-    "ku0": _sb(576, U16), "ku1": _sb(576, U16), "kf0": _sb(576, F16), "kf1": _sb(576, F16),
-    "Lu0": _sb(48, U16), "Lu1": _sb(48, U16), "Lf": _sb(192, F32), "PV": _sb(576, B16),
-    "S": _sb(384, B16), "PR": _sb(960, F16), "key": _sb(L, F32), "keyT": _sb(L, F32), "FT": _sb(L, F32),
-    "ohT": _sb(L, F32), "ohB": _sb(L, B16), "ZR": _sb(L, F32), "eq": _sb(L, F32), "sc": _sb(L, F32),
-    "tg": _sb(12, F32), "Tu": _sb(24, U16), "sm": _sb(L, B16), "hb": _sb(L, B16),
-    "RC": _sb(576, B16), "r1": _sb(L, F32), "r2": _sb(L, F32), "vt": _sb(L, B16), "sg": _sb(L, B16),
-    "x1": _sb(L, F32), "m1": _sb(L, F32), "sa": _sb(L, B16), "acc": _sb(1, F32), "nb": _sb(1, F32), "nh": _sb(1, F32),
-    "I32": _sb(128, F32), "NI32": _sb(128, F32), "NI2": _sb(128, B16), "k2": _sb(L, F32), "x12": _sb(2 * L, F32),
-    "pb": _sb(1, F32), "thL": _sb(12, F32),
-    "pid": _sb(1, I32), "ri": _sb(1, I32), "rf": _sb(1, F32), "pf": _sb(1, F32), "g16": _sb(1, F32), "g15": _sb(1, F32),
-    "kc": _sb(1, F32), "dc": _sb(1, F32), "xr": _sb(144, F32), "blk": _sb(128, F32), "rp": _sb(NM, F32),
-    "Ct": _sb(3072, B16), "nv": _sb(L, B16), "ji": _sb(NM, F32), "I": _sb(128, B16), "NI": _sb(128, B16), "I2": _sb(128, B16), "IP": _sb(128, B16),
-    "IN": _sb(128, B16), "I16": _sb(128, F16), "E1": _sb(144, B16), "En": _sb(144, B16), "E2": _sb(144, F16),
-    "E16": _sb(144, F16), "BO": _sb(128, F16), "MZ": _sb(2 * NM, B16), "kk": _sb(NM, F16), "rst": _sb(NM, F32),
-    "d0": _sb(NM, F32), "d1": _sb(NM, F32), "jc": _sb(NM, F16), "lan": _sb(L, B16), "li": _sb(40, I32),
-    "lu": _sb(40, U16), "lf": _sb(12, F32), "laneL": _sb(12, F32), "n128": _sb(16, B16),
+STREAM = {
+    "X": (XW + XO, B16), "C": (XW, I32), "NV": (9 * N, B16), "Cf": (9 * N, F32), "Ci": (6 * N, I32),
+    "nm": (18, I32), "thi": (1, I32), "nt": (2, F32), "TD": (128, F16),
+    "ya": (N, B16), "yb": (N, B16), "yc": (N, B16), "ys": (3 * N, B16), "yt": (2 * N, B16),
+    "L0": (18, U16), "acin": (12, U16), "ain": (8, U16), "snd": (24, U16), "nf": (66, F32), "ab": (16, B16),
+    "Bt": (16 * N, B16), "E": (16 * N, B16), "Fd": (16 * N, B16), "U": (16 * N, F16),
+    "AF": (16 * N, B16), "AH": (16 * N, B16), "Ct": (16 * N, B16),
+    "ku": (6 * N, U16), "kf": (8 * N, F16), "Lu": (36, U16), "PV": (4 * N, B16),
+    "S": (384 + N, B16), "key": (128, F32), "FT": (128, F32), "oh": (128, F16), "rr": (128, F32), "sel": (128, F16),
+    "PR": (4 * N, F16), "tg": (12, F32), "zl": (36, F16), "eq": (6 * N, F16), "sc": (6 * N, F16), "Tu": (12, U16),
+    "hb": (3 * N, B16), "x2": (N, F32),
 }
-BANKS = ("H0", "H1", "SA", "SB", "OH", "LS", "MX", "MY")
+SCRATCH = {"%s%d" % (k, s): _sb(*w) for k, w in STREAM.items() for s in range(2)}
+SCRATCH.update({
+    "bu": _sb(12, U16), "cin": _sb(12, U16),
+    "pi": _sb(4, I32), "pc": _sb(12, F32), "xr": _sb(144, F32), "w1": _sb(128, F32), "w2": _sb(128, F32),
+    "w3": _sb(128, F32), "rp": _sb(144, F32), "li": _sb(24, I32), "lu": _sb(24, U16), "nb": _sb(12, F32),
+    "lf": _sb(18, F32), "gq": _sb(16, F32),
+    "IB": _sb(5 * 128, B16), "IH": _sb(3 * 128, F16), "SB": _sb(4 * 128, B16), "SH": _sb(5 * 128, F16),
+    "E16": _sb(144, F16), "GB": _sb(24, B16), "GH": _sb(8, F16), "one": _sb(N, F16), "KD": _sb(384, F16),
+    "rq": _sb(6 * N, F32), "sp": _sb(12, F32), "d0": _sb(6 * N, F16), "rst": _sb(128, F32), "dm": _sb(N, B16), "DG": _sb(14 * N, F16), "n128": _sb(N, B16),
+})
+BANKS = ("H0", "H1", "KA0", "KB0", "M0", "KA1", "KB1", "M1")
 for _b in BANKS:
     SCRATCH[_b] = ("psum", [128, 512], F32)
 
-DMAS = ["l_sb", "l_ia", "l_ic", "l_th", "l_y", "l_ch", "l_x", "s_c0", "s_c1", "s_c2", "s_xn", "s_x0", "s_x1", "s_so", "s_yo"]
-ARRIVE = ["r_c", "r_a0", "r_y0", "r_a1", "r_y1"]
-SEMAPHORES = ["pe", "dve", "act", "pool", "sent"] + DMAS + ARRIVE
+OWN = ["l_c", "l_x", "l_n", "l_y", "xs", "cs0", "cs1", "cs2"]
+ARRIVE = ["r_c"] + [k + str(s) for k in ("r_a0", "r_y0", "r_a1", "r_y1") for s in range(2)]
+SEMAPHORES = ["pe", "dve", "act", "pool", "sent", "out"] + [k + str(s) for k in OWN for s in range(2)] + ARRIVE
 
 CY, PCY = np.array([0.92e-3, 1.04e-3, 0.85e-3, 1.2e-3]), np.array([0.47e-3, 0.52e-3, 0.44e-3, 0.6e-3])
 GA, SCA = np.array([1.56, 1.56, 1.2, 2.0]), np.array([3.8, 3.8, 2.5, 5.5])
 HS, HO, WEIGHT = (0.13, 0.08, 0.2, 0.15), (0.27, 0.2, 0.33, 0.3), (1.0, 1.0, 1.0, 0.75)
 HOP_SAME, HOP_OTHER = HS[0], HO[0]
-LOOKS, ROUNDS, TRIES, SOFT = (0.2, 0.5, 0.35), 3, 20, False
-POLISH = 2200
+LOOKS, ROUNDS, TRIES = (0.2, 0.5, 0.35), 3, 20
+BEATS = (10.0, 12.0, 9.0, 14.0, 11.0)
+POLISH = 30000
+SETS, HEAT, WIDE = (0, 3), 0.2, 0.1
+KINDS = ("a", "b", "c")
 
 
-def one_pass(qs, dur, lat, pred, succ, free_pairs, prio, back, look):
+def one_pass(qs, dur, lat, pred, succ, free_pairs, prio, back, look, early=None):
     n = len(qs)
     left = [len(p) for p in pred]
-    ready_at = [lat[i] if back else 0.0 for i in range(n)]
+    ready_at = list(early) if early else [lat[i] if back else 0.0 for i in range(n)]
     ready, free, order = {}, {}, []
     start, fin = [0.0] * n, [0.0] * n
     for i in range(n):
@@ -106,6 +110,15 @@ PLANNED = {}
 
 def order_ops(ops):
     n = len(ops)
+    reach = []
+    for o in ops:
+        m = 0
+        for d in o["deps"]:
+            m |= reach[d]
+        o["deps"] = [d for d in o["deps"] if not m >> d & 1]
+        for d in o["deps"]:
+            m |= 1 << d
+        reach.append(0 if o["q"] == "net" or o["sem"] == ("sent", 0) else m)
     qs, dur, lat = [o["q"] for o in ops], [o["dur"] for o in ops], [o["lat"] for o in ops]
     pred = [o["deps"] + o["soft"] for o in ops]
     pairs = {(d, i) for i, o in enumerate(ops) for d in o["soft"]}
@@ -115,14 +128,21 @@ def order_ops(ops):
         for i in range(n):
             for d in pred[i]:
                 succ[d].append(i)
-        base = [0.0] * n
-        for i in range(n - 1, -1, -1):
-            base[i] = dur[i] + lat[i] + max([base[s] + HOP_OTHER for s in succ[i]] + [0.0])
+        def urgency(beat):
+            base = [0.0] * n
+            for i in range(n - 1, -1, -1):
+                base[i] = dur[i] + lat[i] + max(
+                    [base[s] + (HOP_OTHER if qs[s] != qs[i] else 0.0 if (i, s) in pairs else HOP_SAME)
+                     for s in succ[i]] + [0.0])
+                if "gate" in ops[i]:
+                    base[i] = max(base[i], (2 * TV * LV + 1 - ops[i]["gate"]) * beat)
+            return base
+
         best = None
         rng = np.random.default_rng(1)
         for trial in range(TRIES):
             look = LOOKS[trial % len(LOOKS)]
-            prio = base if best is None or trial % 4 == 0 else [-s for s in best[1]]
+            prio = urgency(BEATS[trial // 2 % len(BEATS)]) if trial % 2 == 0 else [-s for s in best[1]]
             prio = [p + float(e) for p, e in zip(prio, rng.normal(0.0, 0.3 if trial else 1e-9, n))]
             for _ in range(ROUNDS):
                 fw = one_pass(qs, dur, lat, pred, succ, pairs, prio, False, look)
@@ -130,39 +150,104 @@ def order_ops(ops):
                     best = fw
                 prio = one_pass(qs, dur, lat, succ, pred, pairs, fw[2], True, look)[2]
         durs = [[float(x) for x in np.broadcast_to(o["durs"], CY.shape)] for o in ops]
+        same = [[d for d in o["deps"] if qs[d] == o["q"]] for o in ops]
+        other = [[d for d in o["deps"] if qs[d] != o["q"]] for o in ops]
 
-        def length(order):
-            total = 0.0
+        def lengths(order):
+            res = []
             for m in range(len(CY)):
                 hs, ho = float(HS[m]), float(HO[m])
                 free, fin = {}, [0.0] * n
                 for i in order:
                     q = qs[i]
                     t = free.get(q, 0.0)
-                    for d in pred[i]:
-                        r = fin[d] + (hs if qs[d] == q else ho)
-                        if r > t:
-                            t = r
+                    for d in same[i]:
+                        if fin[d] + hs > t:
+                            t = fin[d] + hs
+                    for d in other[i]:
+                        if fin[d] + ho > t:
+                            t = fin[d] + ho
                     free[q] = t + durs[i][m]
                     fin[i] = free[q] + lat[i]
-                total += max(fin) * WEIGHT[m]
-            return total
+                res.append(max(fin))
+            return res
 
-        score = length(best[0])
+        def length(order):
+            return sum(x * w for x, w in zip(lengths(order), WEIGHT))
+
+        def held(order, m):
+            hs, ho, dm = float(HS[m]), float(HO[m]), col[m]
+            free, last, fin, why, start = {}, {}, [0.0] * n, [None] * n, [0.0] * n
+            for i in order:
+                q = qs[i]
+                t, w = free.get(q, 0.0), last.get(q)
+                for d in same[i]:
+                    if fin[d] + hs > t:
+                        t, w = fin[d] + hs, -1 - d
+                for d in other[i]:
+                    if fin[d] + ho > t:
+                        t, w = fin[d] + ho, -1 - d
+                start[i], why[i], last[q] = t, w, i
+                free[q] = t = t + dm[i]
+                fin[i] = t + lat[i]
+            end = max(fin)
+            i, found = fin.index(end), []
+            while why[i] is not None:
+                if why[i] >= 0:
+                    found.append((why[i], i))
+                i = why[i] if why[i] >= 0 else -1 - why[i]
+            return end, start, found
+
+        def judge(order):
+            res = [held(order, m) for m in SETS]
+            return sum(r[0] * WEIGHT[m] for r, m in zip(res, SETS)), order, res
+
+        col = [[d[m] for d in durs] for m in range(len(CY))]
+        alike = {(o["kind"][1:], o["turn"]): i for i, o in enumerate(ops) if o["kind"][0] != "start"}
+        now = top = judge(best[0])
         for trial in range(POLISH):
-            a = float(rng.uniform(-5.0, best[3]))
-            b = a + float(rng.uniform(3.0, 14.0))
-            noise = rng.normal(0.0, (0.15, 0.4, 1.0)[trial % 3], n)
-            prio = [-s + (float(e) if a < s < b else 0.0) for s, e in zip(best[1], noise)]
-            fw = one_pass(qs, dur, lat, pred, succ, pairs, prio, False, LOOKS[trial % 2])
-            sc = length(fw[0])
-            if sc <= score:
-                best, score = fw, sc
-        PLANNED[keyed] = best
-    order, start, _fin, end = PLANNED[keyed]
+            found = now[2][trial % len(SETS)][2]
+            j = int(rng.integers(len(found)))
+            a, b = found[j]
+            for _ in range(int(rng.integers(3))):
+                j -= 1 - 2 * (trial % 2)
+                if 0 <= j < len(found) and found[j][1] == a:
+                    a = found[j][0]
+                elif 0 <= j < len(found) and found[j][0] == b:
+                    b = found[j][1]
+            key = [0.0] * n
+            for p, i in enumerate(now[1]):
+                key[i] = float(p)
+            moves = [(a, b)]
+            if rng.random() < WIDE:
+                ka, kb, gap = ops[a]["kind"][1:], ops[b]["kind"][1:], ops[b]["turn"] - ops[a]["turn"]
+                moves = [(alike[ka, u], alike[kb, u + gap]) for u in range(2 * TV * LV)
+                         if (ka, u) in alike and (kb, u + gap) in alike and key[alike[ka, u]] < key[alike[kb, u + gap]]]
+            if trial % 2:
+                for a, b in moves:
+                    key[b] = key[a] - 0.5
+                for i in range(n - 1, -1, -1):
+                    for d in pred[i]:
+                        if key[d] >= key[i]:
+                            key[d] = key[i] - 1e-4
+            else:
+                for a, b in moves:
+                    key[a] = key[b] + 0.5
+                for i in range(n):
+                    for d in pred[i]:
+                        if key[d] >= key[i]:
+                            key[i] = key[d] + 1e-4
+            new = judge(np.argsort(key, kind="stable").tolist())
+            if new[0] <= now[0] + HEAT * (1.0 - trial / POLISH) * float(rng.random()) ** 2:
+                now = new
+                if new[0] < top[0]:
+                    top = new
+        best = (top[1], top[2][0][1], None, 0.0)
+        PLANNED[keyed] = best + (lengths(best[0]),)
+    order, start, _fin, _end, ends = PLANNED[keyed]
     for i in range(n):
         ops[i]["start"] = start[i]
-    return order, end
+    return order, ends
 
 
 def rank_program(g, core, T, topo):
@@ -178,17 +263,19 @@ def rank_program(g, core, T, topo):
     n_out = len(topo.engines(core, dst))
     n_in = len(topo.engines(src, core))
     Q = {"pe": g.tensor, "dve": g.vector, "act": g.scalar, "pool": g, "sp": g.sync}
-    ops, hist, bank_last = [], {}, {}
-    CHUNKS = [c[:2] for c in PLAN]
-    NVB, ZB = PLACE
+    ops, hist, bank_last, batches, totals, turn, BULK = [], {}, {}, {}, {}, {}, [False]
+    closer, where = {}, ["start", 0, {}]
 
-    def v(name, a=0, b=None, s=1):
-        return (name, a, SCRATCH[name][1][1] if b is None else b, s)
+    def v(name, a=0, b=None, s=1, p=(0, 128)):
+        return (name, a, SCRATCH[name][1][1] if b is None else b, s, p[0], p[1])
+
+    def part(w, p):
+        return w[:4] + tuple(p)
 
     def ap(w):
         if len(w) == 2:
             return ap(w[0]).indirect(ap(w[1]))
-        return T[w[0]][:, w[1]:w[2]] if w[3] == 1 else T[w[0]][:, w[1]:w[2]:w[3]]
+        return T[w[0]][w[4]:w[5], w[1]:w[2]] if w[3] == 1 else T[w[0]][w[4]:w[5], w[1]:w[2]:w[3]]
 
     def cnt(w):
         return 16 * (w[1][2] - w[1][1]) if len(w) == 2 else len(range(w[1], w[2], w[3]))
@@ -196,7 +283,7 @@ def rank_program(g, core, T, topo):
     def narrow(*ws):
         return all(SIZES[SCRATCH[w[0]][2]] == 2 for w in ws)
 
-    def add(q, fn, rd, wr, dur, lat=0.0, sem=None, after=()):
+    def add(q, fn, rd, wr, dur, lat=0.0, sem=None, after=(), acc=None, tag="", free=False):
         i = len(ops)
         r2, w2 = [], []
         for w in rd:
@@ -209,9 +296,12 @@ def rank_program(g, core, T, topo):
         deps, soft = set(after), set()
         for lst, isw in ((r2, False), (w2, True)):
             for w in lst:
-                for (a, b, j, jw) in hist.get(w[0], ()):
-                    if (isw or jw) and a < w[2] and w[1] < b:
-                        if isw and ops[j]["q"] == q and q in ("dve", "act", "pe"):
+                for (a, b, pa, pb, j, jw) in hist.get(w[0], ()):
+                    if (isw or jw) and a < w[2] and w[1] < b and pa < w[5] and w[4] < pb:
+                        if acc and isw and ops[j]["q"] == "pe":
+                            if acc == "close" or not ops[j]["acc"]:
+                                soft.add(j)
+                        elif free and isw and ops[j]["free"]:
                             soft.add(j)
                         else:
                             deps.add(j)
@@ -224,15 +314,23 @@ def rank_program(g, core, T, topo):
         for lst, isw in ((r2, False), (w2, True)):
             for w in lst:
                 h = hist.setdefault(w[0], [])
-                if isw:
-                    h[:] = [e for e in h if not (w[3] == 1 and w[1] <= e[0] and e[1] <= w[2])]
-                h.append((w[1], w[2], i, isw))
+                if isw and not acc:
+                    h[:] = [e for e in h if not (w[3] == 1 and w[1] <= e[0] and e[1] <= w[2]
+                                                 and w[4] <= e[2] and e[3] <= w[5])]
+                h.append((w[1], w[2], w[4], w[5], i, isw))
+        for d in list(deps):
+            if ops[d]["sem"] in batches:
+                deps.update(batches[ops[d]["sem"]])
+        if BULK[0]:
+            soft.update(turn.get(q, ()))
+            turn[q] = [i]
         deps.discard(i)
         soft.discard(i)
-        if not SOFT:
-            deps |= soft
-        ops.append({"q": q, "fn": fn, "deps": sorted(deps), "soft": sorted(soft - deps), "durs": dur,
-                    "dur": float(np.ravel(dur)[0]), "lat": lat, "sem": sem})
+        ops.append({"q": q, "fn": fn, "acc": acc, "free": free, "deps": sorted(deps), "soft": sorted(soft - deps), "durs": dur,
+                    "dur": float(np.ravel(dur)[0]), "lat": lat, "sem": sem, "tag": tag or (w2[0][0] if w2 else "")})
+        name = (where[0], q, ops[i]["tag"].rstrip("01"))
+        where[2][name] = where[2].get(name, 0) + 1
+        ops[i]["kind"], ops[i]["turn"] = name + (where[2][name],), where[1]
         return i
 
     def vdur(out, ins, per):
@@ -249,11 +347,12 @@ def rank_program(g, core, T, topo):
         return [x for x in xs if isinstance(x, tuple)]
 
     def tt(out, a, b, op):
-        per = 1.0 if (len(a) == 4 and a[0] in BANKS) or b[0] in BANKS else 1.5
-        return add("dve", lambda: g.vector.tensor_tensor(ap(out), ap(a), ap(b), op), [a, b], [out], vdur(out, [a], per))
+        per = 1.0 if (len(a) > 2 and a[0] in BANKS) or b[0] in BANKS else 1.5
+        return add("dve", lambda: g.vector.tensor_tensor(ap(out), ap(a), ap(b), op), [a, b], [out], vdur(out, [a], per),
+                   free=SOFT and len(out) == 2)
 
     def ts(out, a, s1, op0, s2=None, op1=None):
-        per = 0.5 if len(a) == 4 and narrow(out, a) else 1.0
+        per = 0.5 if len(a) > 2 and narrow(out, a) else 1.0
         if op1 is None:
             fn = lambda: g.vector.tensor_scalar(ap(out), ap(a), sc_(s1), None, op0)
         else:
@@ -261,36 +360,37 @@ def rank_program(g, core, T, topo):
         return add("dve", fn, [a] + cols(s1, s2), [out], vdur(out, [a], per))
 
     def cp(out, a):
-        per = 0.5 if len(a) == 4 and narrow(out, a) else 1.0
+        per = 0.5 if len(a) > 2 and narrow(out, a) else 1.0
         return add("dve", lambda: g.vector.tensor_copy(ap(out), ap(a)), [a], [out], vdur(out, [a], per))
 
     def scan(out, d0, d1, init, op0, op1):
+        per = 0.5 if narrow(out, d0, d1) else 1.0
         return add("dve", lambda: g.vector.tensor_tensor_scan(ap(out), ap(d0), ap(d1), init, op0, op1),
-                   [d0, d1], [out], vdur(out, [d1], 1.0))
-
-    def tr(out, a):
-        return add("dve", lambda: g.vector.transpose(ap(out), ap(a)), [a], [out], vdur(out, [a], 1.0))
+                   [d0, d1], [out], vdur(out, [d1], per))
 
     def fill(out, c):
         return add("dve", lambda: g.vector.memset(ap(out), c), [], [out], vdur(out, [], 0.5))
 
-    def act(out, a, func, bias=0.0, scale=1.0, accum=None):
+    def act(out, a, func, bias=0.0, scale=1.0):
         dur = 0.065 + cnt(out) * GA * CY if len(a) == 2 else max(64, cnt(out)) * CY + 0.03
-        if accum is None:
-            fn = lambda: g.scalar.activation(ap(out), ap(a), func, bias=sc_(bias), scale=scale)
-        else:
-            fn = lambda: g.scalar.activation(ap(out), ap(a), func, bias=sc_(bias), scale=scale, accum_out=ap(accum))
-        return add("act", fn, [a] + cols(bias), [out] + cols(accum), dur)
+        fn = lambda: g.scalar.activation(ap(out), ap(a), func, bias=sc_(bias), scale=scale)
+        return add("act", fn, [a] + cols(bias), [out], dur)
 
-    def mm(out, terms):
+    def mms(terms, stop=True, each=False, into=None):
+        i = len(ops)
+
         def fn():
             last = None
-            for k, (w, x) in enumerate(terms):
-                last = g.tensor.matmul(ap(out), ap(w), ap(x), k == 0, k == len(terms) - 1)
+            for k, (o, w, x) in enumerate(terms):
+                run = each or len(terms)
+                last = g.tensor.matmul(ap(o), ap(w), ap(x), into is None and k % run == 0, stop and k % run == run - 1)
             return last
-        rd = list({z: 0 for t in terms for z in t})
-        return add("pe", fn, rd, [out],
-                   sum(1 if narrow(x) else 4 for _, x in terms) * max(64, cnt(out)) * PCY + 0.05)
+        rd = list({z: 0 for t in terms for z in t[1:]})
+        wr = list({t[0]: 0 for t in terms})
+        return add("pe", fn, rd, wr, sum(max(min(64, cnt(w)), cnt(o)) for o, w, x in terms) * PCY + 0.05, acc=into)
+
+    def mm(out, terms):
+        return mms([(out, w, x) for w, x in terms])
 
     def iota(out, pat, base, mult):
         if SCRATCH[out[0]][2] == I32:
@@ -299,277 +399,357 @@ def rank_program(g, core, T, topo):
             fn = lambda: g.iota(ap(out), pat, base, mult, allow_small_or_imprecise_dtypes=True)
         return add("pool", fn, [], [out], 0.13 + 2 * cnt(out) * CY)
 
-    def load(q, sem, out, hbm, lat):
-        return add(q, lambda: Q[q].dma_start(ap(out), hbm), [], [out], 0.1, lat, (sem, 16))
-
-    def store(q, sem, hbm, a, lat):
-        return add(q, lambda: Q[q].dma_start(hbm, ap(a)), [a], [], 0.1, lat, (sem, 16))
+    def dmas(sem, moves, lat, more=0):
+        totals[sem] = totals.get(sem, 0) + 16 * len(moves)
+        mark = (sem, totals[sem] + 16 * more)
+        made = []
+        for q, o, a in moves:
+            def fn(q=q, o=o, a=a):
+                return Q[q].dma_start(ap(o) if isinstance(o, tuple) else o, ap(a) if isinstance(a, tuple) else a)
+            made.append(add(q, fn, cols(a), cols(o), 0.1, lat, mark, tag=sem))
+        batches.setdefault(mark, []).extend(made)
 
     def send(sem, land, a):
         i = add("pool", lambda: g.remote_dma(ap(land), ap(a), T.sem[sem], T.sem.sent, pid, rid, mask_out),
                 [a], [], 1.0, 0.0, ("sent", 0))
         return add("net", None, [], [land], 0.0, 3.5, (sem, n_in), after=[i])
 
-    def sel(name, m):
-        return v(name, 15 - m, 143 - m)
+    HALF = ((0, 64), (64, 128))
+    LANES = (0, N)
 
-    load("sp", "l_ch", v("C", 0, V), T.ch[:], 6.0)
-    load("act", "l_sb", v("sbi"), T.sb[:], 2.0)
-    load("act", "l_ia", v("iai"), T.ia[:], 2.0)
-    load("act", "l_ic", v("ici"), T.ic[:], 2.0)
-    load("act", "l_x", v("X", 0, V), T.x[:], 6.5)
-    load("sp", "l_th", v("thi"), T.th[:], 2.0)
-    load("sp", "l_y", v("y0"), T.y[:], 2.0)
-    cp(v("bu"), v("sbi")); cp(v("au"), v("iai")); cp(v("cu"), v("ici"))
-    send("r_c", v("cin"), v("bu"))
-    cp(v("aL"), v("iai")); cp(v("bL0"), v("sbi"))
-    ts(v("nb"), v("thi"), -1.0, A.mult, -0.5, A.add)
-    ts(v("nh"), v("thi"), -1.0, A.mult, -96.5, A.add)
-    ts(v("pb"), v("thi"), 0.5, A.add)
-    for ci, (l0, l1) in enumerate(CHUNKS):
-        fill(v("thL", l0 // 16, l1 // 16), 2049.0 + 16.0 * (QUICK[ci] & 1))
+    for s in range(2):
+        rows = slice(64 * s, 64 * s + 64)
+        q2 = "sp" if s else "act"
+        dmas("l_c%d" % s, [("sp", v("C%d" % s, 0, V, p=h), T.ch[rows, :]) for h in HALF], 6.0 + 5.0 * s)
+        dmas("l_n%d" % s, [(q2, v("nm%d" % s, 6 * j, 6 * j + 6, p=h), z[rows, 6 * r:6 * r + 6])
+                           for j, z in enumerate((T.ia, T.ic, T.sb)) for r, h in enumerate(HALF)]
+             + [(q2, v("thi%d" % s, p=h), T.th[rows, :]) for h in HALF], 2.0)
+        dmas("l_x%d" % s, [(q2, v("X%d" % s, XO, XO + V, p=h), T.x[rows, :]) for h in HALF], 6.5 + 5.0 * s)
+        dmas("l_y%d" % s, [("sp", v("ya%d" % s, p=h), T.y[rows, N * r:N * r + N]) for r, h in enumerate(HALF)], 3.0)
 
-    iota(v("pid"), [[0, 1]], 0, 1)
+    PF, RF, P64, H16, H15, G16, PM, KC, SP0, SP1, LO = [v("pc", j, j + 1) for j in range(11)]
+    iota(v("pi", 0, 1), [[0, 1]], 0, 1)
     iota(v("xr"), [[1, 144]], 0, 0)
-    iota(v("li", 0, 12), [[16, 12]], 15, 0)
-    off = 12
-    bc = []
-    for (l0, l1) in CHUNKS:
-        nc = (l1 - l0) // 16
-        iota(v("li", off, off + nc), [[1, nc]], (3 if bc else 2) * nc, 0)
-        bc.append(v("lu", off, off + nc)); off += nc
-    cp(v("lu", 0, off), v("li", 0, off))
-    iota(v("rp"), [[0, NM // 16], [1, 16]], 0, 0)
-    iota(v("blk"), [[16, 8], [0, 16]], 0, 0)
-    iota(v("ji"), [[16, NM]], -2048, 0)
-    iota(v("lan"), [[1, L]], -L, 0)
-    iota(v("lf"), [[16, 12]], 0, 0)
-    ts(v("ri"), v("pid"), 15, A.bitwise_and)
-    cp(v("rf"), v("ri")); cp(v("pf"), v("pid"))
-    tt(v("g16"), v("pf"), v("rf"), A.subtract)
-    ts(v("g15"), v("g16"), 15.0, A.add)
-    ts(v("I"), v("xr", 0, 128), v("pf"), A.is_equal)
-    for nm, c in (("NI", -1.0), ("I2", 2.0), ("IP", 2048.0), ("IN", -2048.0), ("I16", 1.0),
-                  ("I32", 1.0), ("NI32", -1.0), ("NI2", -2.0)):
-        ts(v(nm), v("I"), c, A.mult)
-    ts(v("E1"), v("xr"), v("g15"), A.is_equal)
-    for nm, c in (("En", -2.0 ** -9), ("E2", 2.0 ** -8), ("E16", 1.0)):
-        ts(v(nm), v("E1"), c, A.mult)
-    ts(v("BO"), v("blk"), v("g16"), A.is_equal)
-    ts(v("MZ", 0, NM), v("rp"), v("rf"), A.is_ge, 8192.0, A.mult)
-    fill(v("MZ", NM, 2 * NM), 0.0)
-    ts(v("kc"), v("rf"), -64.0 * 2.0 ** -19, A.mult, -49.0 * 2.0 ** -19, A.add)
-    ts(v("kk"), v("rp"), 0.0, A.mult, v("kc"), A.add)
-    ts(v("rst"), v("rp"), 0.0, A.is_equal, -8.0, A.mult)
-    ts(v("dc"), v("rf"), float(XW - 1), A.add)
-    ts(v("d1"), v("rp"), 15.0, A.is_equal, v("dc"), A.mult)
-    ts(v("d0"), v("rp"), 0.0, A.not_equal)
-    tt(v("d0"), v("d0"), v("d1"), A.add)
-    ts(v("jc"), v("ji"), v("rf"), A.add)
-    ts(v("laneL"), v("lf"), v("rf"), A.add)
-    fill(v("n128"), -128.0)
+    iota(v("gq"), [[0, 2], [16, 8]], 0, 0)
+    iota(v("li", 0, 8), [[16, 8]], 15, 0)
+    iota(v("li", 8, 14), [[1, 6]], 0, 0)
+    iota(v("rq"), [[-16, 6], [1, N]], 0, 0)
+    iota(v("sp"), [[0, 2], [16, 6]], -(2048 + XO + 2 * 8192), 0)
+    iota(v("rp"), [[0, 9], [1, 16]], 0, 0)
+    iota(v("w1"), [[16, 8], [0, 16]], 0, 0)
+    iota(v("w2"), [[0, 2], [1, 64]], 0, 0)
+    iota(v("w3"), [[0, 2], [16, 4], [0, 16]], 0, 0)
+    iota(v("nb"), [[LV * L, TV], [L, 2], [N, 2]], V + L - 2048, 1)
+    iota(v("lf"), [[LV * L, TV], [16, 6]], V, 0)
+    cp(v("lu", 0, 14), v("li", 0, 14))
+    LAST, REP = v("lu", 0, 8), v("lu", 8, 14)
+    ts(v("pi", 1, 2), v("pi", 0, 1), 15, A.bitwise_and)
+    ts(v("pi", 2, 3), v("pi", 0, 1), 63, A.bitwise_and)
+    cp(v("pc", 0, 3), v("pi", 0, 3))
+    tt(H16, PF, RF, A.subtract)
+    ts(H15, H16, 15.0, A.add)
+    tt(G16, P64, RF, A.subtract)
+    ts(PM, PF, -64.0, A.add)
+    ts(KC, RF, -2.0 ** -13, A.mult)
+    ts(SP0, RF, 0.0, A.is_equal)
+    ts(LO, PF, 64.0, A.is_ge, float(N), A.mult)
+    ts(v("lf"), v("lf"), RF, A.add, LO, A.add)
 
-    first = {0: (v("au"), v("cu"), v("bu")),
-             1: (v("acin", 0, 12), v("cin"), v("snd0", 12, 24)),
-             2: (v("ain"), v("acin", 12, 24), v("snd1", 12, 24))}
-    for t in range(TV):
+    def scaled(name, first, scales):
+        out = []
+        for j, c in enumerate(scales):
+            out.append(v(name, 128 * j, 128 * j + 128))
+            if c is None:
+                continue
+            if first[0] is None:
+                ts(out[-1], first[1], c, A.mult)
+            else:
+                ts(out[-1], first[0], first[1], A.is_equal, c, A.mult)
+        return out
+
+    Ib, = scaled("IB", (v("xr", 0, 128), PF), (1.0,))
+    _, NIb, IKb, I2Kb, N2Kb = scaled("IB", (None, Ib), (None, -1.0, 1024.0, 2048.0, -2048.0))
+    Ih, NIh, Hh = scaled("IH", (None, Ib), (1.0, -1.0, 0.5))
+    ts(v("KD", 256, 384), Ib, 0.25, A.mult)
+    ts(v("GB", 0, 16), v("gq"), H16, A.is_equal)
+    ts(v("GB", 16, 24), v("GB", 0, 8), -2.0 ** -9, A.mult)
+    ts(v("GH"), v("GB", 0, 8), 2.0 ** -8, A.mult)
+    ts(v("E16"), v("xr"), H15, A.is_equal)
+    SPb = [v("SB", 0, 128), v("SB", 128, 256)]
+    SPh = [v("SH", 0, 128), v("SH", 128, 256)]
+    SP8 = [v("SH", 256, 384), v("SH", 384, 512)]
+    BOh, BO64, BO2 = v("SH", 512, 640), v("SB", 256, 384), v("SB", 384, 512)
+    for r, c in enumerate((PF, PM)):
+        ts(SPb[r], v("w2"), c, A.is_equal)
+        cp(SPh[r], SPb[r])
+        ts(SP8[r], SPb[r], -8192.0, A.mult)
+    ts(BOh, v("w1"), H16, A.is_equal)
+    ts(BO64, BOh, -2.0 ** -7, A.mult)
+    ts(BO2, v("w3"), G16, A.is_equal)
+    fill(v("one"), 1.0)
+    ts(v("d0"), v("rq"), RF, A.is_equal, 2.0, A.mult)
+    fill(v("d0", 0, 6 * N, N), -8.0)
+    ts(v("d0", 1, 2), v("d0", 1, 2), SP0, A.add)
+    ts(v("sp"), v("sp"), RF, A.add)
+    ts(v("KD", 0, 128), Ib, KC, A.mult)
+    ts(v("KD", 128, 256), Ib, -49.0 * 2.0 ** -19, A.mult)
+    ts(v("rst"), v("rp", 0, 128), 0.0, A.is_equal, -8.0, A.mult)
+    ts(v("dm"), v("rp", 0, N), RF, A.is_equal)
+    fill(v("n128"), -128.0)
+    for j in range(12):
+        ts(v("DG", N * j, N * j + N), v("IB", 0, N), v("nb", j, j + 1), A.mult)
+    ts(v("DG", 12 * N, 13 * N), v("IB", 0, N), -8.0, A.mult)
+
+    def top(w, n=N):
+        return (w[0], w[1], w[1] + n, 1, 0, N)
+
+    for s in range(2):
+        def u(name, a=0, b=None, st=1, p=(0, 128)):
+            return v(name + str(s), a, b, st, p)
+        cp(u("L0"), u("nm"))
+        cp(v("bu", 6 * s, 6 * s + 6), u("nm", 12, 18))
+        cp(u("nf", 0, 6), u("nm", 0, 6))
+        cp(u("nf", 6, 12), u("nm", 12, 18))
+        ts(u("nt", 0, 1), u("thi"), -1.0, A.mult, -0.5, A.add)
+        ts(u("TD"), Ib, u("nt", 0, 1), A.mult, 1.0, A.mult)
+        for j in range(2):
+            fill(u("kf", 4 * N * j + 3 * N, 4 * N * j + 4 * N), 1.0)
+        fill(u("eq"), 0.0)
+        fill(u("FT"), 0.0)
+        fill(u("key"), 0.0)
+    send("r_c", v("cin"), v("bu"))
+
+    piece = [0]
+
+    def level(s, t, lev):
+        def u(name, a=0, b=None, st=1, p=(0, 128)):
+            return v(name + str(s), a, b, st, p)
+
+        def lanes(name, a=0, b=None, st=1):
+            return u(name, a, b, st, LANES)
+
+        rows = slice(64 * s, 64 * s + 64)
         lim = V + t * LV * L
-        Xw, Cw = v("X", 0, lim), v("C", 0, lim)
-        yv = "y%d" % t
-        ts(v("nlv"), v("laneL"), float(lim), A.add)
-        if t > 0:
-            cp(v("aL"), first[t][0])
-        for lev in range(LV):
-            step = t * LV + lev
-            ku, kf, Lu, Lp = "ku%d" % (step % 2), "kf%d" % (step % 2), "Lu%d" % (step % 2), "Lu%d" % ((step + 1) % 2)
-            nbase = lim + lev * L
-            for (l0, l1) in CHUNKS:
-                n, nc = l1 - l0, (l1 - l0) // 16
-                if lev == 0:
-                    for q in (2, 1, 0):
-                        w = first[t][q]
-                        lst = v(w[0], w[1] + l0 // 16, w[1] + l1 // 16)
-                        o = 3 * l0 + q * n
-                        cp(v(ku, o, o + n), (Cw, lst))
-                        ts(v(kf, o, o + n), v(ku, o, o + n), -2048.0, A.add)
-                        act(v("PV", o, o + n), (Xw, lst), AF.Copy)
+        step = t * LV + lev
+        nbase = lim + lev * L
+        last = lev == LV - 1
+        where[:] = [KINDS[lev], 2 * step + s, {}]
+        Xw, Cw = u("X", XO, XO + lim), u("C", 0, lim - (LV - 1 - lev) * L if t else lim)
+        yv = u(("ya", "yb", "yc")[t])
+        ko, fo, lo, lp = 3 * N * (step % 2), 4 * N * (step % 2), 18 * (step % 2), 18 * ((step + 1) % 2)
+        aL, mx, tl, tl2, an, nl = [u("nf", 6 * j, 6 * j + 6) for j in (0, 5, 6, 7, 8, 9)]
+        bL = [u("nf", 6 + 6 * j, 12 + 6 * j) for j in range(4)]
+        if lev == 0 and t > 0:
+            a_in = u("acin", 0, 6) if t == 1 else u("ain", 0, 6)
+            c_in = v("cin", 6 * s, 6 * s + 6) if t == 1 else u("acin", 6, 12)
+            lists = [(2, 3, u("snd", 12 * t - 6, 12 * t)), (1, 2, c_in), (0, 1, a_in)]
+            cp(aL, a_in)
+        else:
+            lists = [(0, 3, u("Lu", lp, lp + 18) if lev else u("L0"))]
+        for q0, q1, lst in lists:
+            cp(u("ku", ko + q0 * N, ko + q1 * N), (Cw, lst))
+            act(u("PV", q0 * N, q1 * N), (Xw, lst), AF.Copy)
+        ts(u("kf", fo, fo + 3 * N), u("ku", ko, ko + 3 * N), -2048.0, A.add)
+        mms([(lanes("KB", 0, 128), v("one"), u("TD"))], stop=False)
+        if AFT:
+            mms([(lanes("KA", 0, 128), v("one"), u("TD"))], stop=False)
+        mms([(lanes("M", 384, 512), v("one"), v("KD", 0, 128))], stop=False)
+        todo = {k: list(w) for k, w in SUMS.items()}
+        place = {"AH": ("KB", 0, 128, v("GB", 0, 8)), "AF": ("KA", 0, 128, v("GB", 0, 8)), "E": ("M", 384, 512, v("GB", 16, 24)), "U": ("M", 384, 512, v("GH"))}
+
+        def sums(name, done):
+            while todo[name] and todo[name][0][1] <= done:
+                m0, m1 = todo[name].pop(0)
+                if name == "AF" and not AFT:
+                    mm(u("KA", m0, m1), [(v("EB", 15 - k, 143 - k), u("AF", 16 * m0 + k, 16 * m1, 16)) for k in range(16)])
                 else:
-                    lst = v(Lp, l0 // 4 + nc, l0 // 4 + 4 * nc)
-                    cp(v(ku, 3 * l0, 3 * l1), (Cw, lst))
-                    ts(v(kf, 3 * l0, 3 * l1), v(ku, 3 * l0, 3 * l1), -2048.0, A.add)
-                    act(v("PV", 3 * l0, 3 * l1), (Xw, lst), AF.Copy)
-                o = 3 * l0
-                mm(v(NVB, 192 + l0, 192 + l1), [(v("I"), v("PV", o, o + n)), (v("NI"), v("PV", o + n, o + 2 * n)),
-                                                 (v("I"), v("PV", o + 2 * n, o + 3 * n))])
-            newx = v("X", nbase, nbase + L) if t < 2 else v("XN", lev * L, lev * L + L)
-            act(v("nv"), v(NVB, 192, 384), AF.Relu, bias=63.0, scale=-1.0)
-            act(newx, v("nv"), AF.Relu, bias=63.0, scale=-1.0)
-            piece = 0
-            for ci, (l0, l1, pieces, subs) in enumerate(PLAN):
-                n, nc = l1 - l0, (l1 - l0) // 16
-                p0 = l0
-                for pw in pieces:
-                    w = abs(pw)
-                    c0, c1 = 16 * p0, 16 * (p0 + w)
-                    kid = [v(ku, 3 * l0 + q * n + p0 - l0, 3 * l0 + q * n + p0 - l0 + w) for q in range(3)]
-                    p0 += w
-                    Bt, E, Fd = v("Bt", c0, c1), v("E", c0, c1), v("Fd", c0, c1)
-                    if ci == 0 and p0 - l0 <= LEAD[0]:
-                        cp(Bt, (Xw, kid[2]))
-                    else:
-                        act(Bt, (Xw, kid[2]), AF.Copy)
-                    if pw > 0:
-                        tt(Fd, (Xw, kid[1]), Bt, A.subtract)
-                        act(v("AF", c0, c1), Fd, AF.Abs)
-                        terms = [(v("NI"), Fd)]
-                    else:
-                        Ct = v("Ct", c0, c1)
-                        act(Ct, (Xw, kid[1]), AF.Copy)
-                        H = v("H%d" % (piece % 2), 0, 16 * w); piece += 1
-                        mm(H, [(v("I"), Ct), (v("NI"), Bt)])
-                        act(v("AF", c0, c1), H, AF.Abs)
-                        terms = [(v("I"), Bt), (v("NI"), Ct)]
-                    tt(E, (Xw, kid[0]), Bt, A.subtract)
-                    for h0 in range(c0, c1, 512):
-                        h1 = min(c1, h0 + 512)
-                        H = v("H%d" % (piece % 2), 0, h1 - h0); piece += 1
-                        mm(H, [(m, v(x[0], h0, h1)) for m, x in terms + [(v("I"), E)]])
-                        act(v("AH", h0, h1), H, AF.Abs)
-                    ts(v("U", c0, c1), E, 1.0 / 32, A.add, 31.0 / 1024, A.max)
-                SB = "SA" if ci % 2 == 0 else "SB"
-                s0 = 0
-                for w in subs:
-                    c0, c1 = 16 * (l0 + s0), 16 * (l0 + s0 + w)
-                    mm(v(SB, s0, s0 + w), [(sel("E1", k), v("AF", c0 + k, c1, 16)) for k in range(16)])
-                    mm(v(SB, 2 * n + s0, 2 * n + s0 + w), [(v("I16"), v("kk", 0, w))]
-                       + [(sel("En", k), v("E", c0 + k, c1, 16)) for k in range(16)]
-                       + [(sel("E2", k), v("U", c0 + k, c1, 16)) for k in range(16)])
-                    mm(v(SB, n + s0, n + s0 + w), [(sel("E1", k), v("AH", c0 + k, c1, 16)) for k in range(16)])
-                    s0 += w
-                c0, c1 = 16 * l0, 16 * l1
-                so, po, lo, fo = 2 * l0, 5 * l0, l0 // 4, 64 * ci
-                quick = QUICK[ci]
-                if quick & 1:
-                    ts(v("S", so, so + 2 * n), v(SB, 0, 2 * n), v("pb"), A.is_gt, 2.0, A.mult)
-                else:
-                    act(v("S", so, so + 2 * n), v(SB, 0, 2 * n), AF.Sign, bias=v("nb"))
-                col = v("PR", po + 4 * n, po + 5 * n)
-                tt(col, v("S", so, so + n), v("S", so + n, so + 2 * n), A.min)
-                tt(v("key", l0, l1), v(SB, 2 * n, 3 * n), col, A.add)
-                tr(v("keyT", l0, l1), v("key", l0, l1))
-                scan(v("FT", l0, l1), v("rst", 0, n), v("keyT", l0, l1), 0.0, A.add, A.max)
-                tt(v("ohT", l0, l1), (v("FT", l0, l1), v("lu", 0, nc)), v("keyT", l0, l1), A.is_equal)
-                oh = v("OH", l0, l1)
-                tr(oh, v("ohT", l0, l1))
-                for q in ((2, 0, 1) if lev < LV - 1 else (2,)):
-                    tt(v("PR", po + (q + 1) * n, po + (q + 2) * n), oh, v(kf, 3 * l0 + q * n, 3 * l0 + (q + 1) * n), A.mult)
-                j0 = 1 if ci == 0 else 0
-                if j0 == 0:
-                    tt(v("PR", po, po + n), oh, v("jc", 0, n), A.mult)
-                mm(v("LS", j0 * nc, 5 * nc), [(sel("E16", r), v("PR", po + j0 * n + r, po + 5 * n, 16)) for r in range(16)])
-                zold = (Xw, v(Lu, lo + 3 * nc, lo + 4 * nc)) if j0 else (v("Bt", c0, c1), v(Lu, lo, lo + nc))
-                fj, lj = fo + j0 * nc, lo + j0 * nc
-                mm(v(ZB, 192, 192 + 2 * n), [(v("BO"), v("PR", po + 3 * n, po + 5 * n)), (v("I"), v("MZ", NM - n, NM + n))])
-                if quick & 2:
-                    ts(v("Lf", fj, fo + 5 * nc), v("LS", j0 * nc, 5 * nc), 2048.0, A.add)
-                    ts(v(Lu, lj, lo + 4 * nc), v("LS", j0 * nc, 4 * nc), 2048.0, A.add)
-                else:
-                    act(v("Lf", fj, fo + 5 * nc), v("LS", j0 * nc, 5 * nc), AF.Identity, bias=2048.0)
-                    cp(v(Lu, lj, lo + 4 * nc), v("Lf", fj, fo + 4 * nc))
-                act(v("ZR", l0, l1), v(ZB, 192, 192 + n), AF.Identity, bias=2048.0)
-                act(v("RC", lev * L + l0, lev * L + l1), v(ZB, 192 + n, 192 + 2 * n), AF.Relu, bias=-1.0 - 16.0 * (quick & 1))
-                if lev < LV - 1:
-                    act(v("ohB", l0, l1), oh, AF.Copy, scale=float(nbase + 2 * L))
-                mx = v("mxL", l0 // 16, l1 // 16)
-                if lev == 0:
-                    cp(mx, v("Lf", fo + 4 * nc, fo + 5 * nc))
-                else:
-                    tt(mx, mx, v("Lf", fo + 4 * nc, fo + 5 * nc), A.max)
-                tt(v("eq", l0, l1), (v("Lf", fj, fo + 5 * nc), bc[ci]), v("ZR", l0, l1), A.is_equal)
-                scan(v("sc", l0, l1), v("d0", 0, n), v("eq", l0, l1), 0.0, A.mult, A.max)
-                tg = v("tg", l0 // 16, l1 // 16)
-                tt(tg, v("sc", l0 + 15, l1, 16), v("Lf", fo + 3 * nc, fo + 4 * nc), A.max)
-                cp(v("Tu", l0 // 8, l1 // 8, 2), tg)
-                if quick & 4:
-                    tt(v("sm", l0, l1), zold, v(yv, l0, l1), A.add)
-                    ts(v("hb", l0, l1), v("sm", l0, l1), 0.5, A.mult, 127.75, A.add)
-                else:
-                    act(v("sm", l0, l1), zold, AF.Copy)
-                    mm(v("LS", 384, 384 + n), [(v("I"), v(yv, l0, l1)), (v("I"), v("sm", l0, l1))])
-                    act(v("hb", l0, l1), v("LS", 384, 384 + n), AF.Identity, bias=127.75, scale=0.5)
-            if lev == LV - 1:
-                tt(v("tl"), v("mxL"), v("thL"), A.is_le)
-                tt(v("tl2"), v("tl"), v("nlv"), A.mult)
-                bn = v("bL%d" % (t + 1))
-                if t < TV - 1:
-                    snd = "snd%d" % t
-                    tt(v("an"), v("tl2"), v("aL"), A.max)
-                    cp(v(snd, 0, 12), v("an"))
-                tt(bn, v("tl2"), v("bL%d" % t), A.max)
-                if t == 0:
-                    cp(v(snd, 12, 24), bn)
-                    send("r_a0", v("acin"), v(snd))
-                elif t == 1:
-                    send("r_a1", v("ain"), v(snd, 0, 12))
-                    cp(v(snd, 12, 24), bn)
-                else:
-                    store("sp", "s_so", T.so[:], bn, 2.0)
-            for c in range(L // 16 - 1, -1, -1):
-                tt((v("X"), v("Tu", 2 * c, 2 * c + 1)), v("hb", 16 * c, 16 * c + 16), v("n128"), A.add)
-            for ci, (l0, l1) in enumerate(CHUNKS):
-                n, so = l1 - l0, 2 * l0
-                key, r1, r2, sg = v("key", l0, l1), v("r1", l0, l1), v("r2", l0, l1), v("sg", l0, l1)
-                act(r1, key, AF.Identity, bias=MAGIC, scale=8192.0)
-                if WIDE[0]:
-                    act(v("k2", l0, l1), key, AF.Identity, bias=0.5, scale=8192.0)
-                    act(r2, v("k2", l0, l1), AF.Identity, bias=MAGIC)
-                    vote = [(v("I32"), r2), (v("NI32"), r1)]
-                else:
-                    act(r2, r1, AF.Identity, bias=-MAGIC / 8192, scale=1.0 / 8192)
-                    tt(v("vt", l0, l1), key, r2, A.is_gt)
-                    vote = [(v("I"), v("vt", l0, l1))]
-                mm(v("MX", l0, l1), vote + [(v("I2"), v("S", so + n, so + 2 * n)), (v("NI"), v("S", so, so + n))])
-                act(sg, v("MX", l0, l1), AF.Sign, bias=-1.5 - (QUICK[ci] & 1))
-                out = [(v("NI2"), v("ohB", l0, l1))] if WIDE[1] and lev < LV - 1 else []
-                X1, X2, X3 = v("MY", so, so + n), v("MY", so + n, so + 2 * n), v("MX", L + l0, L + l1)
-                mm(X1, [(v("I16"), v(kf, 3 * l0 + 2 * n, 3 * l1)), (v("IN"), sg)] + out)
-                mm(X2, [(v("I16"), v(kf, 3 * l0, 3 * l0 + n)), (v("IP"), sg)] + out)
-                if lev < LV - 1:
-                    mm(X3, [(v("I"), v("lan", l0, l1)), (v("I"), v("ohB", l0, l1))])
-                mo, x1 = v("Cf", step * L + l0, step * L + l1), v("x1", l0, l1)
-                if WIDE[1]:
-                    act(v("x12", so, so + 2 * n), v("MY", so, so + 2 * n), AF.Relu)
-                    parts = [v("x12", so, so + n), v("x12", so + n, so + 2 * n)]
-                    if lev < LV - 1:
-                        act(x1, X3, AF.Relu)
-                        parts.append(x1)
-                    mm(v("MX", l0, l1), [(v("I32"), p) for p in parts])
-                    act(mo, v("MX", l0, l1), AF.Copy)
-                else:
-                    act(x1, X1, AF.Copy)
-                    if lev < LV - 1:
-                        tt(v("m1", l0, l1), X2, x1, A.max)
-                        tt(mo, X3, v("m1", l0, l1), A.max)
-                    else:
-                        tt(mo, X2, x1, A.max)
+                    bank, a, b, w = place[name]
+                    mms([(u(bank, a + k, b, 16, (m0, m1)), u(name, 16 * m0 + k, 16 * m1, 16), w) for k in range(16)],
+                        stop=False, into=True)
+
+        made = {k: set() for k in ("B", "F", "E", "U", "AH")}
+        on_scalar = set()
+
+        def upto(name):
+            n = 0
+            while n in made[name]:
+                n += 1
+            return n
+
+        def bank(n):
+            piece[0] += 1
+            return v("H%d" % (piece[0] % 2), 0, n)
+
+        walk = WALK0 if WALK0 and lev == 0 and t > 0 else WALK
+        for kind, a, b in walk:
+            c0, c1 = 16 * a, 16 * b
+            q = {"B": 2, "b": 2, "F": 1, "C": 1, "E": 0}[kind]
+            kid = (Xw, u("ku", ko + q * N + a, ko + q * N + b))
+            Bt, E, Fd, Ct = [u(k, c0, c1) for k in ("Bt", "E", "Fd", "Ct")]
+            BULK[0] = True
+            if kind == "B":
+                i0 = act(Bt, kid, AF.Copy)
+            elif kind == "b":
+                i0 = cp(Bt, kid)
+            elif kind == "C":
+                act(Ct, kid, AF.Copy)
+            else:
+                tt(Fd if kind == "F" else E, kid, Bt, A.subtract)
+            BULK[0] = False
+            if (kind, a, b) == walk[0]:
+                ops[i0]["gate"] = 2 * step + s
+            made[{"b": "B", "C": "F"}.get(kind, kind)].update(range(a, b))
+            if kind == "F":
+                act(u("AF", c0, c1), Fd, AF.Abs)
+            elif kind == "C":
+                on_scalar.update(range(a, b))
+                H = bank(c1 - c0)
+                mm(H, [(Ib, Ct), (NIb, Bt)])
+                act(u("AF", c0, c1), H, AF.Abs)
+            elif kind == "E":
+                for h0, h1 in UCUT:
+                    if h0 not in made["U"] and h1 <= upto("E"):
+                        made["U"].update(range(h0, h1))
+                        ts(u("U", 16 * h0, 16 * h1), u("E", 16 * h0, 16 * h1), 1.0 / 32, A.add, 31.0 / 1024, A.max)
+                sums("E", upto("E"))
+                sums("U", upto("U"))
+            if kind in "FC":
+                sums("AF", upto("F"))
+                if upto("F") == N and AFT:
+                    mms([(lanes("KA", 0, 128), v("one"), v("KD", 256, 384))], into="close")
+                    act(lanes("S", 0, 128), lanes("KA", 0, 128), AF.Sign)
+                elif upto("F") == N:
+                    act(u("S", 0, N), u("KA", 0, N), AF.Sign, bias=u("nt", min(t, 1), min(t, 1) + 1))
+            for h0, h1 in HCUT:
+                if h0 not in made["AH"] and set(range(h0, h1)) <= made["E"] & made["F"]:
+                    made["AH"].update(range(h0, h1))
+                    H = bank(16 * (h1 - h0))
+                    w = {k: u(k, 16 * h0, 16 * h1) for k in ("Bt", "Ct", "Fd", "E", "AH")}
+                    mm(H, ([(Ib, w["Bt"]), (NIb, w["Ct"])] if h0 in on_scalar else [(NIb, w["Fd"])]) + [(Ib, w["E"])])
+                    act(w["AH"], H, AF.Abs)
+                    sums("AH", upto("AH"))
+        col, only, x = lanes("S", 128, 256), lanes("S", 256, 384), lanes("M", 384, 512)
+        mms([(lanes("KB", 0, 128), top(IKb), lanes("S", 0, 128)) if AFT else (lanes("KB", 0, 128), u("S", 0, N), IKb)],
+            into="close")
+        if COL_ON_VECTOR:
+            ts(col, lanes("KB", 0, 128), 1024.0, A.is_gt, 2.0, A.mult)
+        else:
+            act(col, lanes("KB", 0, 128), AF.Sign, bias=-1024.0)
+        mms([(x, v("one"), v("KD", 128, 256))], into="close")
+        mm(u("KA", 128 + 3 * N, 512), [(col, top(Ib))])
+        if ROUND_ON_SCALAR:
+            act(lanes("rr"), x, AF.Identity, bias=MAGIC)
+            act(lanes("rr"), lanes("rr"), AF.Identity, bias=-MAGIC)
+        else:
+            ts(lanes("rr"), x, MAGIC, A.add, MAGIC, A.subtract)
+        tt(lanes("sel"), x, lanes("rr"), A.is_gt)
+        tt(lanes("key"), x, col, A.add)
+        scan(lanes("FT"), part(v("rst"), LANES), lanes("key"), 0.0, A.add, A.max)
+        tt(u("oh"), (u("FT"), LAST), u("key"), A.is_equal)
+
+        def hot(out, j, h=(0, 128)):
+            return [(out, lanes("oh", h[0], h[1]), v("DG", N * j, N * j + N, p=LANES))]
+
+        q0 = 2 if last else 0
+        mms([(u("KA", 128 + q * N, 128 + q * N + N), lanes("oh"), top(Ih)) for q in range(q0, 3)], each=1)
+        tt(u("PR", q0 * N, 4 * N), u("KA", 128 + q0 * N, 512), u("kf", fo + q0 * N, fo + 4 * N), A.mult)
+        mm(u("M", 6 * q0, 24), [(v("E16", 15 - r, 143 - r), u("PR", q0 * N + r, 4 * N, 16)) for r in range(16)])
+        mm(u("M", 24, 24 + N), [(BOh, u("PR", 2 * N, 3 * N))])
+        ts(u("Lu", lo + 6 * q0, lo + 18), u("M", 6 * q0, 18), 2048.0, A.add)
+        for c in range(5, -1, -1):
+            ts(u("eq", N * c, N * c + 16 * c + 16), u("M", 24, 24 + 16 * c + 16), u("M", 12 + c, 13 + c), A.is_equal)
+        zl = u("zl", 12 * lev, 12 * lev + 6)
+        cp(u("zl", 12 * lev, 12 * lev + 12), u("M", 12, 24))
+        if lev == 1:
+            tt(mx, u("zl", 6, 12), u("zl", 18, 24), A.max)
+        if last:
+            ab = u("ab", 0, 6)
+            tt(tl, u("M", 18, 24), mx, A.max)
+            ts(ab, tl, 1.0 + 16 * COL_ON_VECTOR, A.is_gt, -8192.0, A.mult)
+            tt(tl2, v("lf", 6 * t, 6 * t + 6), ab, A.add)
             if t < TV - 1:
-                cp(v("C", nbase, nbase + L), v("Cf", step * L, step * L + L))
-        store("sp", "s_c%d" % t, T.co[:, t * 576:(t + 1) * 576], v("Cf", t * 576, (t + 1) * 576), 3.0)
-        mm(v("MX", 2 * L - L, 2 * L), [(v("IP"), v("RC", k * L, k * L + L)) for k in range(LV)])
-        x0 = v("X", lim, lim + L) if t < 2 else v("XN", 0, L)
+                tt(an, tl2, aL, A.max)
+                cp(u("snd", 12 * t, 12 * t + 6), an)
+            tt(bL[t + 1], tl2, bL[t], A.max)
+            if t == 0:
+                cp(u("snd", 6, 12), bL[1])
+                send("r_a0%d" % s, u("acin"), u("snd", 0, 12))
+            elif t == 1:
+                send("r_a1%d" % s, u("ain", 0, 6), u("snd", 12, 18))
+                cp(u("snd", 18, 24), bL[2])
+            else:
+                dmas("out", [("sp", T.so[rows, 6 * r:6 * r + 6], part(bL[3], h)) for r, h in enumerate(HALF)], 2.0)
+        scan(u("sc"), v("d0"), u("eq"), 0.0, A.add, A.max)
+        mms([(u("M", 168 + 6 * r, 174 + 6 * r), w, a) for r in range(2)
+             for w, a in ((SPh[r], zl), (SP8[r], u("sc", N - 1, 6 * N, N)))], each=2)
+        tt(u("tg"), u("M", 168, 180), v("sp"), A.max)
+        ts(u("Tu"), u("tg"), 2048.0 + XO + 2 * 8192.0, A.add)
+        sm = u("hb", 2 * N, 3 * N)
+        act(sm, (Xw, u("Lu", lo + 12, lo + 18)), AF.Copy)
+        for r in range(2):
+            mm(u("KA", 320 + N * r, 320 + N * r + N), [(SPb[r], yv), (SPb[r], sm)])
+        act(u("hb", 0, 2 * N), u("KA", 320, 320 + 2 * N), AF.Identity, bias=127.75, scale=0.5)
+        for r in (1, 0):
+            tt((u("X", 0, XO + lim), u("Tu", 6 * r, 6 * r + 6)), u("hb", N * r, N * r + N), v("n128"), A.add)
+        act(only, lanes("KB", 0, 128), AF.Sign, bias=1024.0)
+        MX, sg = u("KB", 256, 256 + N), u("S", 384, 384 + N)
+        mms([(MX, lanes("sel"), top(Ih)), (MX, Hh, u("PR", 3 * N, 4 * N)), (MX, only, top(Ib)),
+             (MX, lanes("S", 0, 128), top(NIb)) if AFT else (MX, NIb, u("S", 0, N))]
+            + ([] if last else hot(MX, 12)))
+        act(sg, MX, AF.Sign, bias=-1.0 - 0.5 * COL_ON_VECTOR)
+        X1, X2 = u("KA", 128, 128 + N), u("KA", 128 + N, 128 + 2 * N)
+        terms = [(X1, Ih, u("kf", fo + 2 * N, fo + 3 * N))]
+        if not last:
+            terms.append((X1, NIh, u("PR", 2 * N, 3 * N)))
+            for r, h in enumerate(HALF):
+                terms += hot(part(X1, h), 2 * (2 * t + lev) + r, h)
+        mms(terms + [(X1, N2Kb, sg)])
+        mm(X2, [(Ih, u("kf", fo, fo + N)), (I2Kb, sg)])
+        act(u("x2"), X2, AF.Copy)
+        nv = u("NV", step * N, step * N + N)
+        mm(u("KB", 384, 384 + N), [(Ib, u("PV", 0, N)), (NIb, u("PV", N, 2 * N)), (Ib, u("PV", 2 * N, 3 * N))])
+        if CLIP_ON_VECTOR:
+            ts(nv, u("KB", 384, 384 + N), 0.0, A.max, 63.0, A.min)
+        else:
+            act(u("PV", 3 * N, 4 * N), u("KB", 384, 384 + N), AF.Relu, bias=63.0, scale=-1.0)
+            act(nv, u("PV", 3 * N, 4 * N), AF.Relu, bias=63.0, scale=-1.0)
         if t < TV - 1:
-            act(v("sa"), v("MX", L, 2 * L), AF.Sign, bias=-1.0, accum=v("acc"))
-            ts(v("nb"), v("acc"), -0.5, A.mult, v("nh"), A.add)
-            ts(v("pb"), v("acc"), 0.5, A.mult, v("nh"), A.subtract)
-        tt(v("yt"), v("MX", L, 2 * L), v(yv), A.min)
-        tt(v("yd"), v("yt"), x0, A.subtract)
-        act(v("ys%d" % t), v("yd"), AF.Abs)
+            dmas("xs%d" % s, [("sp", u("X", XO + nbase + N * r, XO + nbase + N * r + N, p=h2), part(nv, h))
+                              for r, h in enumerate(HALF) for h2 in HALF], 2.5, more=4 * (LV - 1 - lev))
+        else:
+            dmas("out", [("sp", T.xo[rows, nbase + N * r:nbase + N * r + N], part(nv, h)) for r, h in enumerate(HALF)], 2.5)
+        mo = u("Cf", step * N, step * N + N)
+        tt(mo, X1, u("x2"), A.max)
+        j0 = step * L
+        dmas("out", [("sp", T.co[rows, j0 + N * r:j0 + N * r + N], part(mo, h)) for r, h in enumerate(HALF)], 2.5)
         if t < TV - 1:
-            send("r_y%d" % t, v("y%d" % (t + 1)), v("ys%d" % t))
-    store("sp", "s_xn", T.xo[:, XW:XW + 576], v("XN"), 2.5)
-    store("sp", "s_yo", T.yo[:], v("ys2"), 2.0)
-    store("sp", "s_x0", T.xo[:, 0:XW // 2], v("X", 0, XW // 2), 4.0)
-    store("act", "s_x1", T.xo[:, XW // 2:XW], v("X", XW // 2, XW), 4.0)
+            ci = u("Ci", step * N, step * N + N)
+            cp(ci, mo)
+            dmas("cs%d%d" % (lev, s), [("sp", u("C", nbase + N * r, nbase + N * r + N, p=h2), part(ci, h))
+                                       for r, h in enumerate(HALF) for h2 in HALF], 2.5)
+        if last:
+            if t < TV - 1:
+                mm(u("KB", 500, 501), [(BO2, u("ab", c, c + 1)) for c in range(6)])
+                ts(u("nt", 1, 2), u("KB", 500, 501), 2.0 ** -13, A.mult, u("nt", 0, 1), A.add)
+                ts(u("TD"), Ib, u("nt", 1, 2), A.mult)
+            ya, yb, ys = u("yt", 0, N), u("yt", N, 2 * N), u("ys", t * N, t * N + N)
+            tt(ya, (ab, REP), v("dm"), A.mult)
+            mm(u("KA", 0, N), [(BO64, ya)])
+            tt(yb, u("KA", 0, N), yv, A.min)
+            mm(u("KA", 0, N), [(Ib, yb), (NIb, u("NV", t * LV * N, t * LV * N + N))])
+            act(ys, u("KA", 0, N), AF.Abs)
+            if t < TV - 1:
+                send("r_y%d%d" % (t, s), u(("yb", "yc")[t]), ys)
+            else:
+                dmas("out", [("sp", T.yo[rows, N * r:N * r + N], part(ys, h)) for r, h in enumerate(HALF)], 2.0)
+                hw = XW // 2
+                dmas("out", [(q, T.xo[rows, hw * r:hw * r + hw], u("X", XO + hw * r, XO + hw * r + hw, p=HALF[r]))
+                             for r, q in enumerate(("sp", "act"))], 3.5)
+
+    for t in range(TV):
+        for lev in range(LV):
+            for s in range(2):
+                level(s, t, lev)
 
     order, _end = order_ops(ops)
     count = {"pe": 0, "dve": 0, "act": 0, "pool": 0}
@@ -606,5 +786,5 @@ def rank_program(g, core, T, topo):
         else:
             ins.then_inc(T.sem[o["sem"][0]], 16)
             o["mark"] = o["sem"]
-    for s, val in list(count.items()) + [("sent", sent)] + [(s, 16) for s in DMAS] + [(s, n_in) for s in ARRIVE]:
+    for s, val in list(count.items()) + [("sent", sent)] + list(totals.items()) + [(s, n_in) for s in ARRIVE]:
         g.wait_ge(T.sem[s], val)

@@ -7,12 +7,18 @@ XW = V + 2 * LV * L
 XO = 96
 WALK = (("b", 0, 16), ("F", 0, 16), ("B", 16, 48), ("E", 0, 16), ("C", 16, 48), ("B", 48, 80), ("E", 16, 48),
         ("C", 48, 80), ("B", 80, 96), ("E", 48, 80), ("F", 80, 96), ("E", 80, 96))
-UCUT = ((0, 48), (48, 96))
+UCUT = ((0, 48), (48, 80), (80, 96))
 HCUT = ((0, 16), (16, 48), (48, 80), (80, 96))
-SUMS = {"AF": ((0, 96),), "E": ((0, 96),), "U": ((0, 96),), "AH": ((0, 64), (64, 96))}
+CUT = 80
+SUMS = {k: ((0, CUT), (CUT, N)) for k in ("AF", "E", "U", "AH")}
 CLIP_ON_VECTOR = False
 SOFT = False
 AFT = True
+GRAIN = 9999
+SPLIT = False
+SUM_ON_VECTOR = False
+SEG = (0, 50, 100, 150, 248, 346)
+SETS_OF = ((0, 50), (3, 98))
 COL_ON_VECTOR = False
 ROUND_ON_SCALAR = False
 WALK0 = None
@@ -35,7 +41,7 @@ STREAM = {
     "AF": (16 * N, B16), "AH": (16 * N, B16), "Ct": (16 * N, B16),
     "ku": (6 * N, U16), "kf": (8 * N, F16), "Lu": (36, U16), "PV": (4 * N, B16),
     "S": (384 + N, B16), "key": (128, F32), "FT": (128, F32), "oh": (128, F16), "rr": (128, F32), "sel": (128, F16),
-    "PR": (4 * N, F16), "tg": (12, F32), "zl": (36, F16), "eq": (6 * N, F16), "sc": (6 * N, F16), "Tu": (12, U16),
+    "PR": (4 * N, F16), "eq": (444, F16), "sc": (444, F16), "Tu": (12, U16),
     "hb": (3 * N, B16), "x2": (N, F32),
 }
 SCRATCH = {"%s%d" % (k, s): _sb(*w) for k, w in STREAM.items() for s in range(2)}
@@ -45,25 +51,27 @@ SCRATCH.update({
     "w3": _sb(128, F32), "rp": _sb(144, F32), "li": _sb(24, I32), "lu": _sb(24, U16), "nb": _sb(12, F32),
     "lf": _sb(18, F32), "gq": _sb(16, F32),
     "IB": _sb(5 * 128, B16), "IH": _sb(3 * 128, F16), "SB": _sb(4 * 128, B16), "SH": _sb(5 * 128, F16),
-    "E16": _sb(144, F16), "GB": _sb(24, B16), "GH": _sb(8, F16), "one": _sb(N, F16), "KD": _sb(384, F16),
-    "rq": _sb(6 * N, F32), "sp": _sb(12, F32), "d0": _sb(6 * N, F16), "rst": _sb(128, F32), "dm": _sb(N, B16), "DG": _sb(14 * N, F16), "n128": _sb(N, B16),
+    "E16": _sb(144, F16), "GB": _sb(24, B16), "GH": _sb(8, F16), "one": _sb(N + 16, F16), "JB": _sb(2 * N, B16), "KD": _sb(384, F16),
+    "rq": _sb(444, F32), "sp": _sb(6, F32), "d0": _sb(444, F16), "rst": _sb(128, F32), "dm": _sb(N, B16), "DG": _sb(14 * N, F16), "n128": _sb(N, B16),
 })
 BANKS = ("H0", "H1", "KA0", "KB0", "M0", "KA1", "KB1", "M1")
 for _b in BANKS:
     SCRATCH[_b] = ("psum", [128, 512], F32)
 
-OWN = ["l_c", "l_x", "l_n", "l_y", "xs", "cs0", "cs1", "cs2"]
+OWN = ["l_c", "l_x", "l_n", "l_y", "xs", "xt", "cs0", "cs1", "cs2"]
 ARRIVE = ["r_c"] + [k + str(s) for k in ("r_a0", "r_y0", "r_a1", "r_y1") for s in range(2)]
 SEMAPHORES = ["pe", "dve", "act", "pool", "sent", "out"] + [k + str(s) for k in OWN for s in range(2)] + ARRIVE
 
-CY, PCY = np.array([0.92e-3, 1.04e-3, 0.85e-3, 1.2e-3]), np.array([0.47e-3, 0.52e-3, 0.44e-3, 0.6e-3])
-GA, SCA = np.array([1.56, 1.56, 1.2, 2.0]), np.array([3.8, 3.8, 2.5, 5.5])
-HS, HO, WEIGHT = (0.13, 0.08, 0.2, 0.15), (0.27, 0.2, 0.33, 0.3), (1.0, 1.0, 1.0, 0.75)
+CY, PCY = np.array([0.85e-3, 0.83e-3, 0.92e-3, 1.2e-3]), np.array([0.43e-3, 0.42e-3, 0.47e-3, 0.6e-3])
+GA, SCA = np.array([1.56, 1.2, 1.56, 2.0]), np.array([3.8, 2.5, 3.8, 5.5])
+OV = np.array([0.0, 0.5, 0.0, 0.5])
+HS, HO, WEIGHT = (0.15, 0.1, 0.06, 0.2), (0.27, 0.2, 0.15, 0.35), (1.0, 1.0, 1.0, 0.7)
 HOP_SAME, HOP_OTHER = HS[0], HO[0]
 LOOKS, ROUNDS, TRIES = (0.2, 0.5, 0.35), 3, 20
 BEATS = (10.0, 12.0, 9.0, 14.0, 11.0)
-POLISH = 30000
-SETS, HEAT, WIDE = (0, 3), 0.2, 0.1
+PATTERN = 0.0
+POLISH = 24000
+SETS, HEAT, WIDE, FILL, SMOOTH = (0, 1, 3), 0.25, 0.1, 0.3, 0.3
 KINDS = ("a", "b", "c")
 
 
@@ -191,12 +199,12 @@ def order_ops(ops):
                 free[q] = t = t + dm[i]
                 fin[i] = t + lat[i]
             end = max(fin)
-            i, found = fin.index(end), []
+            i, found = fin.index(end) if rng.random() < 0.5 else int(rng.integers(n // 4, n)), [(order[0], order[0])]
             while why[i] is not None:
                 if why[i] >= 0:
                     found.append((why[i], i))
                 i = why[i] if why[i] >= 0 else -1 - why[i]
-            return end, start, found
+            return end + SMOOTH * sum(start) / n, start, found
 
         def judge(order):
             res = [held(order, m) for m in SETS]
@@ -205,8 +213,22 @@ def order_ops(ops):
         col = [[d[m] for d in durs] for m in range(len(CY))]
         alike = {(o["kind"][1:], o["turn"]): i for i, o in enumerate(ops) if o["kind"][0] != "start"}
         now = top = judge(best[0])
+        if PATTERN:
+            gate = {o["gate"]: best[1][i] for i, o in enumerate(ops) if "gate" in o}
+            tried = []
+            for j in range(2, 2 * TV * LV - 2):
+                beat = (gate[j + 1] - gate[j - 1]) / 2
+                key = [best[1][i] - gate[0] if o["kind"][0] == "start" else o["turn"] * beat + best[1][
+                    alike.get((o["kind"][1:], j), i)] - gate[j if (o["kind"][1:], j) in alike else o["turn"]]
+                    for i, o in enumerate(ops)]
+                for i in range(n):
+                    for d in pred[i]:
+                        if key[d] >= key[i]:
+                            key[i] = key[d] + 1e-4
+                tried.append(judge(np.argsort(key, kind="stable").tolist()))
+            now = min(tried, key=lambda e: e[0])
         for trial in range(POLISH):
-            found = now[2][trial % len(SETS)][2]
+            found = now[2][trial // 2 % len(SETS)][2]
             j = int(rng.integers(len(found)))
             a, b = found[j]
             for _ in range(int(rng.integers(3))):
@@ -218,8 +240,14 @@ def order_ops(ops):
             key = [0.0] * n
             for p, i in enumerate(now[1]):
                 key[i] = float(p)
+            if trial % 2 and rng.random() < FILL:
+                start, dm = now[2][trial // 2 % len(SETS)][1], col[SETS[trial // 2 % len(SETS)]]
+                mine = [i for i in now[1][max(0, int(key[a]) - 150):int(key[a]) + 1] if qs[i] == qs[a]]
+                gaps = [e for d, e in zip(mine, mine[1:-1]) if start[e] > start[d] + dm[d] + 0.04]
+                if gaps:
+                    a, b = gaps[-1 - int(rng.integers(min(4, len(gaps))))], a
             moves = [(a, b)]
-            if rng.random() < WIDE:
+            if rng.random() < WIDE + (trial < PATTERN * POLISH) and "start" not in (ops[a]["kind"][0], ops[b]["kind"][0]):
                 ka, kb, gap = ops[a]["kind"][1:], ops[b]["kind"][1:], ops[b]["turn"] - ops[a]["turn"]
                 moves = [(alike[ka, u], alike[kb, u + gap]) for u in range(2 * TV * LV)
                          if (ka, u) in alike and (kb, u + gap) in alike and key[alike[ka, u]] < key[alike[kb, u + gap]]]
@@ -309,6 +337,8 @@ def rank_program(g, core, T, topo):
             run = bank_last.setdefault(b, [q, [], []])
             if run[0] != q:
                 run[0], run[2], run[1] = q, run[1], []
+            elif q == "pe" and acc is not True and run[1]:
+                soft.add(run[1][-1])
             run[1].append(i)
             deps.update(run[2])
         for lst, isw in ((r2, False), (w2, True)):
@@ -338,7 +368,7 @@ def rank_program(g, core, T, topo):
             return 0.05 + cnt(out) * SCA * CY
         if any(len(w) == 2 for w in ins):
             return 0.05 + cnt(out) * GA * CY
-        return max(64, cnt(out) * per) * CY + 0.02
+        return max(64, cnt(out) * per) * CY + 0.02 * OV
 
     def sc_(x):
         return x if isinstance(x, (int, float)) or x is None else ap(x)
@@ -372,22 +402,26 @@ def rank_program(g, core, T, topo):
         return add("dve", lambda: g.vector.memset(ap(out), c), [], [out], vdur(out, [], 0.5))
 
     def act(out, a, func, bias=0.0, scale=1.0):
-        dur = 0.065 + cnt(out) * GA * CY if len(a) == 2 else max(64, cnt(out)) * CY + 0.03
+        dur = 0.065 + cnt(out) * GA * CY if len(a) == 2 else max(64, cnt(out)) * CY + 0.03 * OV
         fn = lambda: g.scalar.activation(ap(out), ap(a), func, bias=sc_(bias), scale=scale)
         return add("act", fn, [a] + cols(bias), [out], dur)
 
     def mms(terms, stop=True, each=False, into=None):
-        i = len(ops)
-
-        def fn():
-            last = None
-            for k, (o, w, x) in enumerate(terms):
-                run = each or len(terms)
-                last = g.tensor.matmul(ap(o), ap(w), ap(x), into is None and k % run == 0, stop and k % run == run - 1)
-            return last
-        rd = list({z: 0 for t in terms for z in t[1:]})
-        wr = list({t[0]: 0 for t in terms})
-        return add("pe", fn, rd, wr, sum(max(min(64, cnt(w)), cnt(o)) for o, w, x in terms) * PCY + 0.05, acc=into)
+        run = each or len(terms)
+        parts, cycles = [[]], 0
+        for k, (o, w, x) in enumerate(terms):
+            c = max(min(64, cnt(w)), cnt(o))
+            if parts[-1] and cycles + c > GRAIN:
+                parts.append([])
+                cycles = 0
+            parts[-1].append((o, w, x, into is None and k % run == 0, stop and k % run == run - 1))
+            cycles += c
+        for j, some in enumerate(parts):
+            def fn(some=some):
+                return [g.tensor.matmul(ap(o), ap(w), ap(x), a, b) for o, w, x, a, b in some][-1]
+            add("pe", fn, list({z: 0 for t in some for z in t[1:3]}), list({t[0]: 0 for t in some}),
+                sum(max(min(64, cnt(t[1])), cnt(t[0])) for t in some) * PCY + 0.05 * OV / len(parts),
+                acc=into or (j > 0 and "close"))
 
     def mm(out, terms):
         return mms([(out, w, x) for w, x in terms])
@@ -399,14 +433,14 @@ def rank_program(g, core, T, topo):
             fn = lambda: g.iota(ap(out), pat, base, mult, allow_small_or_imprecise_dtypes=True)
         return add("pool", fn, [], [out], 0.13 + 2 * cnt(out) * CY)
 
-    def dmas(sem, moves, lat, more=0):
+    def dmas(sem, moves, lat, more=0, after=()):
         totals[sem] = totals.get(sem, 0) + 16 * len(moves)
         mark = (sem, totals[sem] + 16 * more)
         made = []
         for q, o, a in moves:
             def fn(q=q, o=o, a=a):
                 return Q[q].dma_start(ap(o) if isinstance(o, tuple) else o, ap(a) if isinstance(a, tuple) else a)
-            made.append(add(q, fn, cols(a), cols(o), 0.1, lat, mark, tag=sem))
+            made.append(add(q, fn, cols(a), cols(o), 0.1, lat, mark, after, tag=sem))
         batches.setdefault(mark, []).extend(made)
 
     def send(sem, land, a):
@@ -415,26 +449,32 @@ def rank_program(g, core, T, topo):
         return add("net", None, [], [land], 0.0, 3.5, (sem, n_in), after=[i])
 
     HALF = ((0, 64), (64, 128))
-    LANES = (0, N)
+    LANES = (0, N + 16)
+
+    def seat(a, b):
+        return (a, b) if a < CUT else (a + 16, b + 16)
 
     for s in range(2):
         rows = slice(64 * s, 64 * s + 64)
         q2 = "sp" if s else "act"
-        dmas("l_c%d" % s, [("sp", v("C%d" % s, 0, V, p=h), T.ch[rows, :]) for h in HALF], 6.0 + 5.0 * s)
+        dmas("l_c%d" % s, [("sp", v("C%d" % s, 0, V, p=h), T.ch[rows, :]) for h in HALF], 6.0 + 2.0 * s,
+             after=batches.get(("l_n0", 128), ()))
         dmas("l_n%d" % s, [(q2, v("nm%d" % s, 6 * j, 6 * j + 6, p=h), z[rows, 6 * r:6 * r + 6])
                            for j, z in enumerate((T.ia, T.ic, T.sb)) for r, h in enumerate(HALF)]
              + [(q2, v("thi%d" % s, p=h), T.th[rows, :]) for h in HALF], 2.0)
-        dmas("l_x%d" % s, [(q2, v("X%d" % s, XO, XO + V, p=h), T.x[rows, :]) for h in HALF], 6.5 + 5.0 * s)
+        dmas("l_x%d" % s, [(q2, v("X%d" % s, XO, XO + V, p=h), T.x[rows, :]) for h in HALF], 6.0 + 2.5 * s,
+             after=batches[("l_n0", 128)] if s else ())
         dmas("l_y%d" % s, [("sp", v("ya%d" % s, p=h), T.y[rows, N * r:N * r + N]) for r, h in enumerate(HALF)], 3.0)
 
-    PF, RF, P64, H16, H15, G16, PM, KC, SP0, SP1, LO = [v("pc", j, j + 1) for j in range(11)]
+    PF, RF, P64, H16, H15, G16, PM, KC, SP0, PL, LO = [v("pc", j, j + 1) for j in range(11)]
     iota(v("pi", 0, 1), [[0, 1]], 0, 1)
     iota(v("xr"), [[1, 144]], 0, 0)
     iota(v("gq"), [[0, 2], [16, 8]], 0, 0)
     iota(v("li", 0, 8), [[16, 8]], 15, 0)
     iota(v("li", 8, 14), [[1, 6]], 0, 0)
-    iota(v("rq"), [[-16, 6], [1, N]], 0, 0)
-    iota(v("sp"), [[0, 2], [16, 6]], -(2048 + XO + 2 * 8192), 0)
+    iota(v("rq", 0, 150), [[-16, 3], [1, 50]], 0, 0)
+    iota(v("rq", 150, 444), [[-16, 3], [1, 98]], -48, 0)
+    iota(v("sp"), [[-16, 6]], 2048, 0)
     iota(v("rp"), [[0, 9], [1, 16]], 0, 0)
     iota(v("w1"), [[16, 8], [0, 16]], 0, 0)
     iota(v("w2"), [[0, 2], [1, 64]], 0, 0)
@@ -451,7 +491,7 @@ def rank_program(g, core, T, topo):
     tt(G16, P64, RF, A.subtract)
     ts(PM, PF, -64.0, A.add)
     ts(KC, RF, -2.0 ** -13, A.mult)
-    ts(SP0, RF, 0.0, A.is_equal)
+    ts(SP0, RF, 0.0, A.is_equal, 4096.0, A.mult)
     ts(LO, PF, 64.0, A.is_ge, float(N), A.mult)
     ts(v("lf"), v("lf"), RF, A.add, LO, A.add)
 
@@ -472,6 +512,7 @@ def rank_program(g, core, T, topo):
     Ih, NIh, Hh = scaled("IH", (None, Ib), (1.0, -1.0, 0.5))
     ts(v("KD", 256, 384), Ib, 0.25, A.mult)
     ts(v("GB", 0, 16), v("gq"), H16, A.is_equal)
+    ts(v("GB", 8, 16), v("GB", 0, 8), -1.0, A.mult)
     ts(v("GB", 16, 24), v("GB", 0, 8), -2.0 ** -9, A.mult)
     ts(v("GH"), v("GB", 0, 8), 2.0 ** -8, A.mult)
     ts(v("E16"), v("xr"), H15, A.is_equal)
@@ -482,26 +523,31 @@ def rank_program(g, core, T, topo):
     for r, c in enumerate((PF, PM)):
         ts(SPb[r], v("w2"), c, A.is_equal)
         cp(SPh[r], SPb[r])
-        ts(SP8[r], SPb[r], -8192.0, A.mult)
     ts(BOh, v("w1"), H16, A.is_equal)
     ts(BO64, BOh, -2.0 ** -7, A.mult)
     ts(BO2, v("w3"), G16, A.is_equal)
     fill(v("one"), 1.0)
-    ts(v("d0"), v("rq"), RF, A.is_equal, 2.0, A.mult)
-    fill(v("d0", 0, 6 * N, N), -8.0)
+    ts(PL, PF, float(N), A.is_ge, -16.0, A.mult)
+    ts(v("nb"), v("nb"), PL, A.add)
+    ts(v("JB", 0, N), v("xr", 0, N), PL, A.subtract, PF, A.is_equal)
+    fill(v("JB", CUT, N, p=(64, N)), 0.0)
+    ts(v("JB", N, 2 * N), v("JB", 0, N), -1.0, A.mult)
+    ts(v("d0"), v("rq"), RF, A.is_equal, 8192.0, A.mult)
     ts(v("d0", 1, 2), v("d0", 1, 2), SP0, A.add)
-    ts(v("sp"), v("sp"), RF, A.add)
+    for c, n in SETS_OF:
+        fill(v("d0", SEG[c], SEG[c] + 3 * n, n), -32768.0)
+        fill(v("d0", SEG[c] + n - 2, SEG[c] + 3 * n, n), -12288.0)
+        ts(v("d0", SEG[c] + n - 1, SEG[c] + 3 * n, n), v("sp", c, c + 3), RF, A.subtract)
     ts(v("KD", 0, 128), Ib, KC, A.mult)
     ts(v("KD", 128, 256), Ib, -49.0 * 2.0 ** -19, A.mult)
     ts(v("rst"), v("rp", 0, 128), 0.0, A.is_equal, -8.0, A.mult)
     ts(v("dm"), v("rp", 0, N), RF, A.is_equal)
     fill(v("n128"), -128.0)
     for j in range(12):
-        ts(v("DG", N * j, N * j + N), v("IB", 0, N), v("nb", j, j + 1), A.mult)
-    ts(v("DG", 12 * N, 13 * N), v("IB", 0, N), -8.0, A.mult)
-
-    def top(w, n=N):
-        return (w[0], w[1], w[1] + n, 1, 0, N)
+        ts(v("DG", N * j, N * j + N), v("JB", 0, N), v("nb", j, j + 1), A.mult)
+    ts(v("DG", 12 * N, 13 * N), v("JB", 0, N), -8.0, A.mult)
+    cp(v("DG", 13 * N, 14 * N), v("JB", 0, N))
+    Jb, NJb, Jh = v("JB", 0, N, p=LANES), v("JB", N, 2 * N, p=LANES), v("DG", 13 * N, 14 * N, p=LANES)
 
     for s in range(2):
         def u(name, a=0, b=None, st=1, p=(0, 128)):
@@ -514,7 +560,7 @@ def rank_program(g, core, T, topo):
         ts(u("TD"), Ib, u("nt", 0, 1), A.mult, 1.0, A.mult)
         for j in range(2):
             fill(u("kf", 4 * N * j + 3 * N, 4 * N * j + 4 * N), 1.0)
-        fill(u("eq"), 0.0)
+        fill(u("eq"), -8192.0)
         fill(u("FT"), 0.0)
         fill(u("key"), 0.0)
     send("r_c", v("cin"), v("bu"))
@@ -534,7 +580,8 @@ def rank_program(g, core, T, topo):
         nbase = lim + lev * L
         last = lev == LV - 1
         where[:] = [KINDS[lev], 2 * step + s, {}]
-        Xw, Cw = u("X", XO, XO + lim), u("C", 0, lim - (LV - 1 - lev) * L if t else lim)
+        seen = lim - L if t and not lev else lim
+        Xw, Cw = u("X", XO, XO + seen), u("C", 0, lim - (LV - 1 - lev) * L if t else lim)
         yv = u(("ya", "yb", "yc")[t])
         ko, fo, lo, lp = 3 * N * (step % 2), 4 * N * (step % 2), 18 * (step % 2), 18 * ((step + 1) % 2)
         aL, mx, tl, tl2, an, nl = [u("nf", 6 * j, 6 * j + 6) for j in (0, 5, 6, 7, 8, 9)]
@@ -564,7 +611,7 @@ def rank_program(g, core, T, topo):
                     mm(u("KA", m0, m1), [(v("EB", 15 - k, 143 - k), u("AF", 16 * m0 + k, 16 * m1, 16)) for k in range(16)])
                 else:
                     bank, a, b, w = place[name]
-                    mms([(u(bank, a + k, b, 16, (m0, m1)), u(name, 16 * m0 + k, 16 * m1, 16), w) for k in range(16)],
+                    mms([(u(bank, a + k, b, 16, seat(m0, m1)), u(name, 16 * m0 + k, 16 * m1, 16), w) for k in range(16)],
                         stop=False, into=True)
 
         made = {k: set() for k in ("B", "F", "E", "U", "AH")}
@@ -583,7 +630,7 @@ def rank_program(g, core, T, topo):
         walk = WALK0 if WALK0 and lev == 0 and t > 0 else WALK
         for kind, a, b in walk:
             c0, c1 = 16 * a, 16 * b
-            q = {"B": 2, "b": 2, "F": 1, "C": 1, "E": 0}[kind]
+            q = {"B": 2, "b": 2, "F": 1, "f": 1, "C": 1, "E": 0}[kind]
             kid = (Xw, u("ku", ko + q * N + a, ko + q * N + b))
             Bt, E, Fd, Ct = [u(k, c0, c1) for k in ("Bt", "E", "Fd", "Ct")]
             BULK[0] = True
@@ -594,13 +641,17 @@ def rank_program(g, core, T, topo):
             elif kind == "C":
                 act(Ct, kid, AF.Copy)
             else:
-                tt(Fd if kind == "F" else E, kid, Bt, A.subtract)
+                tt(E if kind == "E" else Fd, kid, Bt, A.subtract)
             BULK[0] = False
             if (kind, a, b) == walk[0]:
                 ops[i0]["gate"] = 2 * step + s
-            made[{"b": "B", "C": "F"}.get(kind, kind)].update(range(a, b))
+            made[{"b": "B", "C": "F", "f": "F"}.get(kind, kind)].update(range(a, b))
             if kind == "F":
                 act(u("AF", c0, c1), Fd, AF.Abs)
+            elif kind == "f":
+                ts(u("AF", c0, c1), Fd, 0.0, A.max, 2.0, A.mult)
+                mms([(u("KA", k, 128, 16, seat(a, b)), u("Fd", c0 + k, c1, 16), v("GB", 8, 16)) for k in range(16)],
+                    stop=False, into=True)
             elif kind == "C":
                 on_scalar.update(range(a, b))
                 H = bank(c1 - c0)
@@ -613,7 +664,7 @@ def rank_program(g, core, T, topo):
                         ts(u("U", 16 * h0, 16 * h1), u("E", 16 * h0, 16 * h1), 1.0 / 32, A.add, 31.0 / 1024, A.max)
                 sums("E", upto("E"))
                 sums("U", upto("U"))
-            if kind in "FC":
+            if kind in "FfC":
                 sums("AF", upto("F"))
                 if upto("F") == N and AFT:
                     mms([(lanes("KA", 0, 128), v("one"), v("KD", 256, 384))], into="close")
@@ -629,14 +680,15 @@ def rank_program(g, core, T, topo):
                     act(w["AH"], H, AF.Abs)
                     sums("AH", upto("AH"))
         col, only, x = lanes("S", 128, 256), lanes("S", 256, 384), lanes("M", 384, 512)
-        mms([(lanes("KB", 0, 128), top(IKb), lanes("S", 0, 128)) if AFT else (lanes("KB", 0, 128), u("S", 0, N), IKb)],
+        mms([(lanes("KB", 0, 128), part(v("IB", 256, 256 + N + 16), LANES), lanes("S", 0, 128))],
             into="close")
         if COL_ON_VECTOR:
             ts(col, lanes("KB", 0, 128), 1024.0, A.is_gt, 2.0, A.mult)
         else:
             act(col, lanes("KB", 0, 128), AF.Sign, bias=-1024.0)
+        act(only, lanes("KB", 0, 128), AF.Sign, bias=1024.0)
         mms([(x, v("one"), v("KD", 128, 256))], into="close")
-        mm(u("KA", 128 + 3 * N, 512), [(col, top(Ib))])
+        mm(u("KA", 128 + N, 128 + 2 * N), [(col, Jb)])
         if ROUND_ON_SCALAR:
             act(lanes("rr"), x, AF.Identity, bias=MAGIC)
             act(lanes("rr"), lanes("rr"), AF.Identity, bias=-MAGIC)
@@ -650,21 +702,33 @@ def rank_program(g, core, T, topo):
         def hot(out, j, h=(0, 128)):
             return [(out, lanes("oh", h[0], h[1]), v("DG", N * j, N * j + N, p=LANES))]
 
-        q0 = 2 if last else 0
-        mms([(u("KA", 128 + q * N, 128 + q * N + N), lanes("oh"), top(Ih)) for q in range(q0, 3)], each=1)
-        tt(u("PR", q0 * N, 4 * N), u("KA", 128 + q0 * N, 512), u("kf", fo + q0 * N, fo + 4 * N), A.mult)
-        mm(u("M", 6 * q0, 24), [(v("E16", 15 - r, 143 - r), u("PR", q0 * N + r, 4 * N, 16)) for r in range(16)])
-        mm(u("M", 24, 24 + N), [(BOh, u("PR", 2 * N, 3 * N))])
-        ts(u("Lu", lo + 6 * q0, lo + 18), u("M", 6 * q0, 18), 2048.0, A.add)
+        def listed(out, a, b):
+            mm(out, [(v("E16", 15 - r, 143 - r), u("PR", a + r, b, 16)) for r in range(16)])
+
+        mm(u("KA", 128, 128 + N), [(lanes("oh"), Jh)])
+        tt(u("PR", 2 * N, 4 * N), u("KA", 128, 128 + 2 * N), u("kf", fo + 2 * N, fo + 4 * N), A.mult)
+        if not last:
+            for q in range(2):
+                tt(u("PR", q * N, q * N + N), u("KA", 128, 128 + N), u("kf", fo + q * N, fo + q * N + N), A.mult)
+            if SPLIT:
+                listed(u("KA", 320, 332), 0, 2 * N)
+                ts(u("Lu", lo, lo + 12), u("KA", 320, 332), 2048.0, A.add)
+        q0 = 2 if last or SPLIT else 0
+        listed(u("KB", 128 + 6 * q0, 152), q0 * N, 4 * N)
+        mm(u("KB", 152, 152 + N), [(BOh, u("PR", 2 * N, 3 * N))])
+        ts(u("Lu", lo + 6 * q0, lo + 18), u("KB", 128 + 6 * q0, 146), 2048.0, A.add)
         for c in range(5, -1, -1):
-            ts(u("eq", N * c, N * c + 16 * c + 16), u("M", 24, 24 + 16 * c + 16), u("M", 12 + c, 13 + c), A.is_equal)
-        zl = u("zl", 12 * lev, 12 * lev + 6)
-        cp(u("zl", 12 * lev, 12 * lev + 12), u("M", 12, 24))
-        if lev == 1:
-            tt(mx, u("zl", 6, 12), u("zl", 18, 24), A.max)
+            ts(u("eq", SEG[c], SEG[c] + 16 * c + 16), u("KB", 152, 152 + 16 * c + 16), u("KB", 140 + c, 141 + c),
+               A.is_equal, 4096.0, A.mult)
+        for c, n in SETS_OF:
+            ts(u("eq", SEG[c] + n - 1, SEG[c] + 3 * n, n), u("KB", 140 + c, 143 + c), -1.0, A.mult, -float(XO), A.add)
+        if lev == 0:
+            cp(mx, u("KB", 146, 152))
+        elif not last:
+            tt(mx, u("KB", 146, 152), mx, A.max)
         if last:
             ab = u("ab", 0, 6)
-            tt(tl, u("M", 18, 24), mx, A.max)
+            tt(tl, u("KB", 146, 152), mx, A.max)
             ts(ab, tl, 1.0 + 16 * COL_ON_VECTOR, A.is_gt, -8192.0, A.mult)
             tt(tl2, v("lf", 6 * t, 6 * t + 6), ab, A.add)
             if t < TV - 1:
@@ -680,21 +744,21 @@ def rank_program(g, core, T, topo):
             else:
                 dmas("out", [("sp", T.so[rows, 6 * r:6 * r + 6], part(bL[3], h)) for r, h in enumerate(HALF)], 2.0)
         scan(u("sc"), v("d0"), u("eq"), 0.0, A.add, A.max)
-        mms([(u("M", 168 + 6 * r, 174 + 6 * r), w, a) for r in range(2)
-             for w, a in ((SPh[r], zl), (SP8[r], u("sc", N - 1, 6 * N, N)))], each=2)
-        tt(u("tg"), u("M", 168, 180), v("sp"), A.max)
-        ts(u("Tu"), u("tg"), 2048.0 + XO + 2 * 8192.0, A.add)
+        mms([(u("KB", 248 + 6 * r + c, 251 + 6 * r + c), SPh[r], u("sc", SEG[c] + n - 1, SEG[c] + 3 * n, n))
+             for r in range(2) for c, n in SETS_OF], each=1)
+        ts(u("Tu"), u("KB", 248, 260), -1.0, A.mult, 2048.0, A.add)
         sm = u("hb", 2 * N, 3 * N)
-        act(sm, (Xw, u("Lu", lo + 12, lo + 18)), AF.Copy)
-        for r in range(2):
-            mm(u("KA", 320 + N * r, 320 + N * r + N), [(SPb[r], yv), (SPb[r], sm)])
-        act(u("hb", 0, 2 * N), u("KA", 320, 320 + 2 * N), AF.Identity, bias=127.75, scale=0.5)
+        if SUM_ON_VECTOR:
+            tt(sm, (Xw, u("Lu", lo + 12, lo + 18)), yv, A.add)
+        else:
+            act(sm, (Xw, u("Lu", lo + 12, lo + 18)), AF.Copy)
+        mms([(u("M", N * r, N * r + N), SPb[r], a) for r in range(2) for a in ([sm] if SUM_ON_VECTOR else [yv, sm])],
+            each=1 if SUM_ON_VECTOR else 2)
+        act(u("hb", 0, 2 * N), u("M", 0, 2 * N), AF.Identity, bias=127.75, scale=0.5)
         for r in (1, 0):
-            tt((u("X", 0, XO + lim), u("Tu", 6 * r, 6 * r + 6)), u("hb", N * r, N * r + N), v("n128"), A.add)
-        act(only, lanes("KB", 0, 128), AF.Sign, bias=1024.0)
-        MX, sg = u("KB", 256, 256 + N), u("S", 384, 384 + N)
-        mms([(MX, lanes("sel"), top(Ih)), (MX, Hh, u("PR", 3 * N, 4 * N)), (MX, only, top(Ib)),
-             (MX, lanes("S", 0, 128), top(NIb)) if AFT else (MX, NIb, u("S", 0, N))]
+            tt((u("X", 0, XO + seen), u("Tu", 6 * r, 6 * r + 6)), u("hb", N * r, N * r + N), v("n128"), A.add)
+        MX, sg = u("KB", 260, 260 + N), u("S", 384, 384 + N)
+        mms([(MX, lanes("sel"), Jh), (MX, Hh, u("PR", 3 * N, 4 * N)), (MX, only, Jb), (MX, lanes("S", 0, 128), NJb)]
             + ([] if last else hot(MX, 12)))
         act(sg, MX, AF.Sign, bias=-1.0 - 0.5 * COL_ON_VECTOR)
         X1, X2 = u("KA", 128, 128 + N), u("KA", 128 + N, 128 + 2 * N)
@@ -707,15 +771,16 @@ def rank_program(g, core, T, topo):
         mm(X2, [(Ih, u("kf", fo, fo + N)), (I2Kb, sg)])
         act(u("x2"), X2, AF.Copy)
         nv = u("NV", step * N, step * N + N)
-        mm(u("KB", 384, 384 + N), [(Ib, u("PV", 0, N)), (NIb, u("PV", N, 2 * N)), (Ib, u("PV", 2 * N, 3 * N))])
+        mm(u("M", 192, 192 + N), [(Ib, u("PV", 0, N)), (NIb, u("PV", N, 2 * N)), (Ib, u("PV", 2 * N, 3 * N))])
         if CLIP_ON_VECTOR:
-            ts(nv, u("KB", 384, 384 + N), 0.0, A.max, 63.0, A.min)
+            ts(nv, u("M", 192, 192 + N), 0.0, A.max, 63.0, A.min)
         else:
-            act(u("PV", 3 * N, 4 * N), u("KB", 384, 384 + N), AF.Relu, bias=63.0, scale=-1.0)
+            act(u("PV", 3 * N, 4 * N), u("M", 192, 192 + N), AF.Relu, bias=63.0, scale=-1.0)
             act(nv, u("PV", 3 * N, 4 * N), AF.Relu, bias=63.0, scale=-1.0)
         if t < TV - 1:
-            dmas("xs%d" % s, [("sp", u("X", XO + nbase + N * r, XO + nbase + N * r + N, p=h2), part(nv, h))
-                              for r, h in enumerate(HALF) for h2 in HALF], 2.5, more=4 * (LV - 1 - lev))
+            dmas("x%s%d" % ("t" if last else "s", s),
+                 [("sp", u("X", XO + nbase + N * r, XO + nbase + N * r + N, p=h2), part(nv, h))
+                  for r, h in enumerate(HALF) for h2 in HALF], 2.5, more=4 * (lev == 0))
         else:
             dmas("out", [("sp", T.xo[rows, nbase + N * r:nbase + N * r + N], part(nv, h)) for r, h in enumerate(HALF)], 2.5)
         mo = u("Cf", step * N, step * N + N)
@@ -734,17 +799,17 @@ def rank_program(g, core, T, topo):
                 ts(u("TD"), Ib, u("nt", 1, 2), A.mult)
             ya, yb, ys = u("yt", 0, N), u("yt", N, 2 * N), u("ys", t * N, t * N + N)
             tt(ya, (ab, REP), v("dm"), A.mult)
-            mm(u("KA", 0, N), [(BO64, ya)])
-            tt(yb, u("KA", 0, N), yv, A.min)
-            mm(u("KA", 0, N), [(Ib, yb), (NIb, u("NV", t * LV * N, t * LV * N + N))])
-            act(ys, u("KA", 0, N), AF.Abs)
+            mm(u("KB", 384, 384 + N), [(BO64, ya)])
+            tt(yb, u("KB", 384, 384 + N), yv, A.min)
+            mm(u("KB", 384, 384 + N), [(Ib, yb), (NIb, u("NV", t * LV * N, t * LV * N + N))])
+            act(ys, u("KB", 384, 384 + N), AF.Abs)
             if t < TV - 1:
                 send("r_y%d%d" % (t, s), u(("yb", "yc")[t]), ys)
             else:
                 dmas("out", [("sp", T.yo[rows, N * r:N * r + N], part(ys, h)) for r, h in enumerate(HALF)], 2.0)
                 hw = XW // 2
                 dmas("out", [(q, T.xo[rows, hw * r:hw * r + hw], u("X", XO + hw * r, XO + hw * r + hw, p=HALF[r]))
-                             for r, q in enumerate(("sp", "act"))], 3.5)
+                             for r, q in enumerate(("sp", "act" if s else "sp"))], 3.5 if s else 7.0)
 
     for t in range(TV):
         for lev in range(LV):

from concourse.mybir import AluOpType, ActivationFunctionType
import numpy as np

V, L, TV, LV, HOP = 2304, 192, 3, 3, 3
N = L // 2
XW = V + 2 * LV * L
XO = 96
WALK = (("b", 0, 16), ("F", 0, 16), ("B", 16, 48), ("E", 0, 16), ("C", 16, 48), ("B", 48, 80), ("E", 16, 48),
        ("C", 48, 80), ("B", 80, 96), ("E", 48, 80), ("F", 80, 96), ("E", 80, 96))
UCUT = ((0, 48), (48, 80), (80, 96))
HCUT = ((0, 16), (16, 48), (48, 80), (80, 96))
CUT = 80
SUMS = {k: ((0, CUT), (CUT, N)) for k in ("AF", "E", "U", "AH")}
CLIP_ON_VECTOR = False
SOFT = False
AFT = True
GRAIN = 9999
SPLIT = False
SUM_ON_VECTOR = False
SEG = (0, 50, 100, 150, 248, 346)
SETS_OF = ((0, 50), (3, 98))
COL_ON_VECTOR = False
ROUND_ON_SCALAR = False
WALK0 = None
MAGIC = 1536.0

B16, F16, F32, I32, U16 = "bfloat16", "float16", "float32", "int32", "uint16"
SIZES = {B16: 2, F16: 2, F32: 4, I32: 4, U16: 2}


def _sb(n, d):
    return ("sbuf", [128, n], d)


STREAM = {
    "X": (XW + XO, B16), "C": (XW, I32), "NV": (9 * N, B16), "Cf": (9 * N, F32), "Ci": (6 * N, I32),
    "nm": (18, I32), "thi": (1, I32), "nt": (2, F32), "TD": (128, F16),
    "ya": (N, B16), "yb": (N, B16), "yc": (N, B16), "ys": (3 * N, B16), "yt": (2 * N, B16),
    "L0": (18, U16), "acin": (12, U16), "ain": (8, U16), "snd": (24, U16), "nf": (66, F32), "ab": (16, B16),
    "Bt": (16 * N, B16), "E": (16 * N, B16), "Fd": (16 * N, B16), "U": (16 * N, F16),
    "AF": (16 * N, B16), "AH": (16 * N, B16), "Ct": (16 * N, B16),
    "ku": (6 * N, U16), "kf": (8 * N, F16), "Lu": (36, U16), "PV": (4 * N, B16),
    "S": (384 + N, B16), "key": (128, F32), "FT": (128, F32), "oh": (128, F16), "rr": (128, F32), "sel": (128, F16),
    "PR": (4 * N, F16), "eq": (444, F16), "sc": (444, F16), "Tu": (12, U16),
    "hb": (3 * N, B16), "x2": (N, F32),
}
SCRATCH = {"%s%d" % (k, s): _sb(*w) for k, w in STREAM.items() for s in range(2)}
SCRATCH.update({
    "bu": _sb(12, U16), "cin": _sb(12, U16),
    "pi": _sb(4, I32), "pc": _sb(12, F32), "xr": _sb(144, F32), "w1": _sb(128, F32), "w2": _sb(128, F32),
    "w3": _sb(128, F32), "rp": _sb(144, F32), "li": _sb(24, I32), "lu": _sb(24, U16), "nb": _sb(12, F32),
    "lf": _sb(18, F32), "gq": _sb(16, F32),
    "IB": _sb(5 * 128, B16), "IH": _sb(3 * 128, F16), "SB": _sb(4 * 128, B16), "SH": _sb(5 * 128, F16),
    "E16": _sb(144, F16), "GB": _sb(24, B16), "GH": _sb(8, F16), "one": _sb(N + 16, F16), "JB": _sb(2 * N, B16), "KD": _sb(384, F16),
    "rq": _sb(444, F32), "sp": _sb(6, F32), "d0": _sb(444, F16), "rst": _sb(128, F32), "dm": _sb(N, B16), "DG": _sb(14 * N, F16), "n128": _sb(N, B16),
})
BANKS = ("H0", "H1", "KA0", "KB0", "M0", "KA1", "KB1", "M1")
for _b in BANKS:
    SCRATCH[_b] = ("psum", [128, 512], F32)

OWN = ["l_c", "l_x", "l_n", "l_y", "xs", "xt", "cs0", "cs1", "cs2"]
ARRIVE = ["r_c"] + [k + str(s) for k in ("r_a0", "r_y0", "r_a1", "r_y1") for s in range(2)]
SEMAPHORES = ["pe", "dve", "act", "pool", "sent", "out"] + [k + str(s) for k in OWN for s in range(2)] + ARRIVE

CY, PCY = np.array([0.85e-3, 0.83e-3, 0.92e-3, 1.2e-3]), np.array([0.43e-3, 0.42e-3, 0.47e-3, 0.6e-3])
GA, SCA = np.array([1.56, 1.2, 1.56, 2.0]), np.array([3.8, 2.5, 3.8, 5.5])
OV = np.array([0.0, 0.5, 0.0, 0.5])
HS, HO, WEIGHT = (0.15, 0.1, 0.06, 0.2), (0.27, 0.2, 0.15, 0.35), (1.0, 1.0, 1.0, 0.7)
HOP_SAME, HOP_OTHER = HS[0], HO[0]
LOOKS, ROUNDS, TRIES = (0.2, 0.5, 0.35), 3, 20
BEATS = (10.0, 12.0, 9.0, 14.0, 11.0)
PATTERN = 0.0
POLISH = 24000
SETS, HEAT, WIDE, FILL, SMOOTH = (0, 1, 3), 0.25, 0.1, 0.3, 0.3
KINDS = ("a", "b", "c")


def one_pass(qs, dur, lat, pred, succ, free_pairs, prio, back, look, early=None):
    n = len(qs)
    left = [len(p) for p in pred]
    ready_at = list(early) if early else [lat[i] if back else 0.0 for i in range(n)]
    ready, free, order = {}, {}, []
    start, fin = [0.0] * n, [0.0] * n
    for i in range(n):
        if left[i] == 0:
            ready.setdefault(qs[i], []).append(i)
    while len(order) < n:
        pick, pt = None, None
        for q, lst in ready.items():
            if not lst:
                continue
            t0 = max(free.get(q, 0.0), min(ready_at[i] for i in lst))
            if pt is not None and t0 >= pt[0]:
                continue
            now = max((i for i in lst if ready_at[i] <= t0), key=lambda i: (prio[i], -i))
            for i in lst:
                if ready_at[i] > t0 and prio[i] > prio[now] and ready_at[i] - t0 < look * dur[now]:
                    now = i
            pick, pt = now, (t0, max(t0, ready_at[now]))
        q = qs[pick]
        ready[q].remove(pick)
        start[pick] = pt[1]
        free[q] = pt[1] + dur[pick]
        fin[pick] = free[q] + (0.0 if back else lat[pick])
        order.append(pick)
        for s in succ[pick]:
            hop = HOP_OTHER if qs[s] != q else 0.0 if (min(s, pick), max(s, pick)) in free_pairs else HOP_SAME
            r = fin[pick] + hop + (lat[s] if back else 0.0)
            ready_at[s] = max(ready_at[s], r)
            left[s] -= 1
            if left[s] == 0:
                ready.setdefault(qs[s], []).append(s)
    return order, start, fin, max(fin)


PLANNED = {}


def order_ops(ops):
    n = len(ops)
    reach = []
    for o in ops:
        m = 0
        for d in o["deps"]:
            m |= reach[d]
        o["deps"] = [d for d in o["deps"] if not m >> d & 1]
        for d in o["deps"]:
            m |= 1 << d
        reach.append(0 if o["q"] == "net" or o["sem"] == ("sent", 0) else m)
    qs, dur, lat = [o["q"] for o in ops], [o["dur"] for o in ops], [o["lat"] for o in ops]
    pred = [o["deps"] + o["soft"] for o in ops]
    pairs = {(d, i) for i, o in enumerate(ops) for d in o["soft"]}
    keyed = (n, sum(dur), sum(len(p) for p in pred))
    if keyed not in PLANNED:
        succ = [[] for _ in range(n)]
        for i in range(n):
            for d in pred[i]:
                succ[d].append(i)
        def urgency(beat):
            base = [0.0] * n
            for i in range(n - 1, -1, -1):
                base[i] = dur[i] + lat[i] + max(
                    [base[s] + (HOP_OTHER if qs[s] != qs[i] else 0.0 if (i, s) in pairs else HOP_SAME)
                     for s in succ[i]] + [0.0])
                if "gate" in ops[i]:
                    base[i] = max(base[i], (2 * TV * LV + 1 - ops[i]["gate"]) * beat)
            return base

        best = None
        rng = np.random.default_rng(1)
        for trial in range(TRIES):
            look = LOOKS[trial % len(LOOKS)]
            prio = urgency(BEATS[trial // 2 % len(BEATS)]) if trial % 2 == 0 else [-s for s in best[1]]
            prio = [p + float(e) for p, e in zip(prio, rng.normal(0.0, 0.3 if trial else 1e-9, n))]
            for _ in range(ROUNDS):
                fw = one_pass(qs, dur, lat, pred, succ, pairs, prio, False, look)
                if best is None or fw[3] < best[3]:
                    best = fw
                prio = one_pass(qs, dur, lat, succ, pred, pairs, fw[2], True, look)[2]
        durs = [[float(x) for x in np.broadcast_to(o["durs"], CY.shape)] for o in ops]
        same = [[d for d in o["deps"] if qs[d] == o["q"]] for o in ops]
        other = [[d for d in o["deps"] if qs[d] != o["q"]] for o in ops]

        def lengths(order):
            res = []
            for m in range(len(CY)):
                hs, ho = float(HS[m]), float(HO[m])
                free, fin = {}, [0.0] * n
                for i in order:
                    q = qs[i]
                    t = free.get(q, 0.0)
                    for d in same[i]:
                        if fin[d] + hs > t:
                            t = fin[d] + hs
                    for d in other[i]:
                        if fin[d] + ho > t:
                            t = fin[d] + ho
                    free[q] = t + durs[i][m]
                    fin[i] = free[q] + lat[i]
                res.append(max(fin))
            return res

        def length(order):
            return sum(x * w for x, w in zip(lengths(order), WEIGHT))

        def held(order, m):
            hs, ho, dm = float(HS[m]), float(HO[m]), col[m]
            free, last, fin, why, start = {}, {}, [0.0] * n, [None] * n, [0.0] * n
            for i in order:
                q = qs[i]
                t, w = free.get(q, 0.0), last.get(q)
                for d in same[i]:
                    if fin[d] + hs > t:
                        t, w = fin[d] + hs, -1 - d
                for d in other[i]:
                    if fin[d] + ho > t:
                        t, w = fin[d] + ho, -1 - d
                start[i], why[i], last[q] = t, w, i
                free[q] = t = t + dm[i]
                fin[i] = t + lat[i]
            end = max(fin)
            i, found = fin.index(end) if rng.random() < 0.5 else int(rng.integers(n // 4, n)), [(order[0], order[0])]
            while why[i] is not None:
                if why[i] >= 0:
                    found.append((why[i], i))
                i = why[i] if why[i] >= 0 else -1 - why[i]
            return end + SMOOTH * sum(start) / n, start, found

        def judge(order):
            res = [held(order, m) for m in SETS]
            return sum(r[0] * WEIGHT[m] for r, m in zip(res, SETS)), order, res

        col = [[d[m] for d in durs] for m in range(len(CY))]
        alike = {(o["kind"][1:], o["turn"]): i for i, o in enumerate(ops) if o["kind"][0] != "start"}
        now = top = judge(best[0])
        if PATTERN:
            gate = {o["gate"]: best[1][i] for i, o in enumerate(ops) if "gate" in o}
            tried = []
            for j in range(2, 2 * TV * LV - 2):
                beat = (gate[j + 1] - gate[j - 1]) / 2
                key = [best[1][i] - gate[0] if o["kind"][0] == "start" else o["turn"] * beat + best[1][
                    alike.get((o["kind"][1:], j), i)] - gate[j if (o["kind"][1:], j) in alike else o["turn"]]
                    for i, o in enumerate(ops)]
                for i in range(n):
                    for d in pred[i]:
                        if key[d] >= key[i]:
                            key[i] = key[d] + 1e-4
                tried.append(judge(np.argsort(key, kind="stable").tolist()))
            now = min(tried, key=lambda e: e[0])
        for trial in range(POLISH):
            found = now[2][trial // 2 % len(SETS)][2]
            j = int(rng.integers(len(found)))
            a, b = found[j]
            for _ in range(int(rng.integers(3))):
                j -= 1 - 2 * (trial % 2)
                if 0 <= j < len(found) and found[j][1] == a:
                    a = found[j][0]
                elif 0 <= j < len(found) and found[j][0] == b:
                    b = found[j][1]
            key = [0.0] * n
            for p, i in enumerate(now[1]):
                key[i] = float(p)
            if trial % 2 and rng.random() < FILL:
                start, dm = now[2][trial // 2 % len(SETS)][1], col[SETS[trial // 2 % len(SETS)]]
                mine = [i for i in now[1][max(0, int(key[a]) - 150):int(key[a]) + 1] if qs[i] == qs[a]]
                gaps = [e for d, e in zip(mine, mine[1:-1]) if start[e] > start[d] + dm[d] + 0.04]
                if gaps:
                    a, b = gaps[-1 - int(rng.integers(min(4, len(gaps))))], a
            moves = [(a, b)]
            if rng.random() < WIDE + (trial < PATTERN * POLISH) and "start" not in (ops[a]["kind"][0], ops[b]["kind"][0]):
                ka, kb, gap = ops[a]["kind"][1:], ops[b]["kind"][1:], ops[b]["turn"] - ops[a]["turn"]
                moves = [(alike[ka, u], alike[kb, u + gap]) for u in range(2 * TV * LV)
                         if (ka, u) in alike and (kb, u + gap) in alike and key[alike[ka, u]] < key[alike[kb, u + gap]]]
            if trial % 2:
                for a, b in moves:
                    key[b] = key[a] - 0.5
                for i in range(n - 1, -1, -1):
                    for d in pred[i]:
                        if key[d] >= key[i]:
                            key[d] = key[i] - 1e-4
            else:
                for a, b in moves:
                    key[a] = key[b] + 0.5
                for i in range(n):
                    for d in pred[i]:
                        if key[d] >= key[i]:
                            key[i] = key[d] + 1e-4
            new = judge(np.argsort(key, kind="stable").tolist())
            if new[0] <= now[0] + HEAT * (1.0 - trial / POLISH) * float(rng.random()) ** 2:
                now = new
                if new[0] < top[0]:
                    top = new
        best = (top[1], top[2][0][1], None, 0.0)
        PLANNED[keyed] = best + (lengths(best[0]),)
    order, start, _fin, _end, ends = PLANNED[keyed]
    for i in range(n):
        ops[i]["start"] = start[i]
    return order, ends


def rank_program(g, core, T, topo):
    rank = T.rank_of(core)
    if rank is None:
        return
    A, AF = AluOpType, ActivationFunctionType
    nr = len(T.cores)
    dst = T.cores[(rank + HOP) % nr]
    src = T.cores[(rank - HOP) % nr]
    rid, pid, _ = topo.addr(dst)
    mask_out = topo.mask(core, dst)
    n_out = len(topo.engines(core, dst))
    n_in = len(topo.engines(src, core))
    Q = {"pe": g.tensor, "dve": g.vector, "act": g.scalar, "pool": g, "sp": g.sync}
    ops, hist, bank_last, batches, totals, turn, BULK = [], {}, {}, {}, {}, {}, [False]
    closer, where = {}, ["start", 0, {}]

    def v(name, a=0, b=None, s=1, p=(0, 128)):
        return (name, a, SCRATCH[name][1][1] if b is None else b, s, p[0], p[1])

    def part(w, p):
        return w[:4] + tuple(p)

    def ap(w):
        if len(w) == 2:
            return ap(w[0]).indirect(ap(w[1]))
        return T[w[0]][w[4]:w[5], w[1]:w[2]] if w[3] == 1 else T[w[0]][w[4]:w[5], w[1]:w[2]:w[3]]

    def cnt(w):
        return 16 * (w[1][2] - w[1][1]) if len(w) == 2 else len(range(w[1], w[2], w[3]))

    def narrow(*ws):
        return all(SIZES[SCRATCH[w[0]][2]] == 2 for w in ws)

    def add(q, fn, rd, wr, dur, lat=0.0, sem=None, after=(), acc=None, tag="", free=False):
        i = len(ops)
        r2, w2 = [], []
        for w in rd:
            r2.extend(list(w) if len(w) == 2 else [w])
        for w in wr:
            if len(w) == 2:
                w2.append(w[0]); r2.append(w[1])
            else:
                w2.append(w)
        deps, soft = set(after), set()
        for lst, isw in ((r2, False), (w2, True)):
            for w in lst:
                for (a, b, pa, pb, j, jw) in hist.get(w[0], ()):
                    if (isw or jw) and a < w[2] and w[1] < b and pa < w[5] and w[4] < pb:
                        if acc and isw and ops[j]["q"] == "pe":
                            if acc == "close" or not ops[j]["acc"]:
                                soft.add(j)
                        elif free and isw and ops[j]["free"]:
                            soft.add(j)
                        else:
                            deps.add(j)
        for b in {w[0] for w in r2 + w2 if w[0] in BANKS}:
            run = bank_last.setdefault(b, [q, [], []])
            if run[0] != q:
                run[0], run[2], run[1] = q, run[1], []
            elif q == "pe" and acc is not True and run[1]:
                soft.add(run[1][-1])
            run[1].append(i)
            deps.update(run[2])
        for lst, isw in ((r2, False), (w2, True)):
            for w in lst:
                h = hist.setdefault(w[0], [])
                if isw and not acc:
                    h[:] = [e for e in h if not (w[3] == 1 and w[1] <= e[0] and e[1] <= w[2]
                                                 and w[4] <= e[2] and e[3] <= w[5])]
                h.append((w[1], w[2], w[4], w[5], i, isw))
        for d in list(deps):
            if ops[d]["sem"] in batches:
                deps.update(batches[ops[d]["sem"]])
        if BULK[0]:
            soft.update(turn.get(q, ()))
            turn[q] = [i]
        deps.discard(i)
        soft.discard(i)
        ops.append({"q": q, "fn": fn, "acc": acc, "free": free, "deps": sorted(deps), "soft": sorted(soft - deps), "durs": dur,
                    "dur": float(np.ravel(dur)[0]), "lat": lat, "sem": sem, "tag": tag or (w2[0][0] if w2 else "")})
        name = (where[0], q, ops[i]["tag"].rstrip("01"))
        where[2][name] = where[2].get(name, 0) + 1
        ops[i]["kind"], ops[i]["turn"] = name + (where[2][name],), where[1]
        return i

    def vdur(out, ins, per):
        if len(out) == 2:
            return 0.05 + cnt(out) * SCA * CY
        if any(len(w) == 2 for w in ins):
            return 0.05 + cnt(out) * GA * CY
        return max(64, cnt(out) * per) * CY + 0.02 * OV

    def sc_(x):
        return x if isinstance(x, (int, float)) or x is None else ap(x)

    def cols(*xs):
        return [x for x in xs if isinstance(x, tuple)]

    def tt(out, a, b, op):
        per = 1.0 if (len(a) > 2 and a[0] in BANKS) or b[0] in BANKS else 1.5
        return add("dve", lambda: g.vector.tensor_tensor(ap(out), ap(a), ap(b), op), [a, b], [out], vdur(out, [a], per),
                   free=SOFT and len(out) == 2)

    def ts(out, a, s1, op0, s2=None, op1=None):
        per = 0.5 if len(a) > 2 and narrow(out, a) else 1.0
        if op1 is None:
            fn = lambda: g.vector.tensor_scalar(ap(out), ap(a), sc_(s1), None, op0)
        else:
            fn = lambda: g.vector.tensor_scalar(ap(out), ap(a), sc_(s1), sc_(s2), op0, op1)
        return add("dve", fn, [a] + cols(s1, s2), [out], vdur(out, [a], per))

    def cp(out, a):
        per = 0.5 if len(a) > 2 and narrow(out, a) else 1.0
        return add("dve", lambda: g.vector.tensor_copy(ap(out), ap(a)), [a], [out], vdur(out, [a], per))

    def scan(out, d0, d1, init, op0, op1):
        per = 0.5 if narrow(out, d0, d1) else 1.0
        return add("dve", lambda: g.vector.tensor_tensor_scan(ap(out), ap(d0), ap(d1), init, op0, op1),
                   [d0, d1], [out], vdur(out, [d1], per))

    def fill(out, c):
        return add("dve", lambda: g.vector.memset(ap(out), c), [], [out], vdur(out, [], 0.5))

    def act(out, a, func, bias=0.0, scale=1.0):
        dur = 0.065 + cnt(out) * GA * CY if len(a) == 2 else max(64, cnt(out)) * CY + 0.03 * OV
        fn = lambda: g.scalar.activation(ap(out), ap(a), func, bias=sc_(bias), scale=scale)
        return add("act", fn, [a] + cols(bias), [out], dur)

    def mms(terms, stop=True, each=False, into=None):
        run = each or len(terms)
        parts, cycles = [[]], 0
        for k, (o, w, x) in enumerate(terms):
            c = max(min(64, cnt(w)), cnt(o))
            if parts[-1] and cycles + c > GRAIN:
                parts.append([])
                cycles = 0
            parts[-1].append((o, w, x, into is None and k % run == 0, stop and k % run == run - 1))
            cycles += c
        for j, some in enumerate(parts):
            def fn(some=some):
                return [g.tensor.matmul(ap(o), ap(w), ap(x), a, b) for o, w, x, a, b in some][-1]
            add("pe", fn, list({z: 0 for t in some for z in t[1:3]}), list({t[0]: 0 for t in some}),
                sum(max(min(64, cnt(t[1])), cnt(t[0])) for t in some) * PCY + 0.05 * OV / len(parts),
                acc=into or (j > 0 and "close"))

    def mm(out, terms):
        return mms([(out, w, x) for w, x in terms])

    def iota(out, pat, base, mult):
        if SCRATCH[out[0]][2] == I32:
            fn = lambda: g.iota(ap(out), pat, base, mult)
        else:
            fn = lambda: g.iota(ap(out), pat, base, mult, allow_small_or_imprecise_dtypes=True)
        return add("pool", fn, [], [out], 0.13 + 2 * cnt(out) * CY)

    def dmas(sem, moves, lat, more=0, after=()):
        totals[sem] = totals.get(sem, 0) + 16 * len(moves)
        mark = (sem, totals[sem] + 16 * more)
        made = []
        for q, o, a in moves:
            def fn(q=q, o=o, a=a):
                return Q[q].dma_start(ap(o) if isinstance(o, tuple) else o, ap(a) if isinstance(a, tuple) else a)
            made.append(add(q, fn, cols(a), cols(o), 0.1, lat, mark, after, tag=sem))
        batches.setdefault(mark, []).extend(made)

    def send(sem, land, a):
        i = add("pool", lambda: g.remote_dma(ap(land), ap(a), T.sem[sem], T.sem.sent, pid, rid, mask_out),
                [a], [], 1.0, 0.0, ("sent", 0))
        return add("net", None, [], [land], 0.0, 3.5, (sem, n_in), after=[i])

    HALF = ((0, 64), (64, 128))
    LANES = (0, N + 16)

    def seat(a, b):
        return (a, b) if a < CUT else (a + 16, b + 16)

    for s in range(2):
        rows = slice(64 * s, 64 * s + 64)
        q2 = "sp" if s else "act"
        dmas("l_c%d" % s, [("sp", v("C%d" % s, 0, V, p=h), T.ch[rows, :]) for h in HALF], 6.0 + 2.0 * s,
             after=batches.get(("l_n0", 128), ()))
        dmas("l_n%d" % s, [(q2, v("nm%d" % s, 6 * j, 6 * j + 6, p=h), z[rows, 6 * r:6 * r + 6])
                           for j, z in enumerate((T.ia, T.ic, T.sb)) for r, h in enumerate(HALF)]
             + [(q2, v("thi%d" % s, p=h), T.th[rows, :]) for h in HALF], 2.0)
        dmas("l_x%d" % s, [(q2, v("X%d" % s, XO, XO + V, p=h), T.x[rows, :]) for h in HALF], 6.0 + 2.5 * s,
             after=batches[("l_n0", 128)] if s else ())
        dmas("l_y%d" % s, [("sp", v("ya%d" % s, p=h), T.y[rows, N * r:N * r + N]) for r, h in enumerate(HALF)], 3.0)

    PF, RF, P64, H16, H15, G16, PM, KC, SP0, PL, LO = [v("pc", j, j + 1) for j in range(11)]
    iota(v("pi", 0, 1), [[0, 1]], 0, 1)
    iota(v("xr"), [[1, 144]], 0, 0)
    iota(v("gq"), [[0, 2], [16, 8]], 0, 0)
    iota(v("li", 0, 8), [[16, 8]], 15, 0)
    iota(v("li", 8, 14), [[1, 6]], 0, 0)
    iota(v("rq", 0, 150), [[-16, 3], [1, 50]], 0, 0)
    iota(v("rq", 150, 444), [[-16, 3], [1, 98]], -48, 0)
    iota(v("sp"), [[-16, 6]], 2048, 0)
    iota(v("rp"), [[0, 9], [1, 16]], 0, 0)
    iota(v("w1"), [[16, 8], [0, 16]], 0, 0)
    iota(v("w2"), [[0, 2], [1, 64]], 0, 0)
    iota(v("w3"), [[0, 2], [16, 4], [0, 16]], 0, 0)
    iota(v("nb"), [[LV * L, TV], [L, 2], [N, 2]], V + L - 2048, 1)
    iota(v("lf"), [[LV * L, TV], [16, 6]], V, 0)
    cp(v("lu", 0, 14), v("li", 0, 14))
    LAST, REP = v("lu", 0, 8), v("lu", 8, 14)
    ts(v("pi", 1, 2), v("pi", 0, 1), 15, A.bitwise_and)
    ts(v("pi", 2, 3), v("pi", 0, 1), 63, A.bitwise_and)
    cp(v("pc", 0, 3), v("pi", 0, 3))
    tt(H16, PF, RF, A.subtract)
    ts(H15, H16, 15.0, A.add)
    tt(G16, P64, RF, A.subtract)
    ts(PM, PF, -64.0, A.add)
    ts(KC, RF, -2.0 ** -13, A.mult)
    ts(SP0, RF, 0.0, A.is_equal, 4096.0, A.mult)
    ts(LO, PF, 64.0, A.is_ge, float(N), A.mult)
    ts(v("lf"), v("lf"), RF, A.add, LO, A.add)

    def scaled(name, first, scales):
        out = []
        for j, c in enumerate(scales):
            out.append(v(name, 128 * j, 128 * j + 128))
            if c is None:
                continue
            if first[0] is None:
                ts(out[-1], first[1], c, A.mult)
            else:
                ts(out[-1], first[0], first[1], A.is_equal, c, A.mult)
        return out

    Ib, = scaled("IB", (v("xr", 0, 128), PF), (1.0,))
    _, NIb, IKb, I2Kb, N2Kb = scaled("IB", (None, Ib), (None, -1.0, 1024.0, 2048.0, -2048.0))
    Ih, NIh, Hh = scaled("IH", (None, Ib), (1.0, -1.0, 0.5))
    ts(v("KD", 256, 384), Ib, 0.25, A.mult)
    ts(v("GB", 0, 16), v("gq"), H16, A.is_equal)
    ts(v("GB", 8, 16), v("GB", 0, 8), -1.0, A.mult)
    ts(v("GB", 16, 24), v("GB", 0, 8), -2.0 ** -9, A.mult)
    ts(v("GH"), v("GB", 0, 8), 2.0 ** -8, A.mult)
    ts(v("E16"), v("xr"), H15, A.is_equal)
    SPb = [v("SB", 0, 128), v("SB", 128, 256)]
    SPh = [v("SH", 0, 128), v("SH", 128, 256)]
    SP8 = [v("SH", 256, 384), v("SH", 384, 512)]
    BOh, BO64, BO2 = v("SH", 512, 640), v("SB", 256, 384), v("SB", 384, 512)
    for r, c in enumerate((PF, PM)):
        ts(SPb[r], v("w2"), c, A.is_equal)
        cp(SPh[r], SPb[r])
    ts(BOh, v("w1"), H16, A.is_equal)
    ts(BO64, BOh, -2.0 ** -7, A.mult)
    ts(BO2, v("w3"), G16, A.is_equal)
    fill(v("one"), 1.0)
    ts(PL, PF, float(N), A.is_ge, -16.0, A.mult)
    ts(v("nb"), v("nb"), PL, A.add)
    ts(v("JB", 0, N), v("xr", 0, N), PL, A.subtract, PF, A.is_equal)
    fill(v("JB", CUT, N, p=(64, N)), 0.0)
    ts(v("JB", N, 2 * N), v("JB", 0, N), -1.0, A.mult)
    ts(v("d0"), v("rq"), RF, A.is_equal, 8192.0, A.mult)
    ts(v("d0", 1, 2), v("d0", 1, 2), SP0, A.add)
    for c, n in SETS_OF:
        fill(v("d0", SEG[c], SEG[c] + 3 * n, n), -32768.0)
        fill(v("d0", SEG[c] + n - 2, SEG[c] + 3 * n, n), -12288.0)
        ts(v("d0", SEG[c] + n - 1, SEG[c] + 3 * n, n), v("sp", c, c + 3), RF, A.subtract)
    ts(v("KD", 0, 128), Ib, KC, A.mult)
    ts(v("KD", 128, 256), Ib, -49.0 * 2.0 ** -19, A.mult)
    ts(v("rst"), v("rp", 0, 128), 0.0, A.is_equal, -8.0, A.mult)
    ts(v("dm"), v("rp", 0, N), RF, A.is_equal)
    fill(v("n128"), -128.0)
    for j in range(12):
        ts(v("DG", N * j, N * j + N), v("JB", 0, N), v("nb", j, j + 1), A.mult)
    ts(v("DG", 12 * N, 13 * N), v("JB", 0, N), -8.0, A.mult)
    cp(v("DG", 13 * N, 14 * N), v("JB", 0, N))
    Jb, NJb, Jh = v("JB", 0, N, p=LANES), v("JB", N, 2 * N, p=LANES), v("DG", 13 * N, 14 * N, p=LANES)

    for s in range(2):
        def u(name, a=0, b=None, st=1, p=(0, 128)):
            return v(name + str(s), a, b, st, p)
        cp(u("L0"), u("nm"))
        cp(v("bu", 6 * s, 6 * s + 6), u("nm", 12, 18))
        cp(u("nf", 0, 6), u("nm", 0, 6))
        cp(u("nf", 6, 12), u("nm", 12, 18))
        ts(u("nt", 0, 1), u("thi"), -1.0, A.mult, -0.5, A.add)
        ts(u("TD"), Ib, u("nt", 0, 1), A.mult, 1.0, A.mult)
        for j in range(2):
            fill(u("kf", 4 * N * j + 3 * N, 4 * N * j + 4 * N), 1.0)
        fill(u("eq"), -8192.0)
        fill(u("FT"), 0.0)
        fill(u("key"), 0.0)
    send("r_c", v("cin"), v("bu"))

    piece = [0]

    def level(s, t, lev):
        def u(name, a=0, b=None, st=1, p=(0, 128)):
            return v(name + str(s), a, b, st, p)

        def lanes(name, a=0, b=None, st=1):
            return u(name, a, b, st, LANES)

        rows = slice(64 * s, 64 * s + 64)
        lim = V + t * LV * L
        step = t * LV + lev
        nbase = lim + lev * L
        last = lev == LV - 1
        where[:] = [KINDS[lev], 2 * step + s, {}]
        seen = lim - L if t and not lev else lim
        Xw, Cw = u("X", XO, XO + seen), u("C", 0, lim - (LV - 1 - lev) * L if t else lim)
        yv = u(("ya", "yb", "yc")[t])
        ko, fo, lo, lp = 3 * N * (step % 2), 4 * N * (step % 2), 18 * (step % 2), 18 * ((step + 1) % 2)
        aL, mx, tl, tl2, an, nl = [u("nf", 6 * j, 6 * j + 6) for j in (0, 5, 6, 7, 8, 9)]
        bL = [u("nf", 6 + 6 * j, 12 + 6 * j) for j in range(4)]
        if lev == 0 and t > 0:
            a_in = u("acin", 0, 6) if t == 1 else u("ain", 0, 6)
            c_in = v("cin", 6 * s, 6 * s + 6) if t == 1 else u("acin", 6, 12)
            lists = [(2, 3, u("snd", 12 * t - 6, 12 * t)), (1, 2, c_in), (0, 1, a_in)]
            cp(aL, a_in)
        else:
            lists = [(0, 3, u("Lu", lp, lp + 18) if lev else u("L0"))]
        for q0, q1, lst in lists:
            cp(u("ku", ko + q0 * N, ko + q1 * N), (Cw, lst))
            act(u("PV", q0 * N, q1 * N), (Xw, lst), AF.Copy)
        ts(u("kf", fo, fo + 3 * N), u("ku", ko, ko + 3 * N), -2048.0, A.add)
        mms([(lanes("KB", 0, 128), v("one"), u("TD"))], stop=False)
        if AFT:
            mms([(lanes("KA", 0, 128), v("one"), u("TD"))], stop=False)
        mms([(lanes("M", 384, 512), v("one"), v("KD", 0, 128))], stop=False)
        todo = {k: list(w) for k, w in SUMS.items()}
        place = {"AH": ("KB", 0, 128, v("GB", 0, 8)), "AF": ("KA", 0, 128, v("GB", 0, 8)), "E": ("M", 384, 512, v("GB", 16, 24)), "U": ("M", 384, 512, v("GH"))}

        def sums(name, done):
            while todo[name] and todo[name][0][1] <= done:
                m0, m1 = todo[name].pop(0)
                if name == "AF" and not AFT:
                    mm(u("KA", m0, m1), [(v("EB", 15 - k, 143 - k), u("AF", 16 * m0 + k, 16 * m1, 16)) for k in range(16)])
                else:
                    bank, a, b, w = place[name]
                    mms([(u(bank, a + k, b, 16, seat(m0, m1)), u(name, 16 * m0 + k, 16 * m1, 16), w) for k in range(16)],
                        stop=False, into=True)

        made = {k: set() for k in ("B", "F", "E", "U", "AH")}
        on_scalar = set()

        def upto(name):
            n = 0
            while n in made[name]:
                n += 1
            return n

        def bank(n):
            piece[0] += 1
            return v("H%d" % (piece[0] % 2), 0, n)

        walk = WALK0 if WALK0 and lev == 0 and t > 0 else WALK
        for kind, a, b in walk:
            c0, c1 = 16 * a, 16 * b
            q = {"B": 2, "b": 2, "F": 1, "f": 1, "C": 1, "E": 0}[kind]
            kid = (Xw, u("ku", ko + q * N + a, ko + q * N + b))
            Bt, E, Fd, Ct = [u(k, c0, c1) for k in ("Bt", "E", "Fd", "Ct")]
            BULK[0] = True
            if kind == "B":
                i0 = act(Bt, kid, AF.Copy)
            elif kind == "b":
                i0 = cp(Bt, kid)
            elif kind == "C":
                act(Ct, kid, AF.Copy)
            else:
                tt(E if kind == "E" else Fd, kid, Bt, A.subtract)
            BULK[0] = False
            if (kind, a, b) == walk[0]:
                ops[i0]["gate"] = 2 * step + s
            made[{"b": "B", "C": "F", "f": "F"}.get(kind, kind)].update(range(a, b))
            if kind == "F":
                act(u("AF", c0, c1), Fd, AF.Abs)
            elif kind == "f":
                ts(u("AF", c0, c1), Fd, 0.0, A.max, 2.0, A.mult)
                mms([(u("KA", k, 128, 16, seat(a, b)), u("Fd", c0 + k, c1, 16), v("GB", 8, 16)) for k in range(16)],
                    stop=False, into=True)
            elif kind == "C":
                on_scalar.update(range(a, b))
                H = bank(c1 - c0)
                mm(H, [(Ib, Ct), (NIb, Bt)])
                act(u("AF", c0, c1), H, AF.Abs)
            elif kind == "E":
                for h0, h1 in UCUT:
                    if h0 not in made["U"] and h1 <= upto("E"):
                        made["U"].update(range(h0, h1))
                        ts(u("U", 16 * h0, 16 * h1), u("E", 16 * h0, 16 * h1), 1.0 / 32, A.add, 31.0 / 1024, A.max)
                sums("E", upto("E"))
                sums("U", upto("U"))
            if kind in "FfC":
                sums("AF", upto("F"))
                if upto("F") == N and AFT:
                    mms([(lanes("KA", 0, 128), v("one"), v("KD", 256, 384))], into="close")
                    act(lanes("S", 0, 128), lanes("KA", 0, 128), AF.Sign)
                elif upto("F") == N:
                    act(u("S", 0, N), u("KA", 0, N), AF.Sign, bias=u("nt", min(t, 1), min(t, 1) + 1))
            for h0, h1 in HCUT:
                if h0 not in made["AH"] and set(range(h0, h1)) <= made["E"] & made["F"]:
                    made["AH"].update(range(h0, h1))
                    H = bank(16 * (h1 - h0))
                    w = {k: u(k, 16 * h0, 16 * h1) for k in ("Bt", "Ct", "Fd", "E", "AH")}
                    mm(H, ([(Ib, w["Bt"]), (NIb, w["Ct"])] if h0 in on_scalar else [(NIb, w["Fd"])]) + [(Ib, w["E"])])
                    act(w["AH"], H, AF.Abs)
                    sums("AH", upto("AH"))
        col, only, x = lanes("S", 128, 256), lanes("S", 256, 384), lanes("M", 384, 512)
        mms([(lanes("KB", 0, 128), part(v("IB", 256, 256 + N + 16), LANES), lanes("S", 0, 128))],
            into="close")
        if COL_ON_VECTOR:
            ts(col, lanes("KB", 0, 128), 1024.0, A.is_gt, 2.0, A.mult)
        else:
            act(col, lanes("KB", 0, 128), AF.Sign, bias=-1024.0)
        act(only, lanes("KB", 0, 128), AF.Sign, bias=1024.0)
        mms([(x, v("one"), v("KD", 128, 256))], into="close")
        mm(u("KA", 128 + N, 128 + 2 * N), [(col, Jb)])
        if ROUND_ON_SCALAR:
            act(lanes("rr"), x, AF.Identity, bias=MAGIC)
            act(lanes("rr"), lanes("rr"), AF.Identity, bias=-MAGIC)
        else:
            ts(lanes("rr"), x, MAGIC, A.add, MAGIC, A.subtract)
        tt(lanes("sel"), x, lanes("rr"), A.is_gt)
        tt(lanes("key"), x, col, A.add)
        scan(lanes("FT"), part(v("rst"), LANES), lanes("key"), 0.0, A.add, A.max)
        tt(u("oh"), (u("FT"), LAST), u("key"), A.is_equal)

        def hot(out, j, h=(0, 128)):
            return [(out, lanes("oh", h[0], h[1]), v("DG", N * j, N * j + N, p=LANES))]

        def listed(out, a, b):
            mm(out, [(v("E16", 15 - r, 143 - r), u("PR", a + r, b, 16)) for r in range(16)])

        mm(u("KA", 128, 128 + N), [(lanes("oh"), Jh)])
        tt(u("PR", 2 * N, 4 * N), u("KA", 128, 128 + 2 * N), u("kf", fo + 2 * N, fo + 4 * N), A.mult)
        if not last:
            for q in range(2):
                tt(u("PR", q * N, q * N + N), u("KA", 128, 128 + N), u("kf", fo + q * N, fo + q * N + N), A.mult)
            if SPLIT:
                listed(u("KA", 320, 332), 0, 2 * N)
                ts(u("Lu", lo, lo + 12), u("KA", 320, 332), 2048.0, A.add)
        q0 = 2 if last or SPLIT else 0
        listed(u("KB", 128 + 6 * q0, 152), q0 * N, 4 * N)
        mm(u("KB", 152, 152 + N), [(BOh, u("PR", 2 * N, 3 * N))])
        ts(u("Lu", lo + 6 * q0, lo + 18), u("KB", 128 + 6 * q0, 146), 2048.0, A.add)
        for c in range(5, -1, -1):
            ts(u("eq", SEG[c], SEG[c] + 16 * c + 16), u("KB", 152, 152 + 16 * c + 16), u("KB", 140 + c, 141 + c),
               A.is_equal, 4096.0, A.mult)
        for c, n in SETS_OF:
            ts(u("eq", SEG[c] + n - 1, SEG[c] + 3 * n, n), u("KB", 140 + c, 143 + c), -1.0, A.mult, -float(XO), A.add)
        if lev == 0:
            cp(mx, u("KB", 146, 152))
        elif not last:
            tt(mx, u("KB", 146, 152), mx, A.max)
        if last:
            ab = u("ab", 0, 6)
            tt(tl, u("KB", 146, 152), mx, A.max)
            ts(ab, tl, 1.0 + 16 * COL_ON_VECTOR, A.is_gt, -8192.0, A.mult)
            tt(tl2, v("lf", 6 * t, 6 * t + 6), ab, A.add)
            if t < TV - 1:
                tt(an, tl2, aL, A.max)
                cp(u("snd", 12 * t, 12 * t + 6), an)
            tt(bL[t + 1], tl2, bL[t], A.max)
            if t == 0:
                cp(u("snd", 6, 12), bL[1])
                send("r_a0%d" % s, u("acin"), u("snd", 0, 12))
            elif t == 1:
                send("r_a1%d" % s, u("ain", 0, 6), u("snd", 12, 18))
                cp(u("snd", 18, 24), bL[2])
            else:
                dmas("out", [("sp", T.so[rows, 6 * r:6 * r + 6], part(bL[3], h)) for r, h in enumerate(HALF)], 2.0)
        scan(u("sc"), v("d0"), u("eq"), 0.0, A.add, A.max)
        mms([(u("KB", 248 + 6 * r + c, 251 + 6 * r + c), SPh[r], u("sc", SEG[c] + n - 1, SEG[c] + 3 * n, n))
             for r in range(2) for c, n in SETS_OF], each=1)
        ts(u("Tu"), u("KB", 248, 260), -1.0, A.mult, 2048.0, A.add)
        sm = u("hb", 2 * N, 3 * N)
        if SUM_ON_VECTOR:
            tt(sm, (Xw, u("Lu", lo + 12, lo + 18)), yv, A.add)
        else:
            act(sm, (Xw, u("Lu", lo + 12, lo + 18)), AF.Copy)
        mms([(u("M", N * r, N * r + N), SPb[r], a) for r in range(2) for a in ([sm] if SUM_ON_VECTOR else [yv, sm])],
            each=1 if SUM_ON_VECTOR else 2)
        act(u("hb", 0, 2 * N), u("M", 0, 2 * N), AF.Identity, bias=127.75, scale=0.5)
        for r in (1, 0):
            tt((u("X", 0, XO + seen), u("Tu", 6 * r, 6 * r + 6)), u("hb", N * r, N * r + N), v("n128"), A.add)
        MX, sg = u("KB", 260, 260 + N), u("S", 384, 384 + N)
        mms([(MX, lanes("sel"), Jh), (MX, Hh, u("PR", 3 * N, 4 * N)), (MX, only, Jb), (MX, lanes("S", 0, 128), NJb)]
            + ([] if last else hot(MX, 12)))
        act(sg, MX, AF.Sign, bias=-1.0 - 0.5 * COL_ON_VECTOR)
        X1, X2 = u("KA", 128, 128 + N), u("KA", 128 + N, 128 + 2 * N)
        terms = [(X1, Ih, u("kf", fo + 2 * N, fo + 3 * N))]
        if not last:
            terms.append((X1, NIh, u("PR", 2 * N, 3 * N)))
            for r, h in enumerate(HALF):
                terms += hot(part(X1, h), 2 * (2 * t + lev) + r, h)
        mms(terms + [(X1, N2Kb, sg)])
        mm(X2, [(Ih, u("kf", fo, fo + N)), (I2Kb, sg)])
        act(u("x2"), X2, AF.Copy)
        nv = u("NV", step * N, step * N + N)
        mm(u("M", 192, 192 + N), [(Ib, u("PV", 0, N)), (NIb, u("PV", N, 2 * N)), (Ib, u("PV", 2 * N, 3 * N))])
        if CLIP_ON_VECTOR:
            ts(nv, u("M", 192, 192 + N), 0.0, A.max, 63.0, A.min)
        else:
            act(u("PV", 3 * N, 4 * N), u("M", 192, 192 + N), AF.Relu, bias=63.0, scale=-1.0)
            act(nv, u("PV", 3 * N, 4 * N), AF.Relu, bias=63.0, scale=-1.0)
        if t < TV - 1:
            dmas("x%s%d" % ("t" if last else "s", s),
                 [("sp", u("X", XO + nbase + N * r, XO + nbase + N * r + N, p=h2), part(nv, h))
                  for r, h in enumerate(HALF) for h2 in HALF], 2.5, more=4 * (lev == 0))
        else:
            dmas("out", [("sp", T.xo[rows, nbase + N * r:nbase + N * r + N], part(nv, h)) for r, h in enumerate(HALF)], 2.5)
        mo = u("Cf", step * N, step * N + N)
        tt(mo, X1, u("x2"), A.max)
        j0 = step * L
        dmas("out", [("sp", T.co[rows, j0 + N * r:j0 + N * r + N], part(mo, h)) for r, h in enumerate(HALF)], 2.5)
        if t < TV - 1:
            ci = u("Ci", step * N, step * N + N)
            cp(ci, mo)
            dmas("cs%d%d" % (lev, s), [("sp", u("C", nbase + N * r, nbase + N * r + N, p=h2), part(ci, h))
                                       for r, h in enumerate(HALF) for h2 in HALF], 2.5)
        if last:
            if t < TV - 1:
                mm(u("KB", 500, 501), [(BO2, u("ab", c, c + 1)) for c in range(6)])
                ts(u("nt", 1, 2), u("KB", 500, 501), 2.0 ** -13, A.mult, u("nt", 0, 1), A.add)
                ts(u("TD"), Ib, u("nt", 1, 2), A.mult)
            ya, yb, ys = u("yt", 0, N), u("yt", N, 2 * N), u("ys", t * N, t * N + N)
            tt(ya, (ab, REP), v("dm"), A.mult)
            mm(u("KB", 384, 384 + N), [(BO64, ya)])
            tt(yb, u("KB", 384, 384 + N), yv, A.min)
            mm(u("KB", 384, 384 + N), [(Ib, yb), (NIb, u("NV", t * LV * N, t * LV * N + N))])
            act(ys, u("KB", 384, 384 + N), AF.Abs)
            if t < TV - 1:
                send("r_y%d%d" % (t, s), u(("yb", "yc")[t]), ys)
            else:
                dmas("out", [("sp", T.yo[rows, N * r:N * r + N], part(ys, h)) for r, h in enumerate(HALF)], 2.0)
                hw = XW // 2
                dmas("out", [(q, T.xo[rows, hw * r:hw * r + hw], u("X", XO + hw * r, XO + hw * r + hw, p=HALF[r]))
                             for r, q in enumerate(("sp", "act" if s else "sp"))], 3.5 if s else 7.0)

    for t in range(TV):
        for lev in range(LV):
            for s in range(2):
                level(s, t, lev)

    order, _end = order_ops(ops)
    count = {"pe": 0, "dve": 0, "act": 0, "pool": 0}
    known = {q: {} for q in Q}
    sent = 0
    for i in order:
        o = ops[i]
        q = o["q"]
        if q == "net":
            o["mark"], o["clock"] = o["sem"], {}
            continue
        kn = known[q]
        need = {}
        for d in o["deps"]:
            s, val = ops[d]["mark"]
            if val > need.get(s, (0, 0))[0]:
                need[s] = (val, d)
        for s, (val, d) in sorted(need.items(), key=lambda e: -ops[e[1][1]].get("start", 0.0)):
            if kn.get(s, 0) < val:
                Q[q].wait_ge(T.sem[s], val)
                kn[s] = val
                for s2, v2 in ops[d]["clock"].items():
                    if kn.get(s2, 0) < v2:
                        kn[s2] = v2
        ins = o["fn"]()
        o["clock"] = dict(kn)
        if o["sem"] is None:
            count[q] += 1
            ins.then_inc(T.sem[q], 1)
            o["mark"] = (q, count[q])
        elif o["sem"][0] == "sent":
            sent += n_out
            o["mark"] = ("sent", 0)
        else:
            ins.then_inc(T.sem[o["sem"][0]], 16)
            o["mark"] = o["sem"]
    for s, val in list(count.items()) + [("sent", sent)] + list(totals.items()) + [(s, n_in) for s in ARRIVE]:
        g.wait_ge(T.sem[s], val)
